import numpy as np
import ml_dtypes


def mxq(x, axis, fmt="e4m3"):
    dtype, down = {"e4m3": (ml_dtypes.float8_e4m3fn, 7), "e5m2": (ml_dtypes.float8_e5m2, 14)}[fmt]
    v = np.moveaxis(np.asarray(x, np.float32).astype(ml_dtypes.bfloat16).astype(np.float64), axis, -1)
    blocks = v.reshape(v.shape[:-1] + (-1, 32))
    amax = np.abs(blocks).max(-1, keepdims=True)
    byte = np.maximum(np.where(amax > 0, np.frexp(amax)[1] - 1 + 127, 0) - down, 1)
    scale = np.exp2(byte - 127.0)
    codes = (blocks / scale).astype(np.float32).astype(dtype).astype(np.float64)
    return np.moveaxis((codes * scale).reshape(v.shape), -1, axis)


WIDE = False


def mx_kscale(k):
    if not WIDE:
        return np.ones(k)
    levels = np.array([10, -10, 5, -5, 0])
    if k % 512:
        return np.exp2(np.random.permutation(np.resize(levels, k // 32))).repeat(32)
    a = np.empty((k // 512, 16))
    for p in range(k // 512):
        a[p, :8] = np.random.permutation(np.resize(levels, 8))
        for g in range(8):
            far = levels[np.abs(levels - a[p, g]) >= 10]
            a[p, g + 8] = far[np.random.randint(len(far))]
    return np.exp2(a.ravel()).repeat(32)


def f64(x):
    return np.asarray(x).astype(np.float64)


def striped(idx):
    return np.tile(idx.reshape(-1, 16).T, (8, 1)).astype(np.uint16)


def unstriped(offs):
    return offs[:16].T.reshape(-1).astype(np.int64)


def striped8(idx):
    return np.concatenate([x.reshape(-1, 16).T for x in idx]).astype(np.uint16)


def runs(offs, k):
    lists = np.stack([offs[16 * r : 16 * r + 16].T.reshape(-1) for r in range(8)]).astype(np.int64)
    return lists[np.arange(k) % 512 // 64]


def pack_weight(w):
    k, n = w.shape
    w = f64(np.asarray(w, np.float32).astype(ml_dtypes.bfloat16)).reshape(k // 32, 32, n)
    amax = np.abs(w).max(1)
    byte = np.clip(np.where(amax > 0, np.frexp(amax)[1] - 1 + 127 - 7, 1), 1, 254)
    scaled = (w * np.exp2(127.0 - byte)[:, None, :]).reshape(k, n).astype(np.float32)
    words = np.ascontiguousarray(scaled.reshape(k // 512, 128, 4, n).transpose(0, 1, 3, 2)).astype(ml_dtypes.float8_e4m3fn).view(np.uint8)
    return words, np.ascontiguousarray(byte.astype(np.uint8).reshape(k // 512, 16, n))


def unpack_weight(words, scales):
    g, p, n, _ = words.shape
    vals = np.ascontiguousarray(words).view(ml_dtypes.float8_e4m3fn).astype(np.float64) * np.repeat(np.exp2(scales.astype(np.float64) - 127.0), 8, axis=1)[..., None]
    return vals.transpose(0, 1, 3, 2).reshape(g * 512, n)


K, T, S, N, H = 512, 2048, 512, 512, 512


def setup_inputs():
    n = np.random.standard_normal
    s = mx_kscale(K)[:, None]
    u = mx_kscale(H)
    packed_xT = pack_weight(n((K, T)) * s)
    return {
        "x_words": packed_xT[0],
        "x_scales": packed_xT[1],
        "w1": (n((K, H)) / np.sqrt(K) / s).astype(np.float32),
        "gn": (np.random.uniform(0.5, 1.5, (H, 1)) * u[:, None]).astype(np.float32),
        "w2": (n((H, N)) / np.sqrt(H) / u[:, None]).astype(np.float32),
        "offs": striped(np.random.permutation(T)[:S]),
        "west": striped8(np.stack([np.random.permutation(S) for _ in range(8)])),
        "east": striped8(np.stack([np.random.permutation(S) for _ in range(8)])),
    }


def reference(x_words, x_scales, w1, gn, w2, offs, west, east):
    xq = unpack_weight(x_words, x_scales)[:, unstriped(offs)]
    y = np.tanh(mxq(f64(w1), 0, "e4m3").T @ xq)
    po = y * ((y) ** 2) - y - (0.5 * (y[np.arange(H)[:, None], runs(west, H)] + y[np.arange(H)[:, None], runs(east, H)] - (2.0 * y)))
    z = f64(gn) * (y + 0.25 * (po[np.arange(H)[:, None], runs(west, H)] + po[np.arange(H)[:, None], runs(east, H)] - (2.0 * po)))
    return mxq(f64(w2), 0, "e4m3").T @ mxq(z, 0, "e4m3")

@@ -1,0 +1,197 @@
+from contextlib import ExitStack
+
+import concourse.mybir as mybir
+
+K, T, S, H, N = 512, 2048, 512, 512, 512
+FLOPS = 2 * K * H * S + 2 * H * N * S
+
+F32 = mybir.dt.float32
+BF16 = mybir.dt.bfloat16
+I32 = mybir.dt.int32
+U32 = mybir.dt.uint32
+U16 = mybir.dt.uint16
+U8 = mybir.dt.uint8
+FP8X4 = mybir.dt.float8_e4m3fn_x4
+ACT = mybir.ActivationFunctionType
+MULT = mybir.AluOpType.mult
+ADD = mybir.AluOpType.add
+
+P = 128
+PACK = 4
+HALF = S // 2
+
+
+def tile_picked_cahn8_none_p_kernel(tc, x_words, x_scales, w1, gn, w2, offs, west, east, out):
+    nc = tc.nc
+    with ExitStack() as ctx:
+        keep = ctx.enter_context(tc.tile_pool(name="keep", bufs=1))
+        psum = ctx.enter_context(tc.psum_pool(name="psum", bufs=1))
+
+        def sb(name, shape, dtype):
+            return keep.tile(shape, dtype, name=name, align_bytes=64)
+
+        offs_t = sb("offs_t", [P, S // 16], U16)
+        west_t = sb("west_t", [P, S // 16], U16)
+        east_t = sb("east_t", [P, S // 16], U16)
+        xw = sb("xw", [P, T], I32)
+        xs = sb("xs", [P, T], U8)
+        w1_raw = sb("w1_raw", [P, PACK, H], F32)
+        w2_raw = sb("w2_raw", [P, PACK, N], F32)
+        g = sb("g", [P, PACK], F32)
+        gq = sb("gq", [P, PACK], F32)
+
+        nc.gpsimd.memset(xs[:].bitcast(I32), 0)
+        nc.sync.dma_start(w1_raw[:], w1.rearrange("(p j) c -> p j c", j=PACK))
+        nc.sync.dma_start(offs_t[:], offs)
+        for q in range(4):
+            nc.sync.dma_start(xs[32 * q : 32 * q + 4, :].bitcast(I32), x_scales[0, 4 * q : 4 * q + 4, :].bitcast(I32))
+        nc.sync.dma_start(xw[:], x_words[0].rearrange("p n t -> p (n t)").bitcast(I32))
+        nc.sync.dma_start(g[:], gn.rearrange("(p t) o -> p (t o)", t=PACK))
+        nc.sync.dma_start(west_t[:], west)
+        nc.sync.dma_start(east_t[:], east)
+        nc.sync.dma_start(w2_raw[:], w2.rearrange("(p j) c -> p j c", j=PACK))
+        nc.gpsimd.tensor_scalar(gq[:], g[:], -0.25, 0.0, MULT, ADD)
+
+        w1_bf = [sb(f"w1_bf{u}", [P, 2 * P * PACK], BF16) for u in range(2)]
+        w1_codes = [sb(f"w1_codes{u}", [P, 2 * P], U32) for u in range(2)]
+        w1_scales = [sb(f"w1_scales{u}", [P, 2 * P], U8) for u in range(2)]
+        w1_view = w1_raw[:].rearrange("p j (m t) -> p m t j", t=PACK)
+        nc.vector.tensor_copy(w1_bf[0][:].rearrange("p (t m j) -> p m t j", t=2, j=PACK), w1_view[:, :, 0:2, :])
+        nc.scalar.copy(w1_bf[1][:].rearrange("p (t m j) -> p m t j", t=2, j=PACK), w1_view[:, :, 2:4, :])
+        xg_s = sb("xg_s", [P, S], U8)
+        xg = sb("xg", [P, S], U32)
+        nc.vector.tensor_copy(xg_s[:], xs[:].indirect(offs_t[:]))
+        nc.vector.quantize_mx(w1_codes[0][:].bitcast(FP8X4), w1_scales[0][:], w1_bf[0][:])
+        nc.vector.tensor_copy(xg[:], xw[:].bitcast(U32).indirect(offs_t[:]))
+        nc.vector.quantize_mx(w1_codes[1][:].bitcast(FP8X4), w1_scales[1][:], w1_bf[1][:])
+
+        pre = [psum.tile([P, S], F32, name=f"pre{t}") for t in range(PACK)]
+        for t in range(PACK):
+            cols = slice((t % 2) * P, (t % 2 + 1) * P)
+            nc.tensor.matmul_mx(pre[t][:], lhsT=w1_codes[t // 2][:, cols].bitcast(FP8X4), lhsT_scale=w1_scales[t // 2][:, cols],
+                                rhs=xg[:].bitcast(FP8X4), rhs_scale=xg_s[:], start=True, stop=True)
+
+        win1 = [sb(f"win1_{t}", [P, 2 * S], F32) for t in range(PACK)]
+        win2 = [sb(f"win2_{t}", [P, 2 * S], F32) for t in range(PACK)]
+        y2 = [sb(f"y2_{t}", [P, S], F32) for t in range(PACK)]
+        gy = [sb(f"gy_{t}", [P, S], F32) for t in range(PACK)]
+        sw = [sb(f"sw_{t}", [P, S], F32) for t in range(PACK)]
+        se = [sb(f"se_{t}", [P, S], F32) for t in range(PACK)]
+        cube = [sb(f"cube_{t}", [P, S], F32) for t in range(PACK)]
+        ctr = [sb(f"ctr_{t}", [P, S], F32) for t in range(PACK)]
+        fw = [sb(f"fw_{t}", [P, S], F32) for t in range(PACK)]
+        z = [sb(f"z_{h}", [P, PACK, HALF], F32) for h in range(2)]
+        lo, hi = slice(0, S), slice(S, 2 * S)
+
+        def s_tanh(t):
+            nc.scalar.activation(win1[t][:, hi], pre[t][:], ACT.Tanh)
+
+        def s_pre(t):
+            nc.scalar.copy(win1[t][:, lo], pre[t][:])
+
+        def s_y2(t):
+            nc.scalar.activation(y2[t][:], win1[t][:, hi], ACT.Square)
+
+        def s_gy(t):
+            nc.scalar.activation(gy[t][:], win1[t][:, hi], ACT.Copy, scale=g[:, t : t + 1])
+
+        def s_gather(t):
+            nc.scalar.activation(sw[t][:], win1[t][:].indirect(west_t[:]), ACT.Sigmoid, scale=2.0)
+            nc.scalar.activation(se[t][:], win1[t][:].indirect(east_t[:]), ACT.Sigmoid, scale=2.0)
+
+        def s_all(t):
+            s_tanh(t)
+            s_pre(t)
+            s_y2(t)
+            s_gy(t)
+            s_gather(t)
+
+        def v_c(t):
+            nc.vector.scalar_tensor_tensor(cube[t][:], gy[t][:], 0.25, y2[t][:], MULT, MULT)
+
+        def v_t(t):
+            nc.vector.scalar_tensor_tensor(win2[t][:, hi], sw[t][:], gq[:, t : t + 1], cube[t][:], MULT, ADD)
+
+        def v_p(t):
+            nc.vector.scalar_tensor_tensor(win2[t][:, lo], se[t][:], gq[:, t : t + 1], win2[t][:, hi], MULT, ADD)
+
+        def v_e(t):
+            nc.vector.scalar_tensor_tensor(ctr[t][:], win2[t][:, lo], -2.0, gy[t][:], MULT, ADD)
+
+        def v_f(t, a, b):
+            nc.vector.tensor_tensor(fw[t][:, a:b], win2[t][:].indirect(west_t[:, a // 16 : b // 16]), ctr[t][:, a:b], ADD)
+
+        def v_z(t, h):
+            a, b = h * HALF, (h + 1) * HALF
+            nc.vector.tensor_tensor(z[h][:, t, :], win2[t][:].indirect(east_t[:, a // 16 : b // 16]), fw[t][:, a:b], ADD)
+
+        w2_bf = sb("w2_bf", [P, N * PACK], BF16)
+        w2_codes = sb("w2_codes", [P, N], U32)
+        w2_scales = sb("w2_scales", [P, N], U8)
+        z_bf = [sb(f"z_bf{h}", [P, HALF * PACK], BF16) for h in range(2)]
+        z_codes = [sb(f"z_codes{h}", [P, HALF], U32) for h in range(2)]
+        z_scales = [sb(f"z_scales{h}", [P, HALF], U8) for h in range(2)]
+        out_rows = out.rearrange("(a p) j -> p a j", p=P)
+
+        def weave(h, copy):
+            copy(z_bf[h][:].rearrange("p (c i t) -> p c t i", i=4, t=PACK), z[h][:].rearrange("p t (c i) -> p c t i", i=4))
+
+        def quant(h):
+            nc.vector.quantize_mx(z_codes[h][:].bitcast(FP8X4), z_scales[h][:], z_bf[h][:])
+
+        def product(h, copies):
+            for u in range(2):
+                acc = psum.tile([P, 2, HALF], F32, name=f"acc{h}{u}")
+                res = sb(f"res{h}{u}", [P, 2, HALF], F32)
+                for a in range(2):
+                    cols = slice((2 * u + a) * P, (2 * u + a + 1) * P)
+                    nc.tensor.matmul_mx(acc[:, a, :], lhsT=w2_codes[:, cols].bitcast(FP8X4), lhsT_scale=w2_scales[:, cols],
+                                        rhs=z_codes[h][:].bitcast(FP8X4), rhs_scale=z_scales[h][:], start=True, stop=True)
+                copies[u](res[:], acc[:])
+                nc.sync.dma_start(out_rows[:, 2 * u : 2 * u + 2, h * HALF : (h + 1) * HALF], res[:])
+
+        s_tanh(0)
+        nc.vector.tensor_scalar(win1[0][:, lo], win1[0][:, hi], gq[:, 0:1], 0.5, MULT, MULT)
+        s_y2(0)
+        s_gy(0)
+        nc.vector.scalar_tensor_tensor(cube[0][:], win1[0][:, lo], -2.0, y2[0][:], MULT, MULT)
+        nc.vector.tensor_tensor(win2[0][:, hi], win1[0][:].indirect(west_t[:]), cube[0][:], ADD)
+        nc.vector.tensor_tensor(win2[0][:, lo], win1[0][:].indirect(east_t[:]), win2[0][:, hi], ADD)
+        s_all(1)
+        v_c(1)
+        v_e(0)
+        v_t(1)
+        v_f(0, 0, S)
+        v_p(1)
+        v_z(0, 0)
+        v_e(1)
+        v_z(0, 1)
+        s_all(2)
+        v_c(2)
+        v_f(1, 0, S)
+        v_t(2)
+        v_z(1, 0)
+        v_p(2)
+        s_all(3)
+        v_c(3)
+        v_e(2)
+        v_t(3)
+        v_f(2, 0, HALF)
+        v_p(3)
+        v_z(2, 0)
+        v_e(3)
+        nc.scalar.copy(w2_bf[:].rearrange("p (c i j) -> p c j i", i=4, j=PACK), w2_raw[:].rearrange("p j (c i) -> p c j i", i=4))
+        v_z(1, 1)
+        v_f(3, 0, HALF)
+        v_f(2, HALF, S)
+        v_z(3, 0)
+        weave(0, nc.scalar.copy)
+        nc.vector.quantize_mx(w2_codes[:].bitcast(FP8X4), w2_scales[:], w2_bf[:])
+        v_f(3, HALF, S)
+        v_z(2, 1)
+        quant(0)
+        v_z(3, 1)
+        product(0, [nc.scalar.copy, nc.scalar.copy])
+        weave(1, nc.vector.tensor_copy)
+        quant(1)
+        product(1, [nc.scalar.copy, nc.vector.tensor_copy])

@@ -30,6 +30,9 @@ def tile_picked_cahn8_none_p_kernel(tc, x_words, x_scales, w1, gn, w2, offs, wes
         def sb(name, shape, dtype):
             return keep.tile(shape, dtype, name=name, align_bytes=64)
 
+        def bank(b, shape, name):
+            return psum.tile(shape, F32, name=name, tag=f"bank{b}")
+
         offs_t = sb("offs_t", [P, S // 16], U16)
         west_t = sb("west_t", [P, S // 16], U16)
         east_t = sb("east_t", [P, S // 16], U16)
@@ -39,6 +42,10 @@ def tile_picked_cahn8_none_p_kernel(tc, x_words, x_scales, w1, gn, w2, offs, wes
         w2_raw = sb("w2_raw", [P, PACK, N], F32)
         g = sb("g", [P, PACK], F32)
         gq = sb("gq", [P, PACK], F32)
+        g2 = sb("g2", [P, 1], F32)
+        gm = sb("gm", [P, 1], F32)
+        win1 = [sb(f"win1_{t}", [P, 2 * S], F32) for t in range(PACK)]
+        lo, hi = slice(0, S), slice(S, 2 * S)
 
         nc.gpsimd.memset(xs[:].bitcast(I32), 0)
         nc.sync.dma_start(w1_raw[:], w1.rearrange("(p j) c -> p j c", j=PACK))
@@ -51,147 +58,156 @@ def tile_picked_cahn8_none_p_kernel(tc, x_words, x_scales, w1, gn, w2, offs, wes
         nc.sync.dma_start(east_t[:], east)
         nc.sync.dma_start(w2_raw[:], w2.rearrange("(p j) c -> p j c", j=PACK))
         nc.gpsimd.tensor_scalar(gq[:], g[:], -0.25, 0.0, MULT, ADD)
+        nc.gpsimd.tensor_scalar(g2[:], g[:, 0:1], 2.0, 0.0, MULT, ADD)
+        nc.gpsimd.tensor_scalar(gm[:], g[:, 0:1], -1.0, 0.0, MULT, ADD)
 
-        w1_bf = [sb(f"w1_bf{u}", [P, 2 * P * PACK], BF16) for u in range(2)]
+        w1_bf = sb("w1_bf", [P, H * PACK], BF16)
         w1_codes = [sb(f"w1_codes{u}", [P, 2 * P], U32) for u in range(2)]
         w1_scales = [sb(f"w1_scales{u}", [P, 2 * P], U8) for u in range(2)]
-        w1_view = w1_raw[:].rearrange("p j (m t) -> p m t j", t=PACK)
-        nc.vector.tensor_copy(w1_bf[0][:].rearrange("p (t m j) -> p m t j", t=2, j=PACK), w1_view[:, :, 0:2, :])
-        nc.scalar.copy(w1_bf[1][:].rearrange("p (t m j) -> p m t j", t=2, j=PACK), w1_view[:, :, 2:4, :])
+        nc.vector.tensor_copy(w1_bf[:].rearrange("p (t m j) -> p m j t", t=PACK, j=PACK), w1_raw[:].rearrange("p j (m t) -> p m j t", t=PACK))
         xg_s = sb("xg_s", [P, S], U8)
         xg = sb("xg", [P, S], U32)
         nc.vector.tensor_copy(xg_s[:], xs[:].indirect(offs_t[:]))
-        nc.vector.quantize_mx(w1_codes[0][:].bitcast(FP8X4), w1_scales[0][:], w1_bf[0][:])
-        nc.vector.tensor_copy(xg[:], xw[:].bitcast(U32).indirect(offs_t[:]))
-        nc.vector.quantize_mx(w1_codes[1][:].bitcast(FP8X4), w1_scales[1][:], w1_bf[1][:])
+        nc.vector.quantize_mx(w1_codes[0][:].bitcast(FP8X4), w1_scales[0][:], w1_bf[:, 0:1024])
 
-        pre = [psum.tile([P, S], F32, name=f"pre{t}") for t in range(PACK)]
-        for t in range(PACK):
+        def first_product(acc, t, a, b):
             cols = slice((t % 2) * P, (t % 2 + 1) * P)
-            nc.tensor.matmul_mx(pre[t][:], lhsT=w1_codes[t // 2][:, cols].bitcast(FP8X4), lhsT_scale=w1_scales[t // 2][:, cols],
-                                rhs=xg[:].bitcast(FP8X4), rhs_scale=xg_s[:], start=True, stop=True)
+            nc.tensor.matmul_mx(acc, lhsT=w1_codes[t // 2][:, cols].bitcast(FP8X4), lhsT_scale=w1_scales[t // 2][:, cols],
+                                rhs=xg[:, a:b].bitcast(FP8X4), rhs_scale=xg_s[:, a:b], start=True, stop=True)
 
-        win1 = [sb(f"win1_{t}", [P, 2 * S], F32) for t in range(PACK)]
-        win2 = [sb(f"win2_{t}", [P, 2 * S], F32) for t in range(PACK)]
+        for h in range(2):
+            a, b = h * HALF, (h + 1) * HALF
+            nc.vector.tensor_copy(xg[:, a:b], xw[:].bitcast(U32).indirect(offs_t[:, a // 16 : b // 16]))
+            pre0 = bank(h, [P, HALF], f"pre0{h}")
+            first_product(pre0[:], 0, a, b)
+            nc.scalar.activation(win1[0][:, a:b], pre0[:], ACT.Sigmoid, scale=2.0)
+        pre = [None] + [bank(1 + t, [P, S], f"pre{t}") for t in range(1, PACK)]
+        first_product(pre[1][:], 1, 0, S)
+
+        win2 = [sb(f"win2_{t}", [P, 2 * S if t < 3 else S], F32) for t in range(PACK)]
+        part = [win2[t][:, hi] for t in range(3)] + [sb("part3", [P, S], F32)[:]]
         y2 = [sb(f"y2_{t}", [P, S], F32) for t in range(PACK)]
         gy = [sb(f"gy_{t}", [P, S], F32) for t in range(PACK)]
         sw = [sb(f"sw_{t}", [P, S], F32) for t in range(PACK)]
         se = [sb(f"se_{t}", [P, S], F32) for t in range(PACK)]
         cube = [sb(f"cube_{t}", [P, S], F32) for t in range(PACK)]
         ctr = [sb(f"ctr_{t}", [P, S], F32) for t in range(PACK)]
-        fw = [sb(f"fw_{t}", [P, S], F32) for t in range(PACK)]
+        fwa = [sb(f"fw_{t}", [P, HALF], F32) for t in range(PACK)]
+        fw = {(t, 0): fwa[t] for t in range(PACK)}
+        fw[0, 1] = sb("fw_0b", [P, HALF], F32)
+        fw[1, 1] = sw[3]
+        fw[2, 1] = gy[3]
+        fw[3, 1] = fwa[3]
         z = [sb(f"z_{h}", [P, PACK, HALF], F32) for h in range(2)]
-        lo, hi = slice(0, S), slice(S, 2 * S)
-
-        def s_tanh(t):
-            nc.scalar.activation(win1[t][:, hi], pre[t][:], ACT.Tanh)
-
-        def s_pre(t):
-            nc.scalar.copy(win1[t][:, lo], pre[t][:])
-
-        def s_y2(t):
-            nc.scalar.activation(y2[t][:], win1[t][:, hi], ACT.Square)
-
-        def s_gy(t):
-            nc.scalar.activation(gy[t][:], win1[t][:, hi], ACT.Copy, scale=g[:, t : t + 1])
-
-        def s_gather(t):
-            nc.scalar.activation(sw[t][:], win1[t][:].indirect(west_t[:]), ACT.Sigmoid, scale=2.0)
-            nc.scalar.activation(se[t][:], win1[t][:].indirect(east_t[:]), ACT.Sigmoid, scale=2.0)
 
         def s_all(t):
-            s_tanh(t)
-            s_pre(t)
-            s_y2(t)
-            s_gy(t)
-            s_gather(t)
+            nc.scalar.activation(win1[t][:, hi], pre[t][:], ACT.Tanh)
+            nc.scalar.copy(win1[t][:, lo], pre[t][:])
+            nc.scalar.activation(y2[t][:], win1[t][:, hi], ACT.Square)
+            nc.scalar.activation(gy[t][:], win1[t][:, hi], ACT.Copy, scale=g[:, t : t + 1])
+            nc.scalar.activation(sw[t][:], win1[t][:].indirect(west_t[:]), ACT.Sigmoid, scale=2.0)
+            nc.scalar.activation(se[t][:], win1[t][:].indirect(east_t[:]), ACT.Sigmoid, scale=2.0)
 
         def v_c(t):
             nc.vector.scalar_tensor_tensor(cube[t][:], gy[t][:], 0.25, y2[t][:], MULT, MULT)
 
         def v_t(t):
-            nc.vector.scalar_tensor_tensor(win2[t][:, hi], sw[t][:], gq[:, t : t + 1], cube[t][:], MULT, ADD)
+            nc.vector.scalar_tensor_tensor(part[t], sw[t][:], gq[:, t : t + 1], cube[t][:], MULT, ADD)
 
         def v_p(t):
-            nc.vector.scalar_tensor_tensor(win2[t][:, lo], se[t][:], gq[:, t : t + 1], win2[t][:, hi], MULT, ADD)
+            nc.vector.scalar_tensor_tensor(win2[t][:, lo], se[t][:], gq[:, t : t + 1], part[t], MULT, ADD)
 
         def v_e(t):
             nc.vector.scalar_tensor_tensor(ctr[t][:], win2[t][:, lo], -2.0, gy[t][:], MULT, ADD)
 
-        def v_f(t, a, b):
-            nc.vector.tensor_tensor(fw[t][:, a:b], win2[t][:].indirect(west_t[:, a // 16 : b // 16]), ctr[t][:, a:b], ADD)
-
-        def v_z(t, h):
+        def v_f(t, h):
             a, b = h * HALF, (h + 1) * HALF
-            nc.vector.tensor_tensor(z[h][:, t, :], win2[t][:].indirect(east_t[:, a // 16 : b // 16]), fw[t][:, a:b], ADD)
+            nc.vector.tensor_tensor(fw[t, h][:, 0:HALF], win2[t][:].indirect(west_t[:, a // 16 : b // 16]), ctr[t][:, a:b], ADD)
+
+        def v_z(t, a, b):
+            h = a // HALF
+            nc.vector.tensor_tensor(z[h][:, t, a - h * HALF : b - h * HALF], win2[t][:].indirect(east_t[:, a // 16 : b // 16]), fw[t, h][:, a - h * HALF : b - h * HALF], ADD)
 
         w2_bf = sb("w2_bf", [P, N * PACK], BF16)
         w2_codes = sb("w2_codes", [P, N], U32)
         w2_scales = sb("w2_scales", [P, N], U8)
-        z_bf = [sb(f"z_bf{h}", [P, HALF * PACK], BF16) for h in range(2)]
-        z_codes = [sb(f"z_codes{h}", [P, HALF], U32) for h in range(2)]
-        z_scales = [sb(f"z_scales{h}", [P, HALF], U8) for h in range(2)]
+        chunks = [(0, 256), (256, 384), (384, 512)]
+        z_bf = [sb(f"z_bf{c}", [P, (b - a) * PACK], BF16) for c, (a, b) in enumerate(chunks)]
+        z_codes = [sb(f"z_codes{c}", [P, b - a], U32) for c, (a, b) in enumerate(chunks)]
+        z_scales = [sb(f"z_scales{c}", [P, b - a], U8) for c, (a, b) in enumerate(chunks)]
         out_rows = out.rearrange("(a p) j -> p a j", p=P)
 
-        def weave(h, copy):
-            copy(z_bf[h][:].rearrange("p (c i t) -> p c t i", i=4, t=PACK), z[h][:].rearrange("p t (c i) -> p c t i", i=4))
+        def weave(c, copy):
+            a, b = chunks[c]
+            h = a // HALF
+            copy(z_bf[c][:].rearrange("p (c i t) -> p c t i", i=4, t=PACK), z[h][:, :, a - h * HALF : b - h * HALF].rearrange("p t (c i) -> p c t i", i=4))
 
-        def quant(h):
-            nc.vector.quantize_mx(z_codes[h][:].bitcast(FP8X4), z_scales[h][:], z_bf[h][:])
+        def quant(c):
+            nc.vector.quantize_mx(z_codes[c][:].bitcast(FP8X4), z_scales[c][:], z_bf[c][:])
 
-        def product(h, copies):
-            for u in range(2):
-                acc = psum.tile([P, 2, HALF], F32, name=f"acc{h}{u}")
-                res = sb(f"res{h}{u}", [P, 2, HALF], F32)
-                for a in range(2):
-                    cols = slice((2 * u + a) * P, (2 * u + a + 1) * P)
-                    nc.tensor.matmul_mx(acc[:, a, :], lhsT=w2_codes[:, cols].bitcast(FP8X4), lhsT_scale=w2_scales[:, cols],
-                                        rhs=z_codes[h][:].bitcast(FP8X4), rhs_scale=z_scales[h][:], start=True, stop=True)
-                copies[u](res[:], acc[:])
-                nc.sync.dma_start(out_rows[:, 2 * u : 2 * u + 2, h * HALF : (h + 1) * HALF], res[:])
+        def product(c, first, count, b, copy):
+            j0, j1 = chunks[c]
+            acc = bank(b, [P, count, j1 - j0], f"acc{c}{first}")
+            res = sb(f"res{c}{first}", [P, count, j1 - j0], F32)
+            for a in range(count):
+                cols = slice((first + a) * P, (first + a + 1) * P)
+                nc.tensor.matmul_mx(acc[:, a, :], lhsT=w2_codes[:, cols].bitcast(FP8X4), lhsT_scale=w2_scales[:, cols],
+                                    rhs=z_codes[c][:].bitcast(FP8X4), rhs_scale=z_scales[c][:], start=True, stop=True)
+            copy(res[:], acc[:])
+            nc.sync.dma_start(out_rows[:, first : first + count, j0:j1], res[:])
 
-        s_tanh(0)
-        nc.vector.tensor_scalar(win1[0][:, lo], win1[0][:, hi], gq[:, 0:1], 0.5, MULT, MULT)
-        s_y2(0)
-        s_gy(0)
-        nc.vector.scalar_tensor_tensor(cube[0][:], win1[0][:, lo], -2.0, y2[0][:], MULT, MULT)
-        nc.vector.tensor_tensor(win2[0][:, hi], win1[0][:].indirect(west_t[:]), cube[0][:], ADD)
-        nc.vector.tensor_tensor(win2[0][:, lo], win1[0][:].indirect(east_t[:]), win2[0][:, hi], ADD)
+        nc.vector.tensor_copy(sw[0][:], win1[0][:].indirect(west_t[:]))
+        nc.scalar.activation(y2[0][:], win1[0][:, lo], ACT.Square, scale=2.0, bias=-1.0)
+        nc.scalar.activation(gy[0][:], win1[0][:, lo], ACT.Identity, scale=g2[:], bias=gm[:])
+        v_c(0)
+        nc.vector.tensor_tensor(se[0][:], win1[0][:].indirect(east_t[:]), sw[0][:], ADD)
+        nc.vector.quantize_mx(w1_codes[1][:].bitcast(FP8X4), w1_scales[1][:], w1_bf[:, 1024:2048])
+        first_product(pre[2][:], 2, 0, S)
+        first_product(pre[3][:], 3, 0, S)
         s_all(1)
         v_c(1)
-        v_e(0)
+        nc.vector.scalar_tensor_tensor(win2[0][:, lo], se[0][:], gq[:, 0:1], cube[0][:], MULT, ADD)
         v_t(1)
-        v_f(0, 0, S)
+        v_e(0)
         v_p(1)
-        v_z(0, 0)
+        v_f(0, 0)
         v_e(1)
-        v_z(0, 1)
+        v_z(0, 0, 256)
+        v_f(1, 0)
         s_all(2)
         v_c(2)
-        v_f(1, 0, S)
+        v_z(1, 0, 256)
         v_t(2)
-        v_z(1, 0)
+        v_f(0, 1)
         v_p(2)
+        v_z(0, 256, 512)
+        v_e(2)
         s_all(3)
         v_c(3)
-        v_e(2)
+        v_f(2, 0)
         v_t(3)
-        v_f(2, 0, HALF)
+        v_z(2, 0, 256)
         v_p(3)
-        v_z(2, 0)
+        v_f(1, 1)
         v_e(3)
+        v_z(1, 256, 512)
+        v_f(3, 0)
+        v_f(2, 1)
+        v_z(3, 0, 256)
         nc.scalar.copy(w2_bf[:].rearrange("p (c i j) -> p c j i", i=4, j=PACK), w2_raw[:].rearrange("p j (c i) -> p c j i", i=4))
-        v_z(1, 1)
-        v_f(3, 0, HALF)
-        v_f(2, HALF, S)
-        v_z(3, 0)
         weave(0, nc.scalar.copy)
+        v_z(2, 256, 512)
+        v_f(3, 1)
         nc.vector.quantize_mx(w2_codes[:].bitcast(FP8X4), w2_scales[:], w2_bf[:])
-        v_f(3, HALF, S)
-        v_z(2, 1)
         quant(0)
-        v_z(3, 1)
-        product(0, [nc.scalar.copy, nc.scalar.copy])
+        v_z(3, 256, 384)
+        v_z(3, 384, 512)
+        product(0, 0, 2, 0, nc.scalar.copy)
+        product(0, 2, 2, 1, nc.scalar.copy)
         weave(1, nc.vector.tensor_copy)
+        weave(2, nc.vector.tensor_copy)
         quant(1)
-        product(1, [nc.scalar.copy, nc.vector.tensor_copy])
+        quant(2)
+        product(1, 0, 4, 5, nc.scalar.copy)
+        product(2, 0, 2, 6, nc.scalar.copy)
+        product(2, 2, 2, 7, nc.vector.tensor_copy)

@@ -48,11 +48,11 @@ def tile_picked_cahn8_none_p_kernel(tc, x_words, x_scales, w1, gn, w2, offs, wes
         lo, hi = slice(0, S), slice(S, 2 * S)
 
         nc.gpsimd.memset(xs[:].bitcast(I32), 0)
-        nc.sync.dma_start(w1_raw[:], w1.rearrange("(p j) c -> p j c", j=PACK))
+        nc.sync.dma_start(xw[:], x_words[0].rearrange("p n t -> p (n t)").bitcast(I32))
         nc.sync.dma_start(offs_t[:], offs)
         for q in range(4):
             nc.sync.dma_start(xs[32 * q : 32 * q + 4, :].bitcast(I32), x_scales[0, 4 * q : 4 * q + 4, :].bitcast(I32))
-        nc.sync.dma_start(xw[:], x_words[0].rearrange("p n t -> p (n t)").bitcast(I32))
+        nc.sync.dma_start(w1_raw[:], w1.rearrange("(p j) c -> p j c", j=PACK))
         nc.sync.dma_start(g[:], gn.rearrange("(p t) o -> p (t o)", t=PACK))
         nc.sync.dma_start(west_t[:], west)
         nc.sync.dma_start(east_t[:], east)
@@ -61,28 +61,28 @@ def tile_picked_cahn8_none_p_kernel(tc, x_words, x_scales, w1, gn, w2, offs, wes
         nc.gpsimd.tensor_scalar(g2[:], g[:, 0:1], 2.0, 0.0, MULT, ADD)
         nc.gpsimd.tensor_scalar(gm[:], g[:, 0:1], -1.0, 0.0, MULT, ADD)
 
-        w1_bf = sb("w1_bf", [P, H * PACK], BF16)
-        w1_codes = [sb(f"w1_codes{u}", [P, 2 * P], U32) for u in range(2)]
-        w1_scales = [sb(f"w1_scales{u}", [P, 2 * P], U8) for u in range(2)]
-        nc.vector.tensor_copy(w1_bf[:].rearrange("p (t m j) -> p m j t", t=PACK, j=PACK), w1_raw[:].rearrange("p j (m t) -> p m j t", t=PACK))
         xg_s = sb("xg_s", [P, S], U8)
         xg = sb("xg", [P, S], U32)
+        nc.vector.tensor_copy(xg[:], xw[:].bitcast(U32).indirect(offs_t[:]))
         nc.vector.tensor_copy(xg_s[:], xs[:].indirect(offs_t[:]))
-        nc.vector.quantize_mx(w1_codes[0][:].bitcast(FP8X4), w1_scales[0][:], w1_bf[:, 0:1024])
-
-        def first_product(acc, t, a, b):
-            cols = slice((t % 2) * P, (t % 2 + 1) * P)
-            nc.tensor.matmul_mx(acc, lhsT=w1_codes[t // 2][:, cols].bitcast(FP8X4), lhsT_scale=w1_scales[t // 2][:, cols],
-                                rhs=xg[:, a:b].bitcast(FP8X4), rhs_scale=xg_s[:, a:b], start=True, stop=True)
-
+        pre0 = [bank(4 * h, [P, HALF], f"pre0{h}") for h in range(2)]
+        pre = [None] + [bank(t, [P, S], f"pre{t}") for t in range(1, PACK)]
+        w1_view = w1_raw[:].rearrange("p j (m t) -> p m j t", t=PACK)
+        for u in range(2):
+            w1_bf = sb("w1_bf", [P, 2 * P * PACK], BF16)
+            w1_codes = sb(f"w1_codes{u}", [P, 2 * P], U32)
+            w1_scales = sb(f"w1_scales{u}", [P, 2 * P], U8)
+            nc.vector.tensor_copy(w1_bf[:].rearrange("p (t m j) -> p m j t", t=2, j=PACK), w1_view[:, :, :, 2 * u : 2 * u + 2])
+            nc.vector.quantize_mx(w1_codes[:].bitcast(FP8X4), w1_scales[:], w1_bf[:])
+            for e in range(2):
+                cols = slice(e * P, (e + 1) * P)
+                t = 2 * u + e
+                pieces = [(pre[t], slice(0, S))] if t else [(pre0[0], slice(0, HALF)), (pre0[1], slice(HALF, S))]
+                for acc, c in pieces:
+                    nc.tensor.matmul_mx(acc[:], lhsT=w1_codes[:, cols].bitcast(FP8X4), lhsT_scale=w1_scales[:, cols],
+                                        rhs=xg[:, c].bitcast(FP8X4), rhs_scale=xg_s[:, c], start=True, stop=True)
         for h in range(2):
-            a, b = h * HALF, (h + 1) * HALF
-            nc.vector.tensor_copy(xg[:, a:b], xw[:].bitcast(U32).indirect(offs_t[:, a // 16 : b // 16]))
-            pre0 = bank(h, [P, HALF], f"pre0{h}")
-            first_product(pre0[:], 0, a, b)
-            nc.scalar.activation(win1[0][:, a:b], pre0[:], ACT.Sigmoid, scale=2.0)
-        pre = [None] + [bank(1 + t, [P, S], f"pre{t}") for t in range(1, PACK)]
-        first_product(pre[1][:], 1, 0, S)
+            nc.scalar.activation(win1[0][:, h * HALF : (h + 1) * HALF], pre0[h][:], ACT.Sigmoid, scale=2.0)
 
         win2 = [sb(f"win2_{t}", [P, 2 * S if t < 3 else S], F32) for t in range(PACK)]
         part = [win2[t][:, hi] for t in range(3)] + [sb("part3", [P, S], F32)[:]]
@@ -95,7 +95,7 @@ def tile_picked_cahn8_none_p_kernel(tc, x_words, x_scales, w1, gn, w2, offs, wes
         fwa = [sb(f"fw_{t}", [P, HALF], F32) for t in range(PACK)]
         fw = {(t, 0): fwa[t] for t in range(PACK)}
         fw[0, 1] = sb("fw_0b", [P, HALF], F32)
-        fw[1, 1] = sw[3]
+        fw[1, 1] = sb("fw_1b", [P, HALF], F32)
         fw[2, 1] = gy[3]
         fw[3, 1] = fwa[3]
         z = [sb(f"z_{h}", [P, PACK, HALF], F32) for h in range(2)]
@@ -108,17 +108,23 @@ def tile_picked_cahn8_none_p_kernel(tc, x_words, x_scales, w1, gn, w2, offs, wes
             nc.scalar.activation(sw[t][:], win1[t][:].indirect(west_t[:]), ACT.Sigmoid, scale=2.0)
             nc.scalar.activation(se[t][:], win1[t][:].indirect(east_t[:]), ACT.Sigmoid, scale=2.0)
 
+        halves = [slice(0, HALF), slice(HALF, S)]
+
         def v_c(t):
-            nc.vector.scalar_tensor_tensor(cube[t][:], gy[t][:], 0.25, y2[t][:], MULT, MULT)
+            for c in halves:
+                nc.vector.scalar_tensor_tensor(cube[t][:, c], gy[t][:, c], 0.25, y2[t][:, c], MULT, MULT)
 
         def v_t(t):
-            nc.vector.scalar_tensor_tensor(part[t], sw[t][:], gq[:, t : t + 1], cube[t][:], MULT, ADD)
+            for c in halves:
+                nc.vector.scalar_tensor_tensor(part[t][:, c], sw[t][:, c], gq[:, t : t + 1], cube[t][:, c], MULT, ADD)
 
-        def v_p(t):
-            nc.vector.scalar_tensor_tensor(win2[t][:, lo], se[t][:], gq[:, t : t + 1], part[t], MULT, ADD)
+        def v_p(t, add):
+            for c in halves:
+                nc.vector.scalar_tensor_tensor(win2[t][:, c], se[t][:, c], gq[:, t : t + 1], add[:, c], MULT, ADD)
 
         def v_e(t):
-            nc.vector.scalar_tensor_tensor(ctr[t][:], win2[t][:, lo], -2.0, gy[t][:], MULT, ADD)
+            for c in halves:
+                nc.vector.scalar_tensor_tensor(ctr[t][:, c], win2[t][:, c], -2.0, gy[t][:, c], MULT, ADD)
 
         def v_f(t, h):
             a, b = h * HALF, (h + 1) * HALF
@@ -137,10 +143,9 @@ def tile_picked_cahn8_none_p_kernel(tc, x_words, x_scales, w1, gn, w2, offs, wes
         z_scales = [sb(f"z_scales{c}", [P, b - a], U8) for c, (a, b) in enumerate(chunks)]
         out_rows = out.rearrange("(a p) j -> p a j", p=P)
 
-        def weave(c, copy):
-            a, b = chunks[c]
+        def weave(c, a, b, copy):
             h = a // HALF
-            copy(z_bf[c][:].rearrange("p (c i t) -> p c t i", i=4, t=PACK), z[h][:, :, a - h * HALF : b - h * HALF].rearrange("p t (c i) -> p c t i", i=4))
+            copy(z_bf[c][:, (a - chunks[c][0]) * PACK : (b - chunks[c][0]) * PACK].rearrange("p (c i t) -> p c t i", i=4, t=PACK), z[h][:, :, a - h * HALF : b - h * HALF].rearrange("p t (c i) -> p c t i", i=4))
 
         def quant(c):
             nc.vector.quantize_mx(z_codes[c][:].bitcast(FP8X4), z_scales[c][:], z_bf[c][:])
@@ -156,58 +161,53 @@ def tile_picked_cahn8_none_p_kernel(tc, x_words, x_scales, w1, gn, w2, offs, wes
             copy(res[:], acc[:])
             nc.sync.dma_start(out_rows[:, first : first + count, j0:j1], res[:])
 
-        nc.vector.tensor_copy(sw[0][:], win1[0][:].indirect(west_t[:]))
+        def second(t):
+            v_f(t, 0)
+            v_f(t, 1)
+            v_z(t, 0, HALF)
+            v_z(t, HALF, S)
+
+        def chain(t):
+            s_all(t)
+            v_c(t)
+            v_t(t)
+            v_p(t, part[t])
+            v_e(t)
+
+        for h, c in enumerate(halves):
+            nc.vector.tensor_copy(sw[0][:, c], win1[0][:].indirect(west_t[:, 16 * h : 16 * h + 16]))
         nc.scalar.activation(y2[0][:], win1[0][:, lo], ACT.Square, scale=2.0, bias=-1.0)
         nc.scalar.activation(gy[0][:], win1[0][:, lo], ACT.Identity, scale=g2[:], bias=gm[:])
+        for h, c in enumerate(halves):
+            nc.vector.tensor_tensor(se[0][:, c], win1[0][:].indirect(east_t[:, 16 * h : 16 * h + 16]), sw[0][:, c], ADD)
         v_c(0)
-        nc.vector.tensor_tensor(se[0][:], win1[0][:].indirect(east_t[:]), sw[0][:], ADD)
-        nc.vector.quantize_mx(w1_codes[1][:].bitcast(FP8X4), w1_scales[1][:], w1_bf[:, 1024:2048])
-        first_product(pre[2][:], 2, 0, S)
-        first_product(pre[3][:], 3, 0, S)
-        s_all(1)
-        v_c(1)
-        nc.vector.scalar_tensor_tensor(win2[0][:, lo], se[0][:], gq[:, 0:1], cube[0][:], MULT, ADD)
-        v_t(1)
+        v_p(0, cube[0])
         v_e(0)
-        v_p(1)
-        v_f(0, 0)
-        v_e(1)
-        v_z(0, 0, 256)
-        v_f(1, 0)
-        s_all(2)
-        v_c(2)
-        v_z(1, 0, 256)
-        v_t(2)
-        v_f(0, 1)
-        v_p(2)
-        v_z(0, 256, 512)
-        v_e(2)
-        s_all(3)
-        v_c(3)
+        second(0)
+        chain(1)
+        second(1)
+        chain(2)
         v_f(2, 0)
-        v_t(3)
-        v_z(2, 0, 256)
-        v_p(3)
-        v_f(1, 1)
-        v_e(3)
-        v_z(1, 256, 512)
+        v_z(2, 0, HALF)
+        chain(3)
         v_f(3, 0)
         v_f(2, 1)
-        v_z(3, 0, 256)
+        v_z(3, 0, HALF)
         nc.scalar.copy(w2_bf[:].rearrange("p (c i j) -> p c j i", i=4, j=PACK), w2_raw[:].rearrange("p j (c i) -> p c j i", i=4))
-        weave(0, nc.scalar.copy)
+        weave(0, 128, 256, nc.scalar.copy)
         v_z(2, 256, 512)
+        weave(0, 0, 128, nc.vector.tensor_copy)
         v_f(3, 1)
         nc.vector.quantize_mx(w2_codes[:].bitcast(FP8X4), w2_scales[:], w2_bf[:])
         quant(0)
         v_z(3, 256, 384)
         v_z(3, 384, 512)
-        product(0, 0, 2, 0, nc.scalar.copy)
-        product(0, 2, 2, 1, nc.scalar.copy)
-        weave(1, nc.vector.tensor_copy)
-        weave(2, nc.vector.tensor_copy)
+        product(0, 0, 2, 4, nc.scalar.copy)
+        product(0, 2, 2, 5, nc.scalar.copy)
+        weave(1, 256, 384, nc.vector.tensor_copy)
+        weave(2, 384, 512, nc.vector.tensor_copy)
         quant(1)
         quant(2)
-        product(1, 0, 4, 5, nc.scalar.copy)
+        product(1, 0, 4, 0, nc.scalar.copy)
         product(2, 0, 2, 6, nc.scalar.copy)
         product(2, 2, 2, 7, nc.vector.tensor_copy)

@@ -53,7 +53,7 @@ def tile_picked_cahn8_none_p_kernel(tc, x_words, x_scales, w1, gn, w2, offs, wes
         for q in range(4):
             nc.sync.dma_start(xs[32 * q : 32 * q + 4, :].bitcast(I32), x_scales[0, 4 * q : 4 * q + 4, :].bitcast(I32))
         nc.sync.dma_start(w1_raw[:], w1.rearrange("(p j) c -> p j c", j=PACK))
-        nc.sync.dma_start(g[:], gn.rearrange("(p t) o -> p (t o)", t=PACK))
+        nc.scalar.dma_start(g[:], gn.rearrange("(p t) o -> p (t o)", t=PACK))
         nc.sync.dma_start(west_t[:], west)
         nc.sync.dma_start(east_t[:], east)
         nc.sync.dma_start(w2_raw[:], w2.rearrange("(p j) c -> p j c", j=PACK))
@@ -150,7 +150,7 @@ def tile_picked_cahn8_none_p_kernel(tc, x_words, x_scales, w1, gn, w2, offs, wes
         def quant(c):
             nc.vector.quantize_mx(z_codes[c][:].bitcast(FP8X4), z_scales[c][:], z_bf[c][:])
 
-        def product(c, first, count, b, copy):
+        def product(c, first, count, b, copy, queue=nc.sync):
             j0, j1 = chunks[c]
             acc = bank(b, [P, count, j1 - j0], f"acc{c}{first}")
             res = sb(f"res{c}{first}", [P, count, j1 - j0], F32)
@@ -159,7 +159,7 @@ def tile_picked_cahn8_none_p_kernel(tc, x_words, x_scales, w1, gn, w2, offs, wes
                 nc.tensor.matmul_mx(acc[:, a, :], lhsT=w2_codes[:, cols].bitcast(FP8X4), lhsT_scale=w2_scales[:, cols],
                                     rhs=z_codes[c][:].bitcast(FP8X4), rhs_scale=z_scales[c][:], start=True, stop=True)
             copy(res[:], acc[:])
-            nc.sync.dma_start(out_rows[:, first : first + count, j0:j1], res[:])
+            queue.dma_start(out_rows[:, first : first + count, j0:j1], res[:])
 
         def second(t):
             v_f(t, 0)
@@ -199,15 +199,15 @@ def tile_picked_cahn8_none_p_kernel(tc, x_words, x_scales, w1, gn, w2, offs, wes
         weave(0, 0, 128, nc.vector.tensor_copy)
         v_f(3, 1)
         nc.vector.quantize_mx(w2_codes[:].bitcast(FP8X4), w2_scales[:], w2_bf[:])
-        quant(0)
         v_z(3, 256, 384)
-        v_z(3, 384, 512)
+        quant(0)
         product(0, 0, 2, 4, nc.scalar.copy)
         product(0, 2, 2, 5, nc.scalar.copy)
         weave(1, 256, 384, nc.vector.tensor_copy)
-        weave(2, 384, 512, nc.vector.tensor_copy)
+        v_z(3, 384, 512)
         quant(1)
-        quant(2)
         product(1, 0, 4, 0, nc.scalar.copy)
-        product(2, 0, 2, 6, nc.scalar.copy)
+        weave(2, 384, 512, nc.vector.tensor_copy)
+        quant(2)
+        product(2, 0, 2, 6, nc.scalar.copy, nc.scalar)
         product(2, 2, 2, 7, nc.vector.tensor_copy)

@@ -1,6 +1,7 @@
 from contextlib import ExitStack
 
 import concourse.mybir as mybir
+from concourse.masks import make_identity
 
 K, T, S, H, N = 512, 2048, 512, 512, 512
 FLOPS = 2 * K * H * S + 2 * H * N * S
@@ -41,9 +42,7 @@ def tile_picked_cahn8_none_p_kernel(tc, x_words, x_scales, w1, gn, w2, offs, wes
         w1_raw = sb("w1_raw", [P, PACK, H], F32)
         w2_raw = sb("w2_raw", [P, PACK, N], F32)
         g = sb("g", [P, PACK], F32)
-        gq = sb("gq", [P, PACK], F32)
-        g2 = sb("g2", [P, 1], F32)
-        gm = sb("gm", [P, 1], F32)
+        ident = sb("ident", [P, P], F32)
         win1 = [sb(f"win1_{t}", [P, 2 * S], F32) for t in range(PACK)]
         lo, hi = slice(0, S), slice(S, 2 * S)
 
@@ -57,9 +56,11 @@ def tile_picked_cahn8_none_p_kernel(tc, x_words, x_scales, w1, gn, w2, offs, wes
         nc.sync.dma_start(west_t[:], west)
         nc.sync.dma_start(east_t[:], east)
         nc.sync.dma_start(w2_raw[:], w2.rearrange("(p j) c -> p j c", j=PACK))
-        nc.gpsimd.tensor_scalar(gq[:], g[:], -0.25, 0.0, MULT, ADD)
-        nc.gpsimd.tensor_scalar(g2[:], g[:, 0:1], 2.0, 0.0, MULT, ADD)
-        nc.gpsimd.tensor_scalar(gm[:], g[:, 0:1], -1.0, 0.0, MULT, ADD)
+        gx = {1.0: g}
+        for factor in (2.0, -1.0, -4.0, 0.5, -2.0):
+            gx[factor] = sb(f"gx{len(gx)}", [P, PACK], F32)
+            nc.gpsimd.tensor_scalar(gx[factor][:], g[:], factor, 0.0, MULT, ADD)
+        make_identity(nc, ident[:])
 
         xg_s = sb("xg_s", [P, S], U8)
         xg = sb("xg", [P, S], U32)
@@ -95,35 +96,55 @@ def tile_picked_cahn8_none_p_kernel(tc, x_words, x_scales, w1, gn, w2, offs, wes
         fwa = [sb(f"fw_{t}", [P, HALF], F32) for t in range(PACK)]
         fw = {(t, 0): fwa[t] for t in range(PACK)}
         fw[0, 1] = sb("fw_0b", [P, HALF], F32)
-        fw[1, 1] = sb("fw_1b", [P, HALF], F32)
-        fw[2, 1] = gy[3]
-        fw[3, 1] = fwa[3]
-        z = [sb(f"z_{h}", [P, PACK, HALF], F32) for h in range(2)]
+        fw[1, 1] = se[3][:, HALF:S]
+        fw[2, 1] = se[3]
+        fw[3, 1] = sb("fw_3b", [P, HALF], F32)
+        z = [None, sb("z_1", [P, PACK, HALF], F32)]
+        ew = [sb(f"ew_{t}", [P, HALF], F32) for t in range(PACK)]
+        zt = [bank(5 + j, [P, PACK, P], f"zt{j}") for j in range(2)]
 
         def s_all(t):
             nc.scalar.activation(win1[t][:, hi], pre[t][:], ACT.Tanh)
             nc.scalar.copy(win1[t][:, lo], pre[t][:])
             nc.scalar.activation(y2[t][:], win1[t][:, hi], ACT.Square)
-            nc.scalar.activation(gy[t][:], win1[t][:, hi], ACT.Copy, scale=g[:, t : t + 1])
+            nc.scalar.activation(gy[t][:, 0:HALF], win1[t][:, S : S + HALF], ACT.Copy, scale=g[:, t : t + 1])
+            nc.scalar.activation(gy[t][:, HALF:S], win1[t][:, S + HALF : 2 * S], ACT.Copy, scale=gx[-2.0][:, t : t + 1])
             nc.scalar.activation(sw[t][:], win1[t][:].indirect(west_t[:]), ACT.Sigmoid, scale=2.0)
             nc.scalar.activation(se[t][:], win1[t][:].indirect(east_t[:]), ACT.Sigmoid, scale=2.0)
 
         halves = [slice(0, HALF), slice(HALF, S)]
 
         def v_c(t):
-            for c in halves:
-                nc.vector.scalar_tensor_tensor(cube[t][:, c], gy[t][:, c], 0.25, y2[t][:, c], MULT, MULT)
+            for c, factor in zip(halves, (-0.5, 0.25)):
+                nc.vector.scalar_tensor_tensor(cube[t][:, c], gy[t][:, c], factor, y2[t][:, c], MULT, MULT)
 
         def v_t(t):
             for c in halves:
-                nc.vector.scalar_tensor_tensor(part[t][:, c], sw[t][:, c], gq[:, t : t + 1], cube[t][:, c], MULT, ADD)
+                nc.vector.scalar_tensor_tensor(part[t][:, c], sw[t][:, c], gx[0.5][:, t : t + 1], cube[t][:, c], MULT, ADD)
 
         def v_p(t, add):
             for c in halves:
-                nc.vector.scalar_tensor_tensor(win2[t][:, c], se[t][:, c], gq[:, t : t + 1], add[:, c], MULT, ADD)
+                nc.vector.scalar_tensor_tensor(win2[t][:, c], se[t][:, c], gx[0.5][:, t : t + 1], add[:, c], MULT, ADD)
+
+        def v_gather(dst, t, lst):
+            nc.vector.tensor_scalar(dst[:], win2[t][:].indirect(lst[:, 0:16]), -0.5, 0.0, MULT, ADD)
+
+        def pe_sum(t):
+            terms = [gy[t], win2[t], fwa[t], ew[t]]
+            for i, term in enumerate(terms):
+                for j in range(2):
+                    nc.tensor.matmul(zt[j][:, t, :], lhsT=term[:, j * P : (j + 1) * P], rhs=ident[:], start=i == 0, stop=i == 3, is_transpose=True)
+
+        def turn_back(j):
+            zt_bf = sb(f"zt_bf{j}", [P, PACK * P], BF16)
+            nc.scalar.copy(zt_bf[:].rearrange("q (u p e) -> q u p e", u=2, e=2), zt[j][:].rearrange("q (u e) p -> q u p e", e=2))
+            back = bank(4 * j, [P, 2, P], f"back{j}")
+            for u in range(2):
+                nc.tensor.transpose(back[:, u, :], zt_bf[:].bitcast(F32)[:, u * P : (u + 1) * P], ident[:])
+            nc.scalar.copy(z_bf[0][:].bitcast(F32)[:, 2 * P * j : 2 * P * (j + 1)].rearrange("p (q u) -> p q u", u=2), back[:].rearrange("p u q -> p q u"))
 
         def v_e(t):
-            for c in halves:
+            for c in halves[1:]:
                 nc.vector.scalar_tensor_tensor(ctr[t][:, c], win2[t][:, c], -2.0, gy[t][:, c], MULT, ADD)
 
         def v_f(t, h):
@@ -138,14 +159,15 @@ def tile_picked_cahn8_none_p_kernel(tc, x_words, x_scales, w1, gn, w2, offs, wes
         w2_codes = sb("w2_codes", [P, N], U32)
         w2_scales = sb("w2_scales", [P, N], U8)
         chunks = [(0, 256), (256, 384), (384, 512)]
-        z_bf = [sb(f"z_bf{c}", [P, (b - a) * PACK], BF16) for c, (a, b) in enumerate(chunks)]
+        z_bf0 = sb("z_bf0", [P, HALF * PACK], BF16)
+        z_bf = [z_bf0, z_bf0[:, 0:512], z_bf0[:, 512:1024]]
         z_codes = [sb(f"z_codes{c}", [P, b - a], U32) for c, (a, b) in enumerate(chunks)]
         z_scales = [sb(f"z_scales{c}", [P, b - a], U8) for c, (a, b) in enumerate(chunks)]
         out_rows = out.rearrange("(a p) j -> p a j", p=P)
 
-        def weave(c, a, b, copy):
-            h = a // HALF
-            copy(z_bf[c][:, (a - chunks[c][0]) * PACK : (b - chunks[c][0]) * PACK].rearrange("p (c i t) -> p c t i", i=4, t=PACK), z[h][:, :, a - h * HALF : b - h * HALF].rearrange("p t (c i) -> p c t i", i=4))
+        def weave(c):
+            a, b = chunks[c]
+            nc.vector.tensor_scalar(z_bf[c].rearrange("p (c i t) -> p c t i", i=4, t=PACK), z[1][:, :, a - HALF : b - HALF].rearrange("p t (c i) -> p c t i", i=4), -0.5, None, MULT)
 
         def quant(c):
             nc.vector.quantize_mx(z_codes[c][:].bitcast(FP8X4), z_scales[c][:], z_bf[c][:])
@@ -162,52 +184,56 @@ def tile_picked_cahn8_none_p_kernel(tc, x_words, x_scales, w1, gn, w2, offs, wes
             queue.dma_start(out_rows[:, first : first + count, j0:j1], res[:])
 
         def second(t):
-            v_f(t, 0)
-            v_f(t, 1)
-            v_z(t, 0, HALF)
-            v_z(t, HALF, S)
+            v_gather(fwa[t], t, west_t)
+            v_e(t)
+            v_gather(ew[t], t, east_t)
+            pe_sum(t)
 
         def chain(t):
             s_all(t)
             v_c(t)
             v_t(t)
             v_p(t, part[t])
-            v_e(t)
 
         for h, c in enumerate(halves):
             nc.vector.tensor_copy(sw[0][:, c], win1[0][:].indirect(west_t[:, 16 * h : 16 * h + 16]))
         nc.scalar.activation(y2[0][:], win1[0][:, lo], ACT.Square, scale=2.0, bias=-1.0)
-        nc.scalar.activation(gy[0][:], win1[0][:, lo], ACT.Identity, scale=g2[:], bias=gm[:])
+        nc.scalar.activation(gy[0][:, 0:HALF], win1[0][:, 0:HALF], ACT.Identity, scale=gx[2.0][:, 0:1], bias=gx[-1.0][:, 0:1])
+        nc.scalar.activation(gy[0][:, HALF:S], win1[0][:, HALF:S], ACT.Identity, scale=gx[-4.0][:, 0:1], bias=gx[2.0][:, 0:1])
         for h, c in enumerate(halves):
             nc.vector.tensor_tensor(se[0][:, c], win1[0][:].indirect(east_t[:, 16 * h : 16 * h + 16]), sw[0][:, c], ADD)
         v_c(0)
         v_p(0, cube[0])
-        v_e(0)
         second(0)
+        v_f(0, 1)
+        v_z(0, HALF, S)
         chain(1)
         second(1)
         chain(2)
-        v_f(2, 0)
-        v_z(2, 0, HALF)
+        second(2)
         chain(3)
-        v_f(3, 0)
-        v_f(2, 1)
-        v_z(3, 0, HALF)
+        v_gather(fwa[3], 3, west_t)
+        v_gather(ew[3], 3, east_t)
+        pe_sum(3)
+        turn_back(0)
+        turn_back(1)
         nc.scalar.copy(w2_bf[:].rearrange("p (c i j) -> p c j i", i=4, j=PACK), w2_raw[:].rearrange("p j (c i) -> p c j i", i=4))
-        weave(0, 128, 256, nc.scalar.copy)
-        v_z(2, 256, 512)
-        weave(0, 0, 128, nc.vector.tensor_copy)
+        v_e(3)
+        v_f(2, 1)
+        v_f(1, 1)
+        v_z(2, HALF, S)
         v_f(3, 1)
+        v_z(1, HALF, S)
         nc.vector.quantize_mx(w2_codes[:].bitcast(FP8X4), w2_scales[:], w2_bf[:])
         v_z(3, 256, 384)
         quant(0)
-        product(0, 0, 2, 4, nc.scalar.copy)
-        product(0, 2, 2, 5, nc.scalar.copy)
-        weave(1, 256, 384, nc.vector.tensor_copy)
+        product(0, 0, 2, 1, nc.scalar.copy)
+        product(0, 2, 2, 2, nc.scalar.copy)
         v_z(3, 384, 512)
+        weave(1)
+        weave(2)
         quant(1)
-        product(1, 0, 4, 0, nc.scalar.copy)
-        weave(2, 384, 512, nc.vector.tensor_copy)
         quant(2)
-        product(2, 0, 2, 6, nc.scalar.copy, nc.scalar)
-        product(2, 2, 2, 7, nc.vector.tensor_copy)
+        product(1, 0, 4, 3, nc.scalar.copy)
+        product(2, 0, 2, 7, nc.scalar.copy, nc.scalar)
+        product(2, 2, 2, 0, nc.vector.tensor_copy)

@@ -43,8 +43,9 @@ def tile_picked_cahn8_none_p_kernel(tc, x_words, x_scales, w1, gn, w2, offs, wes
         w2_raw = sb("w2_raw", [P, PACK, N], F32)
         g = sb("g", [P, PACK], F32)
         ident = sb("ident", [P, P], F32)
-        win1 = [sb(f"win1_{t}", [P, 2 * S], F32) for t in range(PACK)]
         lo, hi = slice(0, S), slice(S, 2 * S)
+        halves = [slice(0, HALF), slice(HALF, S)]
+        TURNED = 3 * P
 
         nc.gpsimd.memset(xs[:].bitcast(I32), 0)
         nc.sync.dma_start(xw[:], x_words[0].rearrange("p n t -> p (n t)").bitcast(I32))
@@ -57,10 +58,13 @@ def tile_picked_cahn8_none_p_kernel(tc, x_words, x_scales, w1, gn, w2, offs, wes
         nc.sync.dma_start(east_t[:], east)
         nc.sync.dma_start(w2_raw[:], w2.rearrange("(p j) c -> p j c", j=PACK))
         gx = {1.0: g}
-        for factor in (2.0, -1.0, -4.0, 0.5, -2.0):
+        for factor in (0.5, -0.25, -0.5, -2.0):
             gx[factor] = sb(f"gx{len(gx)}", [P, PACK], F32)
             nc.gpsimd.tensor_scalar(gx[factor][:], g[:], factor, 0.0, MULT, ADD)
         make_identity(nc, ident[:])
+
+        def gain(factor, t):
+            return gx[factor][:, t : t + 1]
 
         xg_s = sb("xg_s", [P, S], U8)
         xg = sb("xg", [P, S], U32)
@@ -78,96 +82,102 @@ def tile_picked_cahn8_none_p_kernel(tc, x_words, x_scales, w1, gn, w2, offs, wes
             for e in range(2):
                 cols = slice(e * P, (e + 1) * P)
                 t = 2 * u + e
-                pieces = [(pre[t], slice(0, S))] if t else [(pre0[0], slice(0, HALF)), (pre0[1], slice(HALF, S))]
+                pieces = [(pre[t], slice(0, S))] if t else [(pre0[0], halves[0]), (pre0[1], halves[1])]
                 for acc, c in pieces:
                     nc.tensor.matmul_mx(acc[:], lhsT=w1_codes[:, cols].bitcast(FP8X4), lhsT_scale=w1_scales[:, cols],
                                         rhs=xg[:, c].bitcast(FP8X4), rhs_scale=xg_s[:, c], start=True, stop=True)
-        for h in range(2):
-            nc.scalar.activation(win1[0][:, h * HALF : (h + 1) * HALF], pre0[h][:], ACT.Sigmoid, scale=2.0)
 
-        win2 = [sb(f"win2_{t}", [P, 2 * S if t < 3 else S], F32) for t in range(PACK)]
-        part = [win2[t][:, hi] for t in range(3)] + [sb("part3", [P, S], F32)[:]]
-        y2 = [sb(f"y2_{t}", [P, S], F32) for t in range(PACK)]
-        gy = [sb(f"gy_{t}", [P, S], F32) for t in range(PACK)]
-        sw = [sb(f"sw_{t}", [P, S], F32) for t in range(PACK)]
-        se = [sb(f"se_{t}", [P, S], F32) for t in range(PACK)]
-        cube = [sb(f"cube_{t}", [P, S], F32) for t in range(PACK)]
-        ctr = [sb(f"ctr_{t}", [P, S], F32) for t in range(PACK)]
-        fwa = [sb(f"fw_{t}", [P, HALF], F32) for t in range(PACK)]
-        fw = {(t, 0): fwa[t] for t in range(PACK)}
-        fw[0, 1] = sb("fw_0b", [P, HALF], F32)
-        fw[1, 1] = se[3][:, HALF:S]
-        fw[2, 1] = se[3]
-        fw[3, 1] = sb("fw_3b", [P, HALF], F32)
-        z = [None, sb("z_1", [P, PACK, HALF], F32)]
-        ew = [sb(f"ew_{t}", [P, HALF], F32) for t in range(PACK)]
-        zt = [bank(5 + j, [P, PACK, P], f"zt{j}") for j in range(2)]
+        def planes(name, width):
+            return [sb(f"{name}_{t}", [P, width], F32) for t in range(PACK)]
 
-        def s_all(t):
-            nc.scalar.activation(win1[t][:, hi], pre[t][:], ACT.Tanh)
+        win1 = [sb("win1_0", [P, S], F32)] + [sb(f"win1_{t}", [P, 2 * S], F32) for t in range(1, PACK)]
+        r, part, cube, y2, sw, se = [planes(name, S) for name in ("r", "part", "cube", "y2", "sw", "se")]
+        gy_tail, ctr = planes("gy_tail", P), planes("ctr", P)
+        fw, fe = planes("fw", TURNED), planes("fe", TURNED)
+        gy2 = [part[0][:, 0:P]] + [sb(f"gy2_{t}", [P, P], F32)[:] for t in range(1, PACK)]
+        z4 = sb("z4", [P, PACK, P], F32)
+        last = slice(TURNED, S)
+
+        def look(lst, a, b):
+            return lst[:, a // 16 : b // 16]
+
+        def first_plane():
+            s = sw[0]
+            for h, c in enumerate(halves):
+                nc.scalar.activation(s[:, c], pre0[h][:], ACT.Sigmoid, scale=2.0)
+            for c in halves:
+                nc.scalar.activation(y2[0][:, c], s[:, c], ACT.Square, scale=2.0, bias=-1.0)
+            for c in halves:
+                nc.vector.tensor_scalar(win1[0][:, c], s[:, c], gain(0.5, 0), gain(-0.25, 0), MULT, ADD)
+            for c in halves:
+                nc.vector.scalar_tensor_tensor(cube[0][:, c], win1[0][:, c], -2.0, y2[0][:, c], MULT, MULT)
+            for c in halves:
+                nc.vector.tensor_tensor(part[0][:, c], win1[0][:].indirect(look(west_t, c.start, c.stop)), cube[0][:, c], ADD)
+            for c in halves:
+                nc.vector.tensor_tensor(r[0][:, c], win1[0][:].indirect(look(east_t, c.start, c.stop)), part[0][:, c], ADD)
+            nc.vector.tensor_scalar(gy2[0], win1[0][:, last], -8.0, None, MULT)
+
+        def later_plane(t):
+            y = win1[t][:, hi]
+            nc.scalar.activation(y, pre[t][:], ACT.Tanh)
             nc.scalar.copy(win1[t][:, lo], pre[t][:])
-            nc.scalar.activation(y2[t][:], win1[t][:, hi], ACT.Square)
-            nc.scalar.activation(gy[t][:, 0:HALF], win1[t][:, S : S + HALF], ACT.Copy, scale=g[:, t : t + 1])
-            nc.scalar.activation(gy[t][:, HALF:S], win1[t][:, S + HALF : 2 * S], ACT.Copy, scale=gx[-2.0][:, t : t + 1])
+            nc.scalar.activation(y2[t][:], y, ACT.Square)
             nc.scalar.activation(sw[t][:], win1[t][:].indirect(west_t[:]), ACT.Sigmoid, scale=2.0)
             nc.scalar.activation(se[t][:], win1[t][:].indirect(east_t[:]), ACT.Sigmoid, scale=2.0)
-
-        halves = [slice(0, HALF), slice(HALF, S)]
-
-        def v_c(t):
-            for c, factor in zip(halves, (-0.5, 0.25)):
-                nc.vector.scalar_tensor_tensor(cube[t][:, c], gy[t][:, c], factor, y2[t][:, c], MULT, MULT)
-
-        def v_t(t):
             for c in halves:
-                nc.vector.scalar_tensor_tensor(part[t][:, c], sw[t][:, c], gx[0.5][:, t : t + 1], cube[t][:, c], MULT, ADD)
-
-        def v_p(t, add):
+                nc.vector.scalar_tensor_tensor(cube[t][:, c], y[:, c], gain(-0.5, t), y2[t][:, c], MULT, MULT)
+            nc.vector.tensor_scalar(gy_tail[t][:], y[:, HALF:TURNED], gain(1.0, t), None, MULT)
+            nc.vector.tensor_scalar(gy2[t], y[:, last], gain(-2.0, t), None, MULT)
             for c in halves:
-                nc.vector.scalar_tensor_tensor(win2[t][:, c], se[t][:, c], gx[0.5][:, t : t + 1], add[:, c], MULT, ADD)
+                nc.vector.scalar_tensor_tensor(part[t][:, c], sw[t][:, c], gain(0.5, t), cube[t][:, c], MULT, ADD)
+            for c in halves:
+                nc.vector.scalar_tensor_tensor(r[t][:, c], se[t][:, c], gain(0.5, t), part[t][:, c], MULT, ADD)
+            nc.vector.tensor_scalar(se[t][:, halves[0]], y[:, halves[0]], gain(1.0, t), None, MULT)
 
-        def v_gather(dst, t, lst):
-            nc.vector.tensor_scalar(dst[:], win2[t][:].indirect(lst[:, 0:16]), -0.5, 0.0, MULT, ADD)
+        def fetch_turned(t):
+            for a, b in ((0, HALF), (HALF, TURNED)):
+                for dst, lst in ((fw[t], west_t), (fe[t], east_t)):
+                    nc.vector.tensor_scalar(dst[:, a:b], r[t][:].indirect(look(lst, a, b)), -0.5, 0.0, MULT, ADD)
 
-        def pe_sum(t):
-            terms = [gy[t], win2[t], fwa[t], ew[t]]
-            for i, term in enumerate(terms):
-                for j in range(2):
-                    nc.tensor.matmul(zt[j][:, t, :], lhsT=term[:, j * P : (j + 1) * P], rhs=ident[:], start=i == 0, stop=i == 3, is_transpose=True)
+        def terms(t, j):
+            c = slice(j * P, (j + 1) * P)
+            own = [win1[0][:, c]] * 4 if t == 0 else [se[t][:, c] if j < 2 else gy_tail[t][:]]
+            return [r[t][:, c]] + own + [fw[t][:, c], fe[t][:, c]]
 
-        def turn_back(j):
-            zt_bf = sb(f"zt_bf{j}", [P, PACK * P], BF16)
-            nc.scalar.copy(zt_bf[:].rearrange("q (u p e) -> q u p e", u=2, e=2), zt[j][:].rearrange("q (u e) p -> q u p e", e=2))
-            back = bank(4 * j, [P, 2, P], f"back{j}")
-            for u in range(2):
-                nc.tensor.transpose(back[:, u, :], zt_bf[:].bitcast(F32)[:, u * P : (u + 1) * P], ident[:])
-            nc.scalar.copy(z_bf[0][:].bitcast(F32)[:, 2 * P * j : 2 * P * (j + 1)].rearrange("p (q u) -> p q u", u=2), back[:].rearrange("p u q -> p q u"))
+        def add_turned(dst, term, i, count):
+            nc.tensor.matmul(dst, lhsT=term, rhs=ident[:], start=i == 0, stop=i == count - 1, is_transpose=True)
 
-        def v_e(t):
-            for c in halves[1:]:
-                nc.vector.scalar_tensor_tensor(ctr[t][:, c], win2[t][:, c], -2.0, gy[t][:, c], MULT, ADD)
+        zt_a = [bank(0, [P, 2, 2, P], "zt_a0"), bank(4, [P, 1, 2, P], "zt_a1")]
+        zt_b = [bank(5 + j, [P, 2, P], f"zt_b{j}") for j in range(3)]
 
-        def v_f(t, h):
-            a, b = h * HALF, (h + 1) * HALF
-            nc.vector.tensor_tensor(fw[t, h][:, 0:HALF], win2[t][:].indirect(west_t[:, a // 16 : b // 16]), ctr[t][:, a:b], ADD)
+        def sum_turned(t):
+            if t < 2:
+                for j in range(3):
+                    for i, term in enumerate(terms(t, j)):
+                        add_turned(zt_a[j // 2][:, j % 2, t, :], term, i, len(terms(t, j)))
+            else:
+                for js, steps in (((0, 1, 2), (0, 1)), ((0, 1), (2, 3)), ((2,), (2, 3))):
+                    for i in steps:
+                        for j in js:
+                            add_turned(zt_b[j][:, t - 2, :], terms(t, j)[i], i, 4)
 
-        def v_z(t, a, b):
-            h = a // HALF
-            nc.vector.tensor_tensor(z[h][:, t, a - h * HALF : b - h * HALF], win2[t][:].indirect(east_t[:, a // 16 : b // 16]), fw[t, h][:, a - h * HALF : b - h * HALF], ADD)
+        def centre(t):
+            nc.vector.scalar_tensor_tensor(ctr[t][:], r[t][:, last], -2.0, gy2[t], MULT, ADD)
+
+        def fetch_west(t, dst):
+            nc.vector.tensor_tensor(dst, r[t][:].indirect(look(west_t, TURNED, S)), ctr[t][:], ADD)
+
+        def fetch_east(t, src):
+            nc.vector.tensor_tensor(z4[:, t, :], r[t][:].indirect(look(east_t, TURNED, S)), src, ADD)
 
         w2_bf = sb("w2_bf", [P, N * PACK], BF16)
         w2_codes = sb("w2_codes", [P, N], U32)
         w2_scales = sb("w2_scales", [P, N], U8)
-        chunks = [(0, 256), (256, 384), (384, 512)]
-        z_bf0 = sb("z_bf0", [P, HALF * PACK], BF16)
-        z_bf = [z_bf0, z_bf0[:, 0:512], z_bf0[:, 512:1024]]
+        z_bf = [sb("z_bf01", [P, 2 * P * PACK], BF16), sb("z_bf2", [P, P * PACK], BF16), sb("z_bf3", [P, P * PACK], BF16)]
+        chunks = [(0, HALF), (HALF, TURNED), (TURNED, S)]
         z_codes = [sb(f"z_codes{c}", [P, b - a], U32) for c, (a, b) in enumerate(chunks)]
         z_scales = [sb(f"z_scales{c}", [P, b - a], U8) for c, (a, b) in enumerate(chunks)]
         out_rows = out.rearrange("(a p) j -> p a j", p=P)
-
-        def weave(c):
-            a, b = chunks[c]
-            nc.vector.tensor_scalar(z_bf[c].rearrange("p (c i t) -> p c t i", i=4, t=PACK), z[1][:, :, a - HALF : b - HALF].rearrange("p t (c i) -> p c t i", i=4), -0.5, None, MULT)
 
         def quant(c):
             nc.vector.quantize_mx(z_codes[c][:].bitcast(FP8X4), z_scales[c][:], z_bf[c][:])
@@ -183,57 +193,47 @@ def tile_picked_cahn8_none_p_kernel(tc, x_words, x_scales, w1, gn, w2, offs, wes
             copy(res[:], acc[:])
             queue.dma_start(out_rows[:, first : first + count, j0:j1], res[:])
 
-        def second(t):
-            v_gather(fwa[t], t, west_t)
-            v_e(t)
-            v_gather(ew[t], t, east_t)
-            pe_sum(t)
+        first_plane()
+        fetch_turned(0)
+        sum_turned(0)
+        centre(0)
+        for t in range(1, PACK):
+            later_plane(t)
+            fetch_turned(t)
+            sum_turned(t)
+            centre(t)
 
-        def chain(t):
-            s_all(t)
-            v_c(t)
-            v_t(t)
-            v_p(t, part[t])
-
-        for h, c in enumerate(halves):
-            nc.vector.tensor_copy(sw[0][:, c], win1[0][:].indirect(west_t[:, 16 * h : 16 * h + 16]))
-        nc.scalar.activation(y2[0][:], win1[0][:, lo], ACT.Square, scale=2.0, bias=-1.0)
-        nc.scalar.activation(gy[0][:, 0:HALF], win1[0][:, 0:HALF], ACT.Identity, scale=gx[2.0][:, 0:1], bias=gx[-1.0][:, 0:1])
-        nc.scalar.activation(gy[0][:, HALF:S], win1[0][:, HALF:S], ACT.Identity, scale=gx[-4.0][:, 0:1], bias=gx[2.0][:, 0:1])
-        for h, c in enumerate(halves):
-            nc.vector.tensor_tensor(se[0][:, c], win1[0][:].indirect(east_t[:, 16 * h : 16 * h + 16]), sw[0][:, c], ADD)
-        v_c(0)
-        v_p(0, cube[0])
-        second(0)
-        v_f(0, 1)
-        v_z(0, HALF, S)
-        chain(1)
-        second(1)
-        chain(2)
-        second(2)
-        chain(3)
-        v_gather(fwa[3], 3, west_t)
-        v_gather(ew[3], 3, east_t)
-        pe_sum(3)
-        turn_back(0)
-        turn_back(1)
+        pair_a = sb("pair_a", [P, 3, 2 * P], BF16)
+        pair_b = [sb(f"pair_b{j}", [P, 2 * P], BF16) for j in range(3)]
+        back = [bank(1 + j, [P, 2, P], f"back{j}") for j in range(3)]
+        nc.scalar.copy(pair_a[:, 0:2, :].rearrange("q j (p e) -> q j p e", e=2), zt_a[0][:].rearrange("q j e p -> q j p e"))
+        nc.scalar.copy(pair_a[:, 2:3, :].rearrange("q j (p e) -> q j p e", e=2), zt_a[1][:].rearrange("q j e p -> q j p e"))
+        for j in range(3):
+            nc.tensor.transpose(back[j][:, 0, :], pair_a[:, j, :].bitcast(F32), ident[:])
         nc.scalar.copy(w2_bf[:].rearrange("p (c i j) -> p c j i", i=4, j=PACK), w2_raw[:].rearrange("p j (c i) -> p c j i", i=4))
-        v_e(3)
-        v_f(2, 1)
-        v_f(1, 1)
-        v_z(2, HALF, S)
-        v_f(3, 1)
-        v_z(1, HALF, S)
+        for j in range(3):
+            nc.scalar.copy(pair_b[j][:].rearrange("q (p e) -> q p e", e=2), zt_b[j][:].rearrange("q e p -> q p e"))
+            nc.tensor.transpose(back[j][:, 1, :], pair_b[j][:].bitcast(F32), ident[:])
+        for j in range(3):
+            words = z_bf[j // 2][:].bitcast(F32)[:, 2 * P * (j % 2) : 2 * P * (j % 2 + 1)]
+            nc.scalar.copy(words.rearrange("p (q u) -> p q u", u=2), back[j][:].rearrange("p u q -> p q u"))
+
+        held = [part[3][:, 0:P], part[3][:, HALF : HALF + P], z_bf[0][:].bitcast(F32)[:, 0:P], z_bf[1][:].bitcast(F32)[:, 0:P]]
+        for t in (0, 1):
+            fetch_west(t, held[t])
         nc.vector.quantize_mx(w2_codes[:].bitcast(FP8X4), w2_scales[:], w2_bf[:])
-        v_z(3, 256, 384)
+        for t in (0, 1):
+            fetch_east(t, held[t])
         quant(0)
-        product(0, 0, 2, 1, nc.scalar.copy)
-        product(0, 2, 2, 2, nc.scalar.copy)
-        v_z(3, 384, 512)
-        weave(1)
-        weave(2)
         quant(1)
+        product(0, 0, 2, 0, nc.scalar.copy)
+        product(0, 2, 2, 4, nc.scalar.copy)
+        product(1, 0, 4, 5, nc.scalar.copy)
+        for t in (2, 3):
+            fetch_west(t, held[t])
+        for t in (2, 3):
+            fetch_east(t, held[t])
+        nc.vector.tensor_scalar(z_bf[2][:].rearrange("p (c i t) -> p c t i", i=4, t=PACK), z4[:].rearrange("p t (c i) -> p c t i", i=4), -0.5, None, MULT)
         quant(2)
-        product(1, 0, 4, 3, nc.scalar.copy)
-        product(2, 0, 2, 7, nc.scalar.copy, nc.scalar)
-        product(2, 2, 2, 0, nc.vector.tensor_copy)
+        product(2, 0, 2, 6, nc.scalar.copy, nc.scalar)
+        product(2, 2, 2, 7, nc.vector.tensor_copy)

@@ -16,6 +16,7 @@ FP8X4 = mybir.dt.float8_e4m3fn_x4
 ACT = mybir.ActivationFunctionType
 MULT = mybir.AluOpType.mult
 ADD = mybir.AluOpType.add
+SUB = mybir.AluOpType.subtract
 
 P = 128
 PACK = 4
@@ -39,64 +40,95 @@ def tile_picked_cahn8_none_p_kernel(tc, x_words, x_scales, w1, gn, w2, offs, wes
         east_t = sb("east_t", [P, S // 16], U16)
         xw = sb("xw", [P, T], I32)
         xs = sb("xs", [P, T], U8)
-        w1_raw = sb("w1_raw", [P, PACK, H], F32)
-        w2_raw = sb("w2_raw", [P, PACK, N], F32)
+        w1_raw = [sb(f"w1_raw{h}", [P, PACK, H // 2], F32) for h in range(2)]
+        w2_raw = [sb(f"w2_raw{h}", [P, PACK, N // 2], F32) for h in range(2)]
         g = sb("g", [P, PACK], F32)
         ident = sb("ident", [P, P], F32)
         lo, hi = slice(0, S), slice(S, 2 * S)
         halves = [slice(0, HALF), slice(HALF, S)]
         TURNED = 3 * P
+        last = slice(TURNED, S)
 
+        w1_rows = w1.rearrange("(p j) c -> p j c", j=PACK)
+        w2_rows = w2.rearrange("(p j) c -> p j c", j=PACK)
         nc.gpsimd.memset(xs[:].bitcast(I32), 0)
         nc.sync.dma_start(xw[:], x_words[0].rearrange("p n t -> p (n t)").bitcast(I32))
         nc.sync.dma_start(offs_t[:], offs)
         for q in range(4):
             nc.sync.dma_start(xs[32 * q : 32 * q + 4, :].bitcast(I32), x_scales[0, 4 * q : 4 * q + 4, :].bitcast(I32))
-        nc.sync.dma_start(w1_raw[:], w1.rearrange("(p j) c -> p j c", j=PACK))
-        nc.scalar.dma_start(g[:], gn.rearrange("(p t) o -> p (t o)", t=PACK))
+        for h in range(2):
+            nc.sync.dma_start(w1_raw[h][:], w1_rows[:, :, halves[h]])
+        nc.sync.dma_start(g[:], gn.rearrange("(p t) o -> p (t o)", t=PACK))
         nc.sync.dma_start(west_t[:], west)
         nc.sync.dma_start(east_t[:], east)
-        nc.sync.dma_start(w2_raw[:], w2.rearrange("(p j) c -> p j c", j=PACK))
+        for h in range(2):
+            nc.sync.dma_start(w2_raw[h][:], w2_rows[:, :, halves[h]])
+        make_identity(nc, ident[:])
         gx = {1.0: g}
-        for factor in (0.5, -0.25, -0.5, -2.0):
+        for factor in (0.5, 2.0):
             gx[factor] = sb(f"gx{len(gx)}", [P, PACK], F32)
             nc.gpsimd.tensor_scalar(gx[factor][:], g[:], factor, 0.0, MULT, ADD)
-        make_identity(nc, ident[:])
 
         def gain(factor, t):
             return gx[factor][:, t : t + 1]
 
         xg_s = sb("xg_s", [P, S], U8)
         xg = sb("xg", [P, S], U32)
+        w1_bf = sb("w1_bf", [P, H * PACK], BF16)
+        w1_codes = sb("w1_codes", [P, H], U32)
+        w1_scales = sb("w1_scales", [P, H], U8)
+        w1_woven = w1_bf[:].rearrange("p (t m j) -> p m j t", t=PACK, j=PACK)
+
+        def weave_w1(h, ts):
+            nc.vector.tensor_copy(w1_woven[:, h * P // 2 : (h + 1) * P // 2, :, ts], w1_raw[h][:].rearrange("p j (m t) -> p m j t", t=PACK)[:, :, :, ts])
+
+        def quant_w1(t0, t1):
+            nc.vector.quantize_mx(w1_codes[:, t0 * P : t1 * P].bitcast(FP8X4), w1_scales[:, t0 * P : t1 * P], w1_bf[:, t0 * P * PACK : t1 * P * PACK])
+
         nc.vector.tensor_copy(xg[:], xw[:].bitcast(U32).indirect(offs_t[:]))
         nc.vector.tensor_copy(xg_s[:], xs[:].indirect(offs_t[:]))
+        weave_w1(0, slice(0, PACK))
+        weave_w1(1, slice(0, 2))
+        weave_w1(1, slice(2, PACK))
+        quant_w1(0, 2)
+        quant_w1(2, PACK)
         pre0 = [bank(4 * h, [P, HALF], f"pre0{h}") for h in range(2)]
         pre = [None] + [bank(t, [P, S], f"pre{t}") for t in range(1, PACK)]
-        w1_view = w1_raw[:].rearrange("p j (m t) -> p m j t", t=PACK)
-        for u in range(2):
-            w1_bf = sb("w1_bf", [P, 2 * P * PACK], BF16)
-            w1_codes = sb(f"w1_codes{u}", [P, 2 * P], U32)
-            w1_scales = sb(f"w1_scales{u}", [P, 2 * P], U8)
-            nc.vector.tensor_copy(w1_bf[:].rearrange("p (t m j) -> p m j t", t=2, j=PACK), w1_view[:, :, :, 2 * u : 2 * u + 2])
-            nc.vector.quantize_mx(w1_codes[:].bitcast(FP8X4), w1_scales[:], w1_bf[:])
-            for e in range(2):
-                cols = slice(e * P, (e + 1) * P)
-                t = 2 * u + e
-                pieces = [(pre[t], slice(0, S))] if t else [(pre0[0], halves[0]), (pre0[1], halves[1])]
-                for acc, c in pieces:
-                    nc.tensor.matmul_mx(acc[:], lhsT=w1_codes[:, cols].bitcast(FP8X4), lhsT_scale=w1_scales[:, cols],
-                                        rhs=xg[:, c].bitcast(FP8X4), rhs_scale=xg_s[:, c], start=True, stop=True)
+
+        def first_product(acc, t, c):
+            cols = slice(t * P, (t + 1) * P)
+            nc.tensor.matmul_mx(acc, lhsT=w1_codes[:, cols].bitcast(FP8X4), lhsT_scale=w1_scales[:, cols],
+                                rhs=xg[:, c].bitcast(FP8X4), rhs_scale=xg_s[:, c], start=True, stop=True)
+
+        for h, c in enumerate(halves):
+            first_product(pre0[h][:], 0, c)
+        for t in range(1, PACK):
+            first_product(pre[t][:], t, slice(0, S))
+
+        w2_bf = [sb(f"w2_bf{h}", [P, HALF * PACK], BF16) for h in range(2)]
+        w2_codes = sb("w2_codes", [P, N], U32)
+        w2_scales = sb("w2_scales", [P, N], U8)
+
+        def weave_w2(h, copy):
+            copy(w2_bf[h][:].rearrange("p (c i j) -> p c j i", i=4, j=PACK), w2_raw[h][:].rearrange("p j (c i) -> p c j i", i=4))
+
+        def quant_w2(h):
+            nc.vector.quantize_mx(w2_codes[:, halves[h]].bitcast(FP8X4), w2_scales[:, halves[h]], w2_bf[h][:])
+
+        weave_w2(0, nc.vector.tensor_copy)
 
         def planes(name, width):
             return [sb(f"{name}_{t}", [P, width], F32) for t in range(PACK)]
 
         win1 = [sb("win1_0", [P, S], F32)] + [sb(f"win1_{t}", [P, 2 * S], F32) for t in range(1, PACK)]
         r, part, cube, y2, sw, se = [planes(name, S) for name in ("r", "part", "cube", "y2", "sw", "se")]
-        gy_tail, ctr = planes("gy_tail", P), planes("ctr", P)
-        fw, fe = planes("fw", TURNED), planes("fe", TURNED)
+        gy = planes("gy", TURNED)
+        own3 = [sb(f"own3_{i}", [P, TURNED], F32) for i in range(2)]
+        wide = [[y2[t + 1][:, c] for c in halves] for t in range(3)] + [[o[:, 0:HALF] for o in own3]]
+        narrow = [[part[t + 1][:, c][:, 0:P] for c in halves] for t in range(2)] + [[cube[2][:, 0:P], part[3][:, 0:P]], [o[:, HALF:TURNED] for o in own3]]
         gy2 = [part[0][:, 0:P]] + [sb(f"gy2_{t}", [P, P], F32)[:] for t in range(1, PACK)]
+        ctr = [gy2[3]] + [sb(f"ctr{t}", [P, P], F32)[:] for t in range(1, PACK)]
         z4 = sb("z4", [P, PACK, P], F32)
-        last = slice(TURNED, S)
 
         def look(lst, a, b):
             return lst[:, a // 16 : b // 16]
@@ -108,41 +140,46 @@ def tile_picked_cahn8_none_p_kernel(tc, x_words, x_scales, w1, gn, w2, offs, wes
             for c in halves:
                 nc.scalar.activation(y2[0][:, c], s[:, c], ACT.Square, scale=2.0, bias=-1.0)
             for c in halves:
-                nc.vector.tensor_scalar(win1[0][:, c], s[:, c], gain(0.5, 0), gain(-0.25, 0), MULT, ADD)
+                nc.vector.tensor_scalar(win1[0][:, c], s[:, c], -0.5, gain(0.5, 0), ADD, MULT)
+            quant_w2(0)
             for c in halves:
-                nc.vector.scalar_tensor_tensor(cube[0][:, c], win1[0][:, c], -2.0, y2[0][:, c], MULT, MULT)
+                nc.vector.scalar_tensor_tensor(cube[0][:, c], win1[0][:, c], 2.0, y2[0][:, c], MULT, MULT)
             for c in halves:
-                nc.vector.tensor_tensor(part[0][:, c], win1[0][:].indirect(look(west_t, c.start, c.stop)), cube[0][:, c], ADD)
+                nc.vector.tensor_tensor(part[0][:, c], win1[0][:].indirect(look(west_t, c.start, c.stop)), cube[0][:, c], SUB)
             for c in halves:
                 nc.vector.tensor_tensor(r[0][:, c], win1[0][:].indirect(look(east_t, c.start, c.stop)), part[0][:, c], ADD)
-            nc.vector.tensor_scalar(gy2[0], win1[0][:, last], -8.0, None, MULT)
+            nc.vector.tensor_scalar(gy2[0], win1[0][:, last], 8.0, None, MULT)
 
-        def later_plane(t):
+        def scalar_plane(t):
             y = win1[t][:, hi]
             nc.scalar.activation(y, pre[t][:], ACT.Tanh)
             nc.scalar.copy(win1[t][:, lo], pre[t][:])
             nc.scalar.activation(y2[t][:], y, ACT.Square)
             nc.scalar.activation(sw[t][:], win1[t][:].indirect(west_t[:]), ACT.Sigmoid, scale=2.0)
             nc.scalar.activation(se[t][:], win1[t][:].indirect(east_t[:]), ACT.Sigmoid, scale=2.0)
+
+        def gain_plane(t):
+            nc.scalar.activation(gy[t][:], win1[t][:, hi][:, 0:TURNED], ACT.Copy, scale=gain(1.0, t))
+
+        def cubes(t):
             for c in halves:
-                nc.vector.scalar_tensor_tensor(cube[t][:, c], y[:, c], gain(-0.5, t), y2[t][:, c], MULT, MULT)
-            nc.vector.tensor_scalar(gy_tail[t][:], y[:, HALF:TURNED], gain(1.0, t), None, MULT)
-            nc.vector.tensor_scalar(gy2[t], y[:, last], gain(-2.0, t), None, MULT)
+                nc.vector.scalar_tensor_tensor(cube[t][:, c], win1[t][:, hi][:, c], gain(0.5, t), y2[t][:, c], MULT, MULT)
+
+        def potential(t):
             for c in halves:
-                nc.vector.scalar_tensor_tensor(part[t][:, c], sw[t][:, c], gain(0.5, t), cube[t][:, c], MULT, ADD)
+                nc.vector.scalar_tensor_tensor(part[t][:, c], sw[t][:, c], gain(0.5, t), cube[t][:, c], MULT, SUB)
             for c in halves:
                 nc.vector.scalar_tensor_tensor(r[t][:, c], se[t][:, c], gain(0.5, t), part[t][:, c], MULT, ADD)
-            nc.vector.tensor_scalar(se[t][:, halves[0]], y[:, halves[0]], gain(1.0, t), None, MULT)
 
-        def fetch_turned(t):
-            for a, b in ((0, HALF), (HALF, TURNED)):
-                for dst, lst in ((fw[t], west_t), (fe[t], east_t)):
-                    nc.vector.tensor_scalar(dst[:, a:b], r[t][:].indirect(look(lst, a, b)), -0.5, 0.0, MULT, ADD)
+        def fetch_turned(t, a, b, sides=slice(0, 2)):
+            for dst, lst in list(zip(narrow[t] if a else wide[t], (west_t, east_t)))[sides]:
+                nc.vector.tensor_scalar(dst, r[t][:].indirect(look(lst, a, b)), -0.5, 0.0, MULT, ADD)
 
         def terms(t, j):
             c = slice(j * P, (j + 1) * P)
-            own = [win1[0][:, c]] * 4 if t == 0 else [se[t][:, c] if j < 2 else gy_tail[t][:]]
-            return [r[t][:, c]] + own + [fw[t][:, c], fe[t][:, c]]
+            own = [win1[0][:, c]] * 4 if t == 0 else [gy[t][:, c]]
+            fetched = [w[:, c] for w in wide[t]] if j < 2 else narrow[t]
+            return [r[t][:, c]] + (fetched + own if t == 2 else own + fetched)
 
         def add_turned(dst, term, i, count):
             nc.tensor.matmul(dst, lhsT=term, rhs=ident[:], start=i == 0, stop=i == count - 1, is_transpose=True)
@@ -151,28 +188,24 @@ def tile_picked_cahn8_none_p_kernel(tc, x_words, x_scales, w1, gn, w2, offs, wes
         zt_b = [bank(5 + j, [P, 2, P], f"zt_b{j}") for j in range(3)]
 
         def sum_turned(t):
-            if t < 2:
-                for j in range(3):
-                    for i, term in enumerate(terms(t, j)):
-                        add_turned(zt_a[j // 2][:, j % 2, t, :], term, i, len(terms(t, j)))
-            else:
-                for js, steps in (((0, 1, 2), (0, 1)), ((0, 1), (2, 3)), ((2,), (2, 3))):
-                    for i in steps:
-                        for j in js:
-                            add_turned(zt_b[j][:, t - 2, :], terms(t, j)[i], i, 4)
+            for j in range(3):
+                for i, term in enumerate(terms(t, j)):
+                    add_turned(zt_a[j // 2][:, j % 2, t, :], term, i, len(terms(t, j)))
+
+        def sum_pair_b(t, steps, js):
+            for i in steps:
+                for j in js:
+                    add_turned(zt_b[j][:, t - 2, :], terms(t, j)[i], i, 4)
 
         def centre(t):
-            nc.vector.scalar_tensor_tensor(ctr[t][:], r[t][:, last], -2.0, gy2[t], MULT, ADD)
+            nc.vector.scalar_tensor_tensor(ctr[t], r[t][:, last], -2.0, gy2[t], MULT, SUB)
 
         def fetch_west(t, dst):
-            nc.vector.tensor_tensor(dst, r[t][:].indirect(look(west_t, TURNED, S)), ctr[t][:], ADD)
+            nc.vector.tensor_tensor(dst, r[t][:].indirect(look(west_t, TURNED, S)), ctr[t], ADD)
 
         def fetch_east(t, src):
             nc.vector.tensor_tensor(z4[:, t, :], r[t][:].indirect(look(east_t, TURNED, S)), src, ADD)
 
-        w2_bf = sb("w2_bf", [P, N * PACK], BF16)
-        w2_codes = sb("w2_codes", [P, N], U32)
-        w2_scales = sb("w2_scales", [P, N], U8)
         z_bf = [sb("z_bf01", [P, 2 * P * PACK], BF16), sb("z_bf2", [P, P * PACK], BF16), sb("z_bf3", [P, P * PACK], BF16)]
         chunks = [(0, HALF), (HALF, TURNED), (TURNED, S)]
         z_codes = [sb(f"z_codes{c}", [P, b - a], U32) for c, (a, b) in enumerate(chunks)]
@@ -194,14 +227,26 @@ def tile_picked_cahn8_none_p_kernel(tc, x_words, x_scales, w1, gn, w2, offs, wes
             queue.dma_start(out_rows[:, first : first + count, j0:j1], res[:])
 
         first_plane()
-        fetch_turned(0)
-        sum_turned(0)
-        centre(0)
         for t in range(1, PACK):
-            later_plane(t)
-            fetch_turned(t)
-            sum_turned(t)
-            centre(t)
+            scalar_plane(t)
+            if t == 1:
+                gain_plane(1)
+        gain_plane(2)
+        gain_plane(3)
+        west_side, east_side = slice(0, 1), slice(1, 2)
+        for t in (1, 2):
+            cubes(t)
+            fetch_turned(t - 1, 0, HALF)
+            potential(t)
+            fetch_turned(t - 1, HALF, TURNED)
+            sum_turned(t - 1)
+        cubes(3)
+        fetch_turned(2, 0, HALF)
+        fetch_turned(2, HALF, TURNED, west_side)
+        potential(3)
+        fetch_turned(2, HALF, TURNED, east_side)
+        fetch_turned(3, 0, HALF)
+        fetch_turned(3, HALF, TURNED)
 
         pair_a = sb("pair_a", [P, 3, 2 * P], BF16)
         pair_b = [sb(f"pair_b{j}", [P, 2 * P], BF16) for j in range(3)]
@@ -210,7 +255,15 @@ def tile_picked_cahn8_none_p_kernel(tc, x_words, x_scales, w1, gn, w2, offs, wes
         nc.scalar.copy(pair_a[:, 2:3, :].rearrange("q j (p e) -> q j p e", e=2), zt_a[1][:].rearrange("q j e p -> q j p e"))
         for j in range(3):
             nc.tensor.transpose(back[j][:, 0, :], pair_a[:, j, :].bitcast(F32), ident[:])
-        nc.scalar.copy(w2_bf[:].rearrange("p (c i j) -> p c j i", i=4, j=PACK), w2_raw[:].rearrange("p j (c i) -> p c j i", i=4))
+        for t in (3, 1, 2):
+            nc.scalar.activation(gy2[t], win1[t][:, hi][:, last], ACT.Copy, scale=gain(2.0, t))
+        for t in (3, 1, 0, 2):
+            centre(t)
+        sum_pair_b(2, range(4), range(3))
+        sum_pair_b(3, (0, 1), range(3))
+        sum_pair_b(3, (2, 3), (0, 1))
+        sum_pair_b(3, (2, 3), (2,))
+        weave_w2(1, nc.scalar.copy)
         for j in range(3):
             nc.scalar.copy(pair_b[j][:].rearrange("q (p e) -> q p e", e=2), zt_b[j][:].rearrange("q e p -> q p e"))
             nc.tensor.transpose(back[j][:, 1, :], pair_b[j][:].bitcast(F32), ident[:])
@@ -218,19 +271,19 @@ def tile_picked_cahn8_none_p_kernel(tc, x_words, x_scales, w1, gn, w2, offs, wes
             words = z_bf[j // 2][:].bitcast(F32)[:, 2 * P * (j % 2) : 2 * P * (j % 2 + 1)]
             nc.scalar.copy(words.rearrange("p (q u) -> p q u", u=2), back[j][:].rearrange("p u q -> p q u"))
 
-        held = [part[3][:, 0:P], part[3][:, HALF : HALF + P], z_bf[0][:].bitcast(F32)[:, 0:P], z_bf[1][:].bitcast(F32)[:, 0:P]]
-        for t in (0, 1):
+        held = [cube[3][:, 0:P], cube[3][:, HALF : HALF + P], z_bf[0][:].bitcast(F32)[:, 0:P], z_bf[1][:].bitcast(F32)[:, 0:P]]
+        for t in (1, 0):
             fetch_west(t, held[t])
-        nc.vector.quantize_mx(w2_codes[:].bitcast(FP8X4), w2_scales[:], w2_bf[:])
-        for t in (0, 1):
+        quant_w2(1)
+        for t in (1, 0):
             fetch_east(t, held[t])
         quant(0)
         quant(1)
+        for t in (2, 3):
+            fetch_west(t, held[t])
         product(0, 0, 2, 0, nc.scalar.copy)
         product(0, 2, 2, 4, nc.scalar.copy)
         product(1, 0, 4, 5, nc.scalar.copy)
-        for t in (2, 3):
-            fetch_west(t, held[t])
         for t in (2, 3):
             fetch_east(t, held[t])
         nc.vector.tensor_scalar(z_bf[2][:].rearrange("p (c i t) -> p c t i", i=4, t=PACK), z4[:].rearrange("p t (c i) -> p c t i", i=4), -0.5, None, MULT)

@@ -40,7 +40,7 @@ def tile_picked_cahn8_none_p_kernel(tc, x_words, x_scales, w1, gn, w2, offs, wes
         east_t = sb("east_t", [P, S // 16], U16)
         xw = sb("xw", [P, T], I32)
         xs = sb("xs", [P, T], U8)
-        w1_raw = [sb(f"w1_raw{h}", [P, PACK, H // 2], F32) for h in range(2)]
+        w1_raw = sb("w1_raw", [P, PACK, H], F32)
         w2_raw = [sb(f"w2_raw{h}", [P, PACK, N // 2], F32) for h in range(2)]
         g = sb("g", [P, PACK], F32)
         ident = sb("ident", [P, P], F32)
@@ -56,8 +56,7 @@ def tile_picked_cahn8_none_p_kernel(tc, x_words, x_scales, w1, gn, w2, offs, wes
         nc.sync.dma_start(offs_t[:], offs)
         for q in range(4):
             nc.sync.dma_start(xs[32 * q : 32 * q + 4, :].bitcast(I32), x_scales[0, 4 * q : 4 * q + 4, :].bitcast(I32))
-        for h in range(2):
-            nc.sync.dma_start(w1_raw[h][:], w1_rows[:, :, halves[h]])
+        nc.sync.dma_start(w1_raw[:], w1_rows)
         nc.sync.dma_start(g[:], gn.rearrange("(p t) o -> p (t o)", t=PACK))
         nc.sync.dma_start(west_t[:], west)
         nc.sync.dma_start(east_t[:], east)
@@ -74,24 +73,24 @@ def tile_picked_cahn8_none_p_kernel(tc, x_words, x_scales, w1, gn, w2, offs, wes
 
         xg_s = sb("xg_s", [P, S], U8)
         xg = sb("xg", [P, S], U32)
-        w1_bf = sb("w1_bf", [P, H * PACK], BF16)
         w1_codes = sb("w1_codes", [P, H], U32)
         w1_scales = sb("w1_scales", [P, H], U8)
-        w1_woven = w1_bf[:].rearrange("p (t m j) -> p m j t", t=PACK, j=PACK)
-
-        def weave_w1(h, ts):
-            nc.vector.tensor_copy(w1_woven[:, h * P // 2 : (h + 1) * P // 2, :, ts], w1_raw[h][:].rearrange("p j (m t) -> p m j t", t=PACK)[:, :, :, ts])
-
-        def quant_w1(t0, t1):
-            nc.vector.quantize_mx(w1_codes[:, t0 * P : t1 * P].bitcast(FP8X4), w1_scales[:, t0 * P : t1 * P], w1_bf[:, t0 * P * PACK : t1 * P * PACK])
-
         nc.vector.tensor_copy(xg[:], xw[:].bitcast(U32).indirect(offs_t[:]))
         nc.vector.tensor_copy(xg_s[:], xs[:].indirect(offs_t[:]))
-        weave_w1(0, slice(0, PACK))
-        weave_w1(1, slice(0, 2))
-        weave_w1(1, slice(2, PACK))
-        quant_w1(0, 2)
-        quant_w1(2, PACK)
+        w1_view = w1_raw[:].rearrange("p j (m t) -> p m j t", t=PACK)
+        w1_bf = [sb(f"w1_bf{u}", [P, 2 * P * PACK], BF16) for u in range(2)]
+
+        def weave_w1(u, ms):
+            nc.vector.tensor_copy(w1_bf[u][:].rearrange("p (t m j) -> p m j t", t=2, j=PACK)[:, ms], w1_view[:, ms, :, 2 * u : 2 * u + 2])
+
+        def quant_w1(u):
+            nc.vector.quantize_mx(w1_codes[:, halves[u]].bitcast(FP8X4), w1_scales[:, halves[u]], w1_bf[u][:])
+
+        weave_w1(0, slice(0, P))
+        weave_w1(1, slice(0, P // 2))
+        quant_w1(0)
+        weave_w1(1, slice(P // 2, P))
+        quant_w1(1)
         pre0 = [bank(4 * h, [P, HALF], f"pre0{h}") for h in range(2)]
         pre = [None] + [bank(t, [P, S], f"pre{t}") for t in range(1, PACK)]
 

@@ -52,16 +52,19 @@ def tile_picked_cahn8_none_p_kernel(tc, x_words, x_scales, w1, gn, w2, offs, wes
         w1_rows = w1.rearrange("(p j) c -> p j c", j=PACK)
         w2_rows = w2.rearrange("(p j) c -> p j c", j=PACK)
         nc.gpsimd.memset(xs[:].bitcast(I32), 0)
+        warm = sb("warm", [P, 2], F32)
+        nc.gpsimd.memset(warm[:, 0:1], 0.0)
+        nc.scalar.activation(warm[:, 1:2], warm[:, 0:1], ACT.Sigmoid)
         nc.sync.dma_start(xw[:], x_words[0].rearrange("p n t -> p (n t)").bitcast(I32))
         nc.sync.dma_start(offs_t[:], offs)
         for q in range(4):
             nc.sync.dma_start(xs[32 * q : 32 * q + 4, :].bitcast(I32), x_scales[0, 4 * q : 4 * q + 4, :].bitcast(I32))
         nc.sync.dma_start(w1_raw[:], w1_rows)
+        nc.sync.dma_start(w2_raw[0][:], w2_rows[:, :, halves[0]])
         nc.sync.dma_start(g[:], gn.rearrange("(p t) o -> p (t o)", t=PACK))
         nc.sync.dma_start(west_t[:], west)
         nc.sync.dma_start(east_t[:], east)
-        for h in range(2):
-            nc.sync.dma_start(w2_raw[h][:], w2_rows[:, :, halves[h]])
+        nc.sync.dma_start(w2_raw[1][:], w2_rows[:, :, halves[1]])
         make_identity(nc, ident[:])
         gx = {1.0: g}
         for factor in (0.5, 2.0):
@@ -80,16 +83,17 @@ def tile_picked_cahn8_none_p_kernel(tc, x_words, x_scales, w1, gn, w2, offs, wes
         w1_view = w1_raw[:].rearrange("p j (m t) -> p m j t", t=PACK)
         w1_bf = [sb(f"w1_bf{u}", [P, 2 * P * PACK], BF16) for u in range(2)]
 
-        def weave_w1(u, ms):
-            nc.vector.tensor_copy(w1_bf[u][:].rearrange("p (t m j) -> p m j t", t=2, j=PACK)[:, ms], w1_view[:, ms, :, 2 * u : 2 * u + 2])
+        def weave_w1(u, copy, ms=slice(0, P)):
+            copy(w1_bf[u][:].rearrange("p (t m j) -> p m j t", t=2, j=PACK)[:, ms], w1_view[:, ms, :, 2 * u : 2 * u + 2])
 
         def quant_w1(u):
             nc.vector.quantize_mx(w1_codes[:, halves[u]].bitcast(FP8X4), w1_scales[:, halves[u]], w1_bf[u][:])
 
-        weave_w1(0, slice(0, P))
-        weave_w1(1, slice(0, P // 2))
+        weave_w1(0, nc.vector.tensor_copy, slice(0, 80))
+        weave_w1(0, nc.scalar.copy, slice(80, P))
+        weave_w1(1, nc.scalar.copy, slice(0, P // 2))
+        weave_w1(1, nc.vector.tensor_copy, slice(P // 2, P))
         quant_w1(0)
-        weave_w1(1, slice(P // 2, P))
         quant_w1(1)
         pre0 = [bank(4 * h, [P, HALF], f"pre0{h}") for h in range(2)]
         pre = [None] + [bank(t, [P, S], f"pre{t}") for t in range(1, PACK)]
@@ -126,7 +130,7 @@ def tile_picked_cahn8_none_p_kernel(tc, x_words, x_scales, w1, gn, w2, offs, wes
         wide = [[y2[t + 1][:, c] for c in halves] for t in range(3)] + [[o[:, 0:HALF] for o in own3]]
         narrow = [[part[t + 1][:, c][:, 0:P] for c in halves] for t in range(2)] + [[cube[2][:, 0:P], part[3][:, 0:P]], [o[:, HALF:TURNED] for o in own3]]
         gy2 = [part[0][:, 0:P]] + [sb(f"gy2_{t}", [P, P], F32)[:] for t in range(1, PACK)]
-        ctr = [gy2[3]] + [sb(f"ctr{t}", [P, P], F32)[:] for t in range(1, PACK)]
+        ctr = [sb(f"ctr{t}", [P, P], F32)[:] for t in range(PACK)]
         z4 = sb("z4", [P, PACK, P], F32)
 
         def look(lst, a, b):
@@ -147,7 +151,6 @@ def tile_picked_cahn8_none_p_kernel(tc, x_words, x_scales, w1, gn, w2, offs, wes
                 nc.vector.tensor_tensor(part[0][:, c], win1[0][:].indirect(look(west_t, c.start, c.stop)), cube[0][:, c], SUB)
             for c in halves:
                 nc.vector.tensor_tensor(r[0][:, c], win1[0][:].indirect(look(east_t, c.start, c.stop)), part[0][:, c], ADD)
-            nc.vector.tensor_scalar(gy2[0], win1[0][:, last], 8.0, None, MULT)
 
         def scalar_plane(t):
             y = win1[t][:, hi]
@@ -250,19 +253,20 @@ def tile_picked_cahn8_none_p_kernel(tc, x_words, x_scales, w1, gn, w2, offs, wes
         pair_a = sb("pair_a", [P, 3, 2 * P], BF16)
         pair_b = [sb(f"pair_b{j}", [P, 2 * P], BF16) for j in range(3)]
         back = [bank(1 + j, [P, 2, P], f"back{j}") for j in range(3)]
-        nc.scalar.copy(pair_a[:, 0:2, :].rearrange("q j (p e) -> q j p e", e=2), zt_a[0][:].rearrange("q j e p -> q j p e"))
-        nc.scalar.copy(pair_a[:, 2:3, :].rearrange("q j (p e) -> q j p e", e=2), zt_a[1][:].rearrange("q j e p -> q j p e"))
-        for j in range(3):
-            nc.tensor.transpose(back[j][:, 0, :], pair_a[:, j, :].bitcast(F32), ident[:])
+        weave_w2(1, nc.scalar.copy)
         for t in (3, 1, 2):
             nc.scalar.activation(gy2[t], win1[t][:, hi][:, last], ACT.Copy, scale=gain(2.0, t))
-        for t in (3, 1, 0, 2):
+        nc.scalar.activation(gy2[0], win1[0][:, last], ACT.Copy, scale=8.0)
+        for t in (3, 1, 2, 0):
             centre(t)
         sum_pair_b(2, range(4), range(3))
         sum_pair_b(3, (0, 1), range(3))
         sum_pair_b(3, (2, 3), (0, 1))
         sum_pair_b(3, (2, 3), (2,))
-        weave_w2(1, nc.scalar.copy)
+        nc.scalar.copy(pair_a[:, 0:2, :].rearrange("q j (p e) -> q j p e", e=2), zt_a[0][:].rearrange("q j e p -> q j p e"))
+        nc.scalar.copy(pair_a[:, 2:3, :].rearrange("q j (p e) -> q j p e", e=2), zt_a[1][:].rearrange("q j e p -> q j p e"))
+        for j in range(3):
+            nc.tensor.transpose(back[j][:, 0, :], pair_a[:, j, :].bitcast(F32), ident[:])
         for j in range(3):
             nc.scalar.copy(pair_b[j][:].rearrange("q (p e) -> q p e", e=2), zt_b[j][:].rearrange("q e p -> q p e"))
             nc.tensor.transpose(back[j][:, 1, :], pair_b[j][:].bitcast(F32), ident[:])

@@ -55,13 +55,13 @@ def tile_picked_cahn8_none_p_kernel(tc, x_words, x_scales, w1, gn, w2, offs, wes
         warm = sb("warm", [P, 2], F32)
         nc.gpsimd.memset(warm[:, 0:1], 0.0)
         nc.scalar.activation(warm[:, 1:2], warm[:, 0:1], ACT.Sigmoid)
+        nc.scalar.dma_start(g[:], gn.rearrange("(p t) o -> p (t o)", t=PACK))
         nc.sync.dma_start(xw[:], x_words[0].rearrange("p n t -> p (n t)").bitcast(I32))
         nc.sync.dma_start(offs_t[:], offs)
         for q in range(4):
             nc.sync.dma_start(xs[32 * q : 32 * q + 4, :].bitcast(I32), x_scales[0, 4 * q : 4 * q + 4, :].bitcast(I32))
         nc.sync.dma_start(w1_raw[:], w1_rows)
         nc.sync.dma_start(w2_raw[0][:], w2_rows[:, :, halves[0]])
-        nc.sync.dma_start(g[:], gn.rearrange("(p t) o -> p (t o)", t=PACK))
         nc.sync.dma_start(west_t[:], west)
         nc.sync.dma_start(east_t[:], east)
         nc.sync.dma_start(w2_raw[1][:], w2_rows[:, :, halves[1]])

@@ -21,6 +21,7 @@ SUB = mybir.AluOpType.subtract
 P = 128
 PACK = 4
 HALF = S // 2
+BLOCKS = S // P
 
 
 def tile_picked_cahn8_none_p_kernel(tc, x_words, x_scales, w1, gn, w2, offs, west, east, out):
@@ -29,11 +30,14 @@ def tile_picked_cahn8_none_p_kernel(tc, x_words, x_scales, w1, gn, w2, offs, wes
         keep = ctx.enter_context(tc.tile_pool(name="keep", bufs=1))
         psum = ctx.enter_context(tc.psum_pool(name="psum", bufs=1))
 
-        def sb(name, shape, dtype):
-            return keep.tile(shape, dtype, name=name, align_bytes=64)
+        def sb(name, shape, dtype, over=None):
+            return keep.tile(shape, dtype, name=name, tag=over or name, align_bytes=64)
 
         def bank(b, shape, name):
             return psum.tile(shape, F32, name=name, tag=f"bank{b}")
+
+        def planes(name):
+            return [sb(f"{name}_{t}", [P, S], F32) for t in range(PACK)]
 
         offs_t = sb("offs_t", [P, S // 16], U16)
         west_t = sb("west_t", [P, S // 16], U16)
@@ -44,17 +48,12 @@ def tile_picked_cahn8_none_p_kernel(tc, x_words, x_scales, w1, gn, w2, offs, wes
         w2_raw = [sb(f"w2_raw{h}", [P, PACK, N // 2], F32) for h in range(2)]
         g = sb("g", [P, PACK], F32)
         ident = sb("ident", [P, P], F32)
-        lo, hi = slice(0, S), slice(S, 2 * S)
         halves = [slice(0, HALF), slice(HALF, S)]
-        TURNED = 3 * P
-        last = slice(TURNED, S)
+        blocks = [slice(j * P, (j + 1) * P) for j in range(BLOCKS)]
 
         w1_rows = w1.rearrange("(p j) c -> p j c", j=PACK)
         w2_rows = w2.rearrange("(p j) c -> p j c", j=PACK)
         nc.gpsimd.memset(xs[:].bitcast(I32), 0)
-        warm = sb("warm", [P, 2], F32)
-        nc.gpsimd.memset(warm[:, 0:1], 0.0)
-        nc.scalar.activation(warm[:, 1:2], warm[:, 0:1], ACT.Sigmoid)
         nc.scalar.dma_start(g[:], gn.rearrange("(p t) o -> p (t o)", t=PACK))
         nc.sync.dma_start(xw[:], x_words[0].rearrange("p n t -> p (n t)").bitcast(I32))
         nc.sync.dma_start(offs_t[:], offs)
@@ -66,13 +65,12 @@ def tile_picked_cahn8_none_p_kernel(tc, x_words, x_scales, w1, gn, w2, offs, wes
         nc.sync.dma_start(east_t[:], east)
         nc.sync.dma_start(w2_raw[1][:], w2_rows[:, :, halves[1]])
         make_identity(nc, ident[:])
-        gx = {1.0: g}
-        for factor in (0.5, 2.0):
-            gx[factor] = sb(f"gx{len(gx)}", [P, PACK], F32)
-            nc.gpsimd.tensor_scalar(gx[factor][:], g[:], factor, 0.0, MULT, ADD)
 
-        def gain(factor, t):
-            return gx[factor][:, t : t + 1]
+        spread = bank(5, [P, PACK, P], "spread")
+        for t in range(PACK):
+            nc.tensor.transpose(spread[:, t, :], g[:, t : t + 1].to_broadcast([P, P]), ident[:])
+        gain_row = sb("gain_row", [P, 2, P, 2], F32)
+        nc.scalar.activation(gain_row[:], spread[:].rearrange("q (u e) p -> q u p e", e=2), ACT.Copy, scale=0.25)
 
         xg_s = sb("xg_s", [P, S], U8)
         xg = sb("xg", [P, S], U32)
@@ -83,24 +81,20 @@ def tile_picked_cahn8_none_p_kernel(tc, x_words, x_scales, w1, gn, w2, offs, wes
         w1_view = w1_raw[:].rearrange("p j (m t) -> p m j t", t=PACK)
         w1_bf = [sb(f"w1_bf{u}", [P, 2 * P * PACK], BF16) for u in range(2)]
 
-        def weave_w1(u, copy, ms=slice(0, P)):
+        def weave_w1(u, copy, ms):
             copy(w1_bf[u][:].rearrange("p (t m j) -> p m j t", t=2, j=PACK)[:, ms], w1_view[:, ms, :, 2 * u : 2 * u + 2])
-
-        def quant_w1(u):
-            nc.vector.quantize_mx(w1_codes[:, halves[u]].bitcast(FP8X4), w1_scales[:, halves[u]], w1_bf[u][:])
 
         weave_w1(0, nc.vector.tensor_copy, slice(0, 80))
         weave_w1(0, nc.scalar.copy, slice(80, P))
         weave_w1(1, nc.scalar.copy, slice(0, P // 2))
         weave_w1(1, nc.vector.tensor_copy, slice(P // 2, P))
-        quant_w1(0)
-        quant_w1(1)
+        for u in range(2):
+            nc.vector.quantize_mx(w1_codes[:, halves[u]].bitcast(FP8X4), w1_scales[:, halves[u]], w1_bf[u][:])
         pre0 = [bank(4 * h, [P, HALF], f"pre0{h}") for h in range(2)]
         pre = [None] + [bank(t, [P, S], f"pre{t}") for t in range(1, PACK)]
 
         def first_product(acc, t, c):
-            cols = slice(t * P, (t + 1) * P)
-            nc.tensor.matmul_mx(acc, lhsT=w1_codes[:, cols].bitcast(FP8X4), lhsT_scale=w1_scales[:, cols],
+            nc.tensor.matmul_mx(acc, lhsT=w1_codes[:, blocks[t]].bitcast(FP8X4), lhsT_scale=w1_scales[:, blocks[t]],
                                 rhs=xg[:, c].bitcast(FP8X4), rhs_scale=xg_s[:, c], start=True, stop=True)
 
         for h, c in enumerate(halves):
@@ -108,188 +102,125 @@ def tile_picked_cahn8_none_p_kernel(tc, x_words, x_scales, w1, gn, w2, offs, wes
         for t in range(1, PACK):
             first_product(pre[t][:], t, slice(0, S))
 
-        w2_bf = [sb(f"w2_bf{h}", [P, HALF * PACK], BF16) for h in range(2)]
         w2_codes = sb("w2_codes", [P, N], U32)
         w2_scales = sb("w2_scales", [P, N], U8)
 
-        def weave_w2(h, copy):
-            copy(w2_bf[h][:].rearrange("p (c i j) -> p c j i", i=4, j=PACK), w2_raw[h][:].rearrange("p j (c i) -> p c j i", i=4))
+        def weave_w2(c, copy, over):
+            woven = sb(f"w2_bf{c.start}", [P, (c.stop - c.start) * PACK], BF16, over)
+            h, c0 = divmod(c.start, HALF)
+            raw = w2_raw[h][:, :, c0 : c0 + c.stop - c.start]
+            copy(woven[:].rearrange("p (c i j) -> p c j i", i=4, j=PACK), raw.rearrange("p j (c i) -> p c j i", i=4))
+            return woven
 
-        def quant_w2(h):
-            nc.vector.quantize_mx(w2_codes[:, halves[h]].bitcast(FP8X4), w2_scales[:, halves[h]], w2_bf[h][:])
+        def quant_w2(c, woven):
+            nc.vector.quantize_mx(w2_codes[:, c].bitcast(FP8X4), w2_scales[:, c], woven[:])
 
-        weave_w2(0, nc.vector.tensor_copy)
+        y, sq, cube, part, r, rw, re = [planes(name) for name in ("y", "sq", "cube", "part", "r", "rw", "re")]
+        y4 = {t: sb(f"y4_{t}", [P, S], F32) for t in (0, 3)}
+        turned = [bank(4 + j, [P, PACK, P], f"turned{j}") for j in range(BLOCKS)]
 
-        def planes(name, width):
-            return [sb(f"{name}_{t}", [P, width], F32) for t in range(PACK)]
+        def look(lst, c):
+            return lst[:, c.start // 16 : c.stop // 16]
 
-        win1 = [sb("win1_0", [P, S], F32)] + [sb(f"win1_{t}", [P, 2 * S], F32) for t in range(1, PACK)]
-        r, part, cube, y2, sw, se = [planes(name, S) for name in ("r", "part", "cube", "y2", "sw", "se")]
-        gy = planes("gy", TURNED)
-        own3 = [sb(f"own3_{i}", [P, TURNED], F32) for i in range(2)]
-        wide = [[y2[t + 1][:, c] for c in halves] for t in range(3)] + [[o[:, 0:HALF] for o in own3]]
-        narrow = [[part[t + 1][:, c][:, 0:P] for c in halves] for t in range(2)] + [[cube[2][:, 0:P], part[3][:, 0:P]], [o[:, HALF:TURNED] for o in own3]]
-        gy2 = [part[0][:, 0:P]] + [sb(f"gy2_{t}", [P, P], F32)[:] for t in range(1, PACK)]
-        ctr = [sb(f"ctr{t}", [P, P], F32)[:] for t in range(PACK)]
-        z4 = sb("z4", [P, PACK, P], F32)
-
-        def look(lst, a, b):
-            return lst[:, a // 16 : b // 16]
-
-        def first_plane():
-            s = sw[0]
-            for h, c in enumerate(halves):
-                nc.scalar.activation(s[:, c], pre0[h][:], ACT.Sigmoid, scale=2.0)
-            for c in halves:
-                nc.scalar.activation(y2[0][:, c], s[:, c], ACT.Square, scale=2.0, bias=-1.0)
-            for c in halves:
-                nc.vector.tensor_scalar(win1[0][:, c], s[:, c], -0.5, gain(0.5, 0), ADD, MULT)
-            quant_w2(0)
-            for c in halves:
-                nc.vector.scalar_tensor_tensor(cube[0][:, c], win1[0][:, c], 2.0, y2[0][:, c], MULT, MULT)
-            for c in halves:
-                nc.vector.tensor_tensor(part[0][:, c], win1[0][:].indirect(look(west_t, c.start, c.stop)), cube[0][:, c], SUB)
-            for c in halves:
-                nc.vector.tensor_tensor(r[0][:, c], win1[0][:].indirect(look(east_t, c.start, c.stop)), part[0][:, c], ADD)
-
-        def scalar_plane(t):
-            y = win1[t][:, hi]
-            nc.scalar.activation(y, pre[t][:], ACT.Tanh)
-            nc.scalar.copy(win1[t][:, lo], pre[t][:])
-            nc.scalar.activation(y2[t][:], y, ACT.Square)
-            nc.scalar.activation(sw[t][:], win1[t][:].indirect(west_t[:]), ACT.Sigmoid, scale=2.0)
-            nc.scalar.activation(se[t][:], win1[t][:].indirect(east_t[:]), ACT.Sigmoid, scale=2.0)
-
-        def gain_plane(t):
-            nc.scalar.activation(gy[t][:], win1[t][:, hi][:, 0:TURNED], ACT.Copy, scale=gain(1.0, t))
-
-        def cubes(t):
-            for c in halves:
-                nc.vector.scalar_tensor_tensor(cube[t][:, c], win1[t][:, hi][:, c], gain(0.5, t), y2[t][:, c], MULT, MULT)
+        def add_turned(term, t, first=False, last=False, js=range(BLOCKS)):
+            for j in js:
+                nc.tensor.matmul(turned[j][:, t, :], lhsT=term[:, blocks[j]], rhs=ident[:], start=first, stop=last, is_transpose=True)
 
         def potential(t):
             for c in halves:
-                nc.vector.scalar_tensor_tensor(part[t][:, c], sw[t][:, c], gain(0.5, t), cube[t][:, c], MULT, SUB)
+                nc.vector.scalar_tensor_tensor(cube[t][:, c], y[t][:, c], 2.0, sq[t][:, c], MULT, MULT)
             for c in halves:
-                nc.vector.scalar_tensor_tensor(r[t][:, c], se[t][:, c], gain(0.5, t), part[t][:, c], MULT, ADD)
+                nc.vector.tensor_tensor(part[t][:, c], y[t][:].indirect(look(west_t, c)), cube[t][:, c], SUB)
+            for c in halves:
+                nc.vector.tensor_tensor(r[t][:, c], y[t][:].indirect(look(east_t, c)), part[t][:, c], ADD)
 
-        def fetch_turned(t, a, b, sides=slice(0, 2)):
-            for dst, lst in list(zip(narrow[t] if a else wide[t], (west_t, east_t)))[sides]:
-                nc.vector.tensor_scalar(dst, r[t][:].indirect(look(lst, a, b)), -0.5, 0.0, MULT, ADD)
+        def fetch_scalar(dst, lst, t, c):
+            nc.scalar.activation(dst[t][:, c], r[t][:].indirect(look(lst, c)), ACT.Copy, scale=-0.5)
 
-        def terms(t, j):
-            c = slice(j * P, (j + 1) * P)
-            own = [win1[0][:, c]] * 4 if t == 0 else [gy[t][:, c]]
-            fetched = [w[:, c] for w in wide[t]] if j < 2 else narrow[t]
-            return [r[t][:, c]] + (fetched + own if t == 2 else own + fetched)
+        def fetch_vector(dst, lst, t, c):
+            nc.vector.tensor_scalar(dst[t][:, c], r[t][:].indirect(look(lst, c)), -0.5, 0.0, MULT, ADD)
 
-        def add_turned(dst, term, i, count):
-            nc.tensor.matmul(dst, lhsT=term, rhs=ident[:], start=i == 0, stop=i == count - 1, is_transpose=True)
+        def neighbours(t):
+            add_turned(r[t], t)
+            for dst, lst in ((rw, west_t), (re, east_t)):
+                for c in halves:
+                    fetch_scalar(dst, lst, t, c)
+                add_turned(dst[t], t)
 
-        zt_a = [bank(0, [P, 2, 2, P], "zt_a0"), bank(4, [P, 1, 2, P], "zt_a1")]
-        zt_b = [bank(5 + j, [P, 2, P], f"zt_b{j}") for j in range(3)]
+        w2_first = weave_w2(halves[0], nc.vector.tensor_copy, "w1_bf0")
+        for h, c in enumerate(halves):
+            nc.scalar.activation(y[0][:, c], pre0[h][:], ACT.Tanh)
+        for c in halves:
+            nc.scalar.activation(sq[0][:, c], y[0][:, c], ACT.Square)
+        for t in range(1, PACK):
+            nc.scalar.activation(y[t][:], pre[t][:], ACT.Tanh)
+            nc.scalar.activation(sq[t][:], y[t][:], ACT.Square)
+        nc.vector.tensor_scalar(y4[0][:], y[0][:], 4.0, None, MULT)
+        add_turned(y4[0], 0, first=True)
+        quant_w2(halves[0], w2_first)
+        for t in (1, 2):
+            for repeat in range(4):
+                add_turned(y[t], t)
+        for t in range(PACK):
+            potential(t)
+        neighbours(0)
+        nc.scalar.activation(y4[3][:], y[3][:], ACT.Copy, scale=4.0)
+        add_turned(y4[3], 3)
+        w2_late = []
+        for t in (1, 2):
+            neighbours(t)
+            w2_late.append(weave_w2(blocks[t + 1], nc.scalar.copy, f"sq_{t}"))
 
-        def sum_turned(t):
-            for j in range(3):
-                for i, term in enumerate(terms(t, j)):
-                    add_turned(zt_a[j // 2][:, j % 2, t, :], term, i, len(terms(t, j)))
-
-        def sum_pair_b(t, steps, js):
-            for i in steps:
-                for j in js:
-                    add_turned(zt_b[j][:, t - 2, :], terms(t, j)[i], i, 4)
-
-        def centre(t):
-            nc.vector.scalar_tensor_tensor(ctr[t], r[t][:, last], -2.0, gy2[t], MULT, SUB)
-
-        def fetch_west(t, dst):
-            nc.vector.tensor_tensor(dst, r[t][:].indirect(look(west_t, TURNED, S)), ctr[t], ADD)
-
-        def fetch_east(t, src):
-            nc.vector.tensor_tensor(z4[:, t, :], r[t][:].indirect(look(east_t, TURNED, S)), src, ADD)
-
-        z_bf = [sb("z_bf01", [P, 2 * P * PACK], BF16), sb("z_bf2", [P, P * PACK], BF16), sb("z_bf3", [P, P * PACK], BF16)]
-        chunks = [(0, HALF), (HALF, TURNED), (TURNED, S)]
-        z_codes = [sb(f"z_codes{c}", [P, b - a], U32) for c, (a, b) in enumerate(chunks)]
-        z_scales = [sb(f"z_scales{c}", [P, b - a], U8) for c, (a, b) in enumerate(chunks)]
+        pairs = [sb(f"pairs{j}", [P, 2, 2 * P], BF16) for j in range(BLOCKS)]
+        back = [bank(j, [P, 2, P], f"back{j}") for j in range(BLOCKS)]
+        z_bf = [sb(f"z_bf{j}", [P, P * PACK], BF16) for j in range(BLOCKS)]
+        z_codes = [sb(f"z_codes{j}", [P, P], U32) for j in range(BLOCKS)]
+        z_scales = [sb(f"z_scales{j}", [P, P], U8) for j in range(BLOCKS)]
         out_rows = out.rearrange("(a p) j -> p a j", p=P)
 
-        def quant(c):
-            nc.vector.quantize_mx(z_codes[c][:].bitcast(FP8X4), z_scales[c][:], z_bf[c][:])
+        def round_pairs(j):
+            nc.vector.tensor_tensor(pairs[j][:].rearrange("q u (p e) -> q u p e", e=2), turned[j][:].rearrange("q (u e) p -> q u p e", e=2), gain_row[:], MULT)
+            for u in range(2):
+                nc.tensor.transpose(back[j][:, u, :], pairs[j][:, u, :].bitcast(F32), ident[:])
 
-        def product(c, first, count, b, copy, queue=nc.sync):
-            j0, j1 = chunks[c]
-            acc = bank(b, [P, count, j1 - j0], f"acc{c}{first}")
-            res = sb(f"res{c}{first}", [P, count, j1 - j0], F32)
+        def weave_z(j):
+            nc.scalar.copy(z_bf[j][:].bitcast(F32).rearrange("p (q u) -> p q u", u=2), back[j][:].rearrange("p u q -> p q u"))
+
+        def quant_z(j):
+            nc.vector.quantize_mx(z_codes[j][:].bitcast(FP8X4), z_scales[j][:], z_bf[j][:])
+
+        def product(j, first, count, b, copy, queue=nc.sync):
+            acc = bank(b, [P, count, P], f"acc{j}{first}")
+            res = sb(f"res{j}{first}", [P, count, P], F32)
             for a in range(count):
-                cols = slice((first + a) * P, (first + a + 1) * P)
-                nc.tensor.matmul_mx(acc[:, a, :], lhsT=w2_codes[:, cols].bitcast(FP8X4), lhsT_scale=w2_scales[:, cols],
-                                    rhs=z_codes[c][:].bitcast(FP8X4), rhs_scale=z_scales[c][:], start=True, stop=True)
+                nc.tensor.matmul_mx(acc[:, a, :], lhsT=w2_codes[:, blocks[first + a]].bitcast(FP8X4), lhsT_scale=w2_scales[:, blocks[first + a]],
+                                    rhs=z_codes[j][:].bitcast(FP8X4), rhs_scale=z_scales[j][:], start=True, stop=True)
             copy(res[:], acc[:])
-            queue.dma_start(out_rows[:, first : first + count, j0:j1], res[:])
+            queue.dma_start(out_rows[:, first : first + count, blocks[j]], res[:])
 
-        first_plane()
-        for t in range(1, PACK):
-            scalar_plane(t)
-            if t == 1:
-                gain_plane(1)
-        gain_plane(2)
-        gain_plane(3)
-        west_side, east_side = slice(0, 1), slice(1, 2)
+        t = PACK - 1
+        add_turned(r[t], t)
+        for j in range(BLOCKS):
+            fetch_scalar(rw, west_t, t, blocks[j])
+            (fetch_vector if j < 2 else fetch_scalar)(re, east_t, t, blocks[j])
+            add_turned(rw[t], t, js=[j])
+            add_turned(re[t], t, last=True, js=[j])
         for t in (1, 2):
-            cubes(t)
-            fetch_turned(t - 1, 0, HALF)
-            potential(t)
-            fetch_turned(t - 1, HALF, TURNED)
-            sum_turned(t - 1)
-        cubes(3)
-        fetch_turned(2, 0, HALF)
-        fetch_turned(2, HALF, TURNED, west_side)
-        potential(3)
-        fetch_turned(2, HALF, TURNED, east_side)
-        fetch_turned(3, 0, HALF)
-        fetch_turned(3, HALF, TURNED)
-
-        pair_a = sb("pair_a", [P, 3, 2 * P], BF16)
-        pair_b = [sb(f"pair_b{j}", [P, 2 * P], BF16) for j in range(3)]
-        back = [bank(1 + j, [P, 2, P], f"back{j}") for j in range(3)]
-        weave_w2(1, nc.scalar.copy)
-        for t in (3, 1, 2):
-            nc.scalar.activation(gy2[t], win1[t][:, hi][:, last], ACT.Copy, scale=gain(2.0, t))
-        nc.scalar.activation(gy2[0], win1[0][:, last], ACT.Copy, scale=8.0)
-        for t in (3, 1, 2, 0):
-            centre(t)
-        sum_pair_b(2, range(4), range(3))
-        sum_pair_b(3, (0, 1), range(3))
-        sum_pair_b(3, (2, 3), (0, 1))
-        sum_pair_b(3, (2, 3), (2,))
-        nc.scalar.copy(pair_a[:, 0:2, :].rearrange("q j (p e) -> q j p e", e=2), zt_a[0][:].rearrange("q j e p -> q j p e"))
-        nc.scalar.copy(pair_a[:, 2:3, :].rearrange("q j (p e) -> q j p e", e=2), zt_a[1][:].rearrange("q j e p -> q j p e"))
-        for j in range(3):
-            nc.tensor.transpose(back[j][:, 0, :], pair_a[:, j, :].bitcast(F32), ident[:])
-        for j in range(3):
-            nc.scalar.copy(pair_b[j][:].rearrange("q (p e) -> q p e", e=2), zt_b[j][:].rearrange("q e p -> q p e"))
-            nc.tensor.transpose(back[j][:, 1, :], pair_b[j][:].bitcast(F32), ident[:])
-        for j in range(3):
-            words = z_bf[j // 2][:].bitcast(F32)[:, 2 * P * (j % 2) : 2 * P * (j % 2 + 1)]
-            nc.scalar.copy(words.rearrange("p (q u) -> p q u", u=2), back[j][:].rearrange("p u q -> p q u"))
-
-        held = [cube[3][:, 0:P], cube[3][:, HALF : HALF + P], z_bf[0][:].bitcast(F32)[:, 0:P], z_bf[1][:].bitcast(F32)[:, 0:P]]
-        for t in (1, 0):
-            fetch_west(t, held[t])
-        quant_w2(1)
-        for t in (1, 0):
-            fetch_east(t, held[t])
-        quant(0)
-        quant(1)
-        for t in (2, 3):
-            fetch_west(t, held[t])
-        product(0, 0, 2, 0, nc.scalar.copy)
-        product(0, 2, 2, 4, nc.scalar.copy)
-        product(1, 0, 4, 5, nc.scalar.copy)
-        for t in (2, 3):
-            fetch_east(t, held[t])
-        nc.vector.tensor_scalar(z_bf[2][:].rearrange("p (c i t) -> p c t i", i=4, t=PACK), z4[:].rearrange("p t (c i) -> p c t i", i=4), -0.5, None, MULT)
-        quant(2)
-        product(2, 0, 2, 6, nc.scalar.copy, nc.scalar)
-        product(2, 2, 2, 7, nc.vector.tensor_copy)
+            quant_w2(blocks[t + 1], w2_late[t - 1])
+        round_pairs(0)
+        round_pairs(1)
+        weave_z(0)
+        quant_z(0)
+        round_pairs(2)
+        weave_z(1)
+        quant_z(1)
+        product(0, 0, 4, 4, nc.scalar.copy)
+        round_pairs(3)
+        weave_z(2)
+        quant_z(2)
+        weave_z(3)
+        product(1, 0, 4, 5, nc.vector.tensor_copy)
+        quant_z(3)
+        product(2, 0, 4, 6, nc.scalar.copy)
+        product(3, 0, 2, 7, nc.scalar.copy, nc.scalar)
+        product(3, 2, 2, 0, nc.vector.tensor_copy)

@@ -102,7 +102,6 @@ def tile_picked_cahn8_none_p_kernel(tc, x_words, x_scales, w1, gn, w2, offs, wes
         for t in range(1, PACK):
             first_product(pre[t][:], t, slice(0, S))
 
-        w2_codes = sb("w2_codes", [P, N], U32)
         w2_scales = sb("w2_scales", [P, N], U8)
 
         def weave_w2(c, copy, over):
@@ -112,11 +111,8 @@ def tile_picked_cahn8_none_p_kernel(tc, x_words, x_scales, w1, gn, w2, offs, wes
             copy(woven[:].rearrange("p (c i j) -> p c j i", i=4, j=PACK), raw.rearrange("p j (c i) -> p c j i", i=4))
             return woven
 
-        def quant_w2(c, woven):
-            nc.vector.quantize_mx(w2_codes[:, c].bitcast(FP8X4), w2_scales[:, c], woven[:])
-
         y, sq, cube, part, r, rw, re = [planes(name) for name in ("y", "sq", "cube", "part", "r", "rw", "re")]
-        y4 = {t: sb(f"y4_{t}", [P, S], F32) for t in (0, 3)}
+        y4 = {t: sb(f"y4_{t}", [P, S], F32) for t in (0, 2, 3)}
         turned = [bank(4 + j, [P, PACK, P], f"turned{j}") for j in range(BLOCKS)]
 
         def look(lst, c):
@@ -157,19 +153,19 @@ def tile_picked_cahn8_none_p_kernel(tc, x_words, x_scales, w1, gn, w2, offs, wes
             nc.scalar.activation(sq[t][:], y[t][:], ACT.Square)
         nc.vector.tensor_scalar(y4[0][:], y[0][:], 4.0, None, MULT)
         add_turned(y4[0], 0, first=True)
-        quant_w2(halves[0], w2_first)
-        for t in (1, 2):
-            for repeat in range(4):
-                add_turned(y[t], t)
+        for repeat in range(4):
+            add_turned(y[1], 1)
         for t in range(PACK):
             potential(t)
+            if t == 1:
+                nc.vector.tensor_scalar(y4[2][:], y[2][:], 4.0, None, MULT)
         neighbours(0)
+        add_turned(y4[2], 2)
         nc.scalar.activation(y4[3][:], y[3][:], ACT.Copy, scale=4.0)
         add_turned(y4[3], 3)
-        w2_late = []
-        for t in (1, 2):
-            neighbours(t)
-            w2_late.append(weave_w2(blocks[t + 1], nc.scalar.copy, f"sq_{t}"))
+        neighbours(1)
+        w2_third = weave_w2(blocks[2], nc.scalar.copy, "sq_1")
+        neighbours(2)
 
         pairs = [sb(f"pairs{j}", [P, 2, 2 * P], BF16) for j in range(BLOCKS)]
         back = [bank(j, [P, 2, P], f"back{j}") for j in range(BLOCKS)]
@@ -177,6 +173,14 @@ def tile_picked_cahn8_none_p_kernel(tc, x_words, x_scales, w1, gn, w2, offs, wes
         z_codes = [sb(f"z_codes{j}", [P, P], U32) for j in range(BLOCKS)]
         z_scales = [sb(f"z_scales{j}", [P, P], U8) for j in range(BLOCKS)]
         out_rows = out.rearrange("(a p) j -> p a j", p=P)
+
+        w2_codes = {}
+
+        def quant_w2(c, woven, over):
+            codes = sb(f"w2_codes{c.start}", [P, c.stop - c.start], U32, over)
+            nc.vector.quantize_mx(codes[:].bitcast(FP8X4), w2_scales[:, c], woven[:])
+            for a in range(c.start // P, c.stop // P):
+                w2_codes[a] = codes[:, a * P - c.start : (a + 1) * P - c.start]
 
         def round_pairs(j):
             nc.vector.tensor_tensor(pairs[j][:].rearrange("q u (p e) -> q u p e", e=2), turned[j][:].rearrange("q (u e) p -> q u p e", e=2), gain_row[:], MULT)
@@ -193,7 +197,7 @@ def tile_picked_cahn8_none_p_kernel(tc, x_words, x_scales, w1, gn, w2, offs, wes
             acc = bank(b, [P, count, P], f"acc{j}{first}")
             res = sb(f"res{j}{first}", [P, count, P], F32)
             for a in range(count):
-                nc.tensor.matmul_mx(acc[:, a, :], lhsT=w2_codes[:, blocks[first + a]].bitcast(FP8X4), lhsT_scale=w2_scales[:, blocks[first + a]],
+                nc.tensor.matmul_mx(acc[:, a, :], lhsT=w2_codes[first + a].bitcast(FP8X4), lhsT_scale=w2_scales[:, blocks[first + a]],
                                     rhs=z_codes[j][:].bitcast(FP8X4), rhs_scale=z_scales[j][:], start=True, stop=True)
             copy(res[:], acc[:])
             queue.dma_start(out_rows[:, first : first + count, blocks[j]], res[:])
@@ -205,10 +209,12 @@ def tile_picked_cahn8_none_p_kernel(tc, x_words, x_scales, w1, gn, w2, offs, wes
             (fetch_vector if j < 2 else fetch_scalar)(re, east_t, t, blocks[j])
             add_turned(rw[t], t, js=[j])
             add_turned(re[t], t, last=True, js=[j])
-        for t in (1, 2):
-            quant_w2(blocks[t + 1], w2_late[t - 1])
+        quant_w2(halves[0], w2_first, "cube_3")
+        quant_w2(blocks[2], w2_third, "sq_3")
+        w2_last = weave_w2(blocks[3], nc.scalar.copy, "part_3")
         round_pairs(0)
         round_pairs(1)
+        quant_w2(blocks[3], w2_last, "pairs0")
         weave_z(0)
         quant_z(0)
         round_pairs(2)

@@ -1,3 +1,4 @@
+import math
 from contextlib import ExitStack
 
 import concourse.mybir as mybir
@@ -22,6 +23,7 @@ P = 128
 PACK = 4
 HALF = S // 2
 BLOCKS = S // P
+LAST = PACK - 1
 
 
 def tile_picked_cahn8_none_p_kernel(tc, x_words, x_scales, w1, gn, w2, offs, west, east, out):
@@ -67,8 +69,11 @@ def tile_picked_cahn8_none_p_kernel(tc, x_words, x_scales, w1, gn, w2, offs, wes
         make_identity(nc, ident[:])
 
         spread = bank(5, [P, PACK, P], "spread")
+        g_last = sb("g_last", [P, 1], F32)
+        nc.scalar.activation(g_last[:], g[:, LAST : LAST + 1], ACT.Copy, scale=-1.0)
         for t in range(PACK):
-            nc.tensor.transpose(spread[:, t, :], g[:, t : t + 1].to_broadcast([P, P]), ident[:])
+            column = g_last[:] if t == LAST else g[:, t : t + 1]
+            nc.tensor.transpose(spread[:, t, :], column.to_broadcast([P, P]), ident[:])
         gain_row = sb("gain_row", [P, 2, P, 2], F32)
         nc.scalar.activation(gain_row[:], spread[:].rearrange("q (u e) p -> q u p e", e=2), ACT.Copy, scale=0.25)
 
@@ -111,61 +116,84 @@ def tile_picked_cahn8_none_p_kernel(tc, x_words, x_scales, w1, gn, w2, offs, wes
             copy(woven[:].rearrange("p (c i j) -> p c j i", i=4, j=PACK), raw.rearrange("p j (c i) -> p c j i", i=4))
             return woven
 
-        y, sq, cube, part, r, rw, re = [planes(name) for name in ("y", "sq", "cube", "part", "r", "rw", "re")]
+        cube, rw, re = [planes(name) for name in ("cube", "rw", "re")]
+        y_win = [sb("y_win0", [P, S], F32)] + [sb(f"y_win{t}", [P, 2 * S], F32) for t in range(1, PACK)]
+        r_win = [sb(f"r_win{t}", [P, 2 * S], F32) for t in range(LAST)] + [sb("r_win3", [P, S], F32)]
+        y = [w[:, 0:S] for w in y_win]
+        r = [w[:, 0:S] for w in r_win]
+        sq = [sb("sq_0", [P, S], F32)[:]] + [w[:, S : 2 * S] for w in y_win[1:]]
+        part = [w[:, S : 2 * S] for w in r_win[:LAST]] + [sb("part_3", [P, S], F32)[:]]
+        whole = slice(0, S)
         y4 = {t: sb(f"y4_{t}", [P, S], F32) for t in (0, 2, 3)}
         turned = [bank(4 + j, [P, PACK, P], f"turned{j}") for j in range(BLOCKS)]
 
         def look(lst, c):
             return lst[:, c.start // 16 : c.stop // 16]
 
-        def add_turned(term, t, first=False, last=False, js=range(BLOCKS)):
-            for j in js:
-                nc.tensor.matmul(turned[j][:, t, :], lhsT=term[:, blocks[j]], rhs=ident[:], start=first, stop=last, is_transpose=True)
+        def add_block(term, t, j, first=False, last=False):
+            nc.tensor.matmul(turned[j][:, t, :], lhsT=term, rhs=ident[:], start=first, stop=last, is_transpose=True)
 
-        def potential(t):
-            for c in halves:
-                nc.vector.scalar_tensor_tensor(cube[t][:, c], y[t][:, c], 2.0, sq[t][:, c], MULT, MULT)
-            for c in halves:
-                nc.vector.tensor_tensor(part[t][:, c], y[t][:].indirect(look(west_t, c)), cube[t][:, c], SUB)
-            for c in halves:
-                nc.vector.tensor_tensor(r[t][:, c], y[t][:].indirect(look(east_t, c)), part[t][:, c], ADD)
+        def add_turned(term, t, first=False):
+            for j in range(BLOCKS):
+                add_block(term[:, blocks[j]], t, j, first)
+
+        def cubes(t, c):
+            nc.vector.scalar_tensor_tensor(cube[t][:, c], sq[t][:, c], 2.0 if t == LAST else 0.0, y[t][:, c], ADD, MULT)
+
+        def add_west(t, c):
+            nc.vector.tensor_tensor(part[t][:, c], y_win[t][:].indirect(look(west_t, c)), cube[t][:, c], SUB)
+
+        def add_east(t, c):
+            nc.vector.tensor_tensor(r[t][:, c], y_win[t][:].indirect(look(east_t, c)), part[t][:, c], ADD)
 
         def fetch_scalar(dst, lst, t, c):
-            nc.scalar.activation(dst[t][:, c], r[t][:].indirect(look(lst, c)), ACT.Copy, scale=-0.5)
+            nc.scalar.activation(dst, r_win[t][:].indirect(look(lst, c)), ACT.Copy, scale=0.5 if t == LAST else -0.5)
 
         def fetch_vector(dst, lst, t, c):
-            nc.vector.tensor_scalar(dst[t][:, c], r[t][:].indirect(look(lst, c)), -0.5, 0.0, MULT, ADD)
+            nc.vector.tensor_scalar(dst, r_win[t][:].indirect(look(lst, c)), 0.5, 0.0, MULT, ADD)
 
         def neighbours(t):
             add_turned(r[t], t)
             for dst, lst in ((rw, west_t), (re, east_t)):
-                for c in halves:
-                    fetch_scalar(dst, lst, t, c)
+                fetch_scalar(dst[t][:], lst, t, whole)
                 add_turned(dst[t], t)
 
         w2_first = weave_w2(halves[0], nc.vector.tensor_copy, "w1_bf0")
         for h, c in enumerate(halves):
             nc.scalar.activation(y[0][:, c], pre0[h][:], ACT.Tanh)
         for c in halves:
-            nc.scalar.activation(sq[0][:, c], y[0][:, c], ACT.Square)
+            nc.scalar.activation(sq[0][:, c], y[0][:, c], ACT.Square, scale=math.sqrt(2.0))
         for t in range(1, PACK):
-            nc.scalar.activation(y[t][:], pre[t][:], ACT.Tanh)
-            nc.scalar.activation(sq[t][:], y[t][:], ACT.Square)
-        nc.vector.tensor_scalar(y4[0][:], y[0][:], 4.0, None, MULT)
+            nc.scalar.activation(y[t], pre[t][:], ACT.Tanh)
+            nc.scalar.activation(sq[t], y[t], ACT.Square, scale=math.sqrt(2.0))
+        nc.vector.tensor_scalar(y4[0][:], y[0], 4.0, None, MULT)
         add_turned(y4[0], 0, first=True)
         for repeat in range(4):
             add_turned(y[1], 1)
-        for t in range(PACK):
-            potential(t)
-            if t == 1:
-                nc.vector.tensor_scalar(y4[2][:], y[2][:], 4.0, None, MULT)
+        for step in (cubes, add_west):
+            for c in halves:
+                step(0, c)
+        cubes(1, whole)
+        for c in halves:
+            add_east(0, c)
+        nc.vector.tensor_scalar(y4[2][:], y[2], 4.0, None, MULT)
+        for t in range(1, LAST):
+            add_west(t, whole)
+            cubes(t + 1, whole)
+            add_east(t, whole)
+        add_west(LAST, whole)
+        w2_last = weave_w2(halves[1], nc.vector.tensor_copy, "cube_2")
+        add_east(LAST, whole)
         neighbours(0)
         add_turned(y4[2], 2)
-        nc.scalar.activation(y4[3][:], y[3][:], ACT.Copy, scale=4.0)
+        nc.scalar.activation(y4[3][:], y[3], ACT.Copy, scale=-6.0)
         add_turned(y4[3], 3)
         neighbours(1)
-        w2_third = weave_w2(blocks[2], nc.scalar.copy, "sq_1")
-        neighbours(2)
+        add_turned(cube[LAST], LAST)
+        add_turned(r[2], 2)
+        fetch_scalar(rw[2][:], west_t, 2, whole)
+        add_turned(rw[2], 2)
+        fetch_scalar(re[2][:], east_t, 2, whole)
 
         pairs = [sb(f"pairs{j}", [P, 2, 2 * P], BF16) for j in range(BLOCKS)]
         back = [bank(j, [P, 2, P], f"back{j}") for j in range(BLOCKS)]
@@ -193,40 +221,44 @@ def tile_picked_cahn8_none_p_kernel(tc, x_words, x_scales, w1, gn, w2, offs, wes
         def quant_z(j):
             nc.vector.quantize_mx(z_codes[j][:].bitcast(FP8X4), z_scales[j][:], z_bf[j][:])
 
-        def product(j, first, count, b, copy, queue=nc.sync):
-            acc = bank(b, [P, count, P], f"acc{j}{first}")
-            res = sb(f"res{j}{first}", [P, count, P], F32)
-            for a in range(count):
-                nc.tensor.matmul_mx(acc[:, a, :], lhsT=w2_codes[first + a].bitcast(FP8X4), lhsT_scale=w2_scales[:, blocks[first + a]],
-                                    rhs=z_codes[j][:].bitcast(FP8X4), rhs_scale=z_scales[j][:], start=True, stop=True)
-            copy(res[:], acc[:])
-            queue.dma_start(out_rows[:, first : first + count, blocks[j]], res[:])
+        results = [sb(f"res{j}", [P, PACK, P], F32) for j in range(BLOCKS)]
 
-        t = PACK - 1
-        add_turned(r[t], t)
-        for j in range(BLOCKS):
-            fetch_scalar(rw, west_t, t, blocks[j])
-            (fetch_vector if j < 2 else fetch_scalar)(re, east_t, t, blocks[j])
-            add_turned(rw[t], t, js=[j])
-            add_turned(re[t], t, last=True, js=[j])
-        quant_w2(halves[0], w2_first, "cube_3")
-        quant_w2(blocks[2], w2_third, "sq_3")
-        w2_last = weave_w2(blocks[3], nc.scalar.copy, "part_3")
+        def product(j):
+            acc = [bank(b, [P, 2, P], f"acc{j}{h}") for h, b in enumerate((4 + j, j))]
+            for a in range(PACK):
+                nc.tensor.matmul_mx(acc[a // 2][:, a % 2, :], lhsT=w2_codes[a].bitcast(FP8X4), lhsT_scale=w2_scales[:, blocks[a]],
+                                    rhs=z_codes[j][:].bitcast(FP8X4), rhs_scale=z_scales[j][:], start=True, stop=True)
+            return acc
+
+        def store(j, acc, queues):
+            for h, copy in enumerate((nc.scalar.copy, nc.vector.tensor_copy)):
+                copy(results[j][:, 2 * h : 2 * h + 2, :], acc[h][:])
+            rows = PACK // len(queues)
+            for i, queue in enumerate(queues):
+                queue.dma_start(out_rows[:, i * rows : (i + 1) * rows, blocks[j]], results[j][:, i * rows : (i + 1) * rows, :])
+
+        def last_neighbours(j):
+            add_block(re[2][:, blocks[j]], 2, j)
+            fetch_scalar(rw[LAST][:, blocks[j]], west_t, LAST, blocks[j])
+            (fetch_vector if j < 2 else fetch_scalar)(re[LAST][:, blocks[j]], east_t, LAST, blocks[j])
+            add_block(rw[LAST][:, blocks[j]], LAST, j)
+            add_block(re[LAST][:, blocks[j]], LAST, j, last=True)
+
+        for j in range(LAST):
+            last_neighbours(j)
+        quant_w2(halves[0], w2_first, "y_win3")
         round_pairs(0)
+        last_neighbours(LAST)
         round_pairs(1)
-        quant_w2(blocks[3], w2_last, "pairs0")
+        round_pairs(2)
         weave_z(0)
         quant_z(0)
-        round_pairs(2)
-        weave_z(1)
-        quant_z(1)
-        product(0, 0, 4, 4, nc.scalar.copy)
-        round_pairs(3)
-        weave_z(2)
-        quant_z(2)
-        weave_z(3)
-        product(1, 0, 4, 5, nc.vector.tensor_copy)
-        quant_z(3)
-        product(2, 0, 4, 6, nc.scalar.copy)
-        product(3, 0, 2, 7, nc.scalar.copy, nc.scalar)
-        product(3, 2, 2, 0, nc.vector.tensor_copy)
+        quant_w2(halves[1], w2_last, "pairs0")
+        acc = product(0)
+        round_pairs(LAST)
+        for j in range(1, BLOCKS):
+            weave_z(j)
+            quant_z(j)
+            store(j - 1, acc, [nc.sync])
+            acc = product(j)
+        store(LAST, acc, [nc.scalar, nc.sync])

@@ -116,6 +116,14 @@ def tile_picked_cahn8_none_p_kernel(tc, x_words, x_scales, w1, gn, w2, offs, wes
             copy(woven[:].rearrange("p (c i j) -> p c j i", i=4, j=PACK), raw.rearrange("p j (c i) -> p c j i", i=4))
             return woven
 
+        w2_codes = {}
+
+        def quant_w2(c, woven, over=None):
+            codes = sb(f"w2_codes{c.start}", [P, c.stop - c.start], U32, over)
+            nc.vector.quantize_mx(codes[:].bitcast(FP8X4), w2_scales[:, c], woven[:])
+            for a in range(c.start // P, c.stop // P):
+                w2_codes[a] = codes[:, a * P - c.start : (a + 1) * P - c.start]
+
         cube, rw, re = [planes(name) for name in ("cube", "rw", "re")]
         y_win = [sb("y_win0", [P, S], F32)] + [sb(f"y_win{t}", [P, 2 * S], F32) for t in range(1, PACK)]
         r_win = [sb(f"r_win{t}", [P, 2 * S], F32) for t in range(LAST)] + [sb("r_win3", [P, S], F32)]
@@ -124,7 +132,7 @@ def tile_picked_cahn8_none_p_kernel(tc, x_words, x_scales, w1, gn, w2, offs, wes
         sq = [sb("sq_0", [P, S], F32)[:]] + [w[:, S : 2 * S] for w in y_win[1:]]
         part = [w[:, S : 2 * S] for w in r_win[:LAST]] + [sb("part_3", [P, S], F32)[:]]
         whole = slice(0, S)
-        y4 = {t: sb(f"y4_{t}", [P, S], F32) for t in (0, 2, 3)}
+        y4 = {t: sb(f"y4_{t}", [P, S], F32) for t in (0, 3)}
         turned = [bank(4 + j, [P, PACK, P], f"turned{j}") for j in range(BLOCKS)]
 
         def look(lst, c):
@@ -158,7 +166,7 @@ def tile_picked_cahn8_none_p_kernel(tc, x_words, x_scales, w1, gn, w2, offs, wes
                 fetch_scalar(dst[t][:], lst, t, whole)
                 add_turned(dst[t], t)
 
-        w2_first = weave_w2(halves[0], nc.vector.tensor_copy, "w1_bf0")
+        quant_w2(halves[0], weave_w2(halves[0], nc.vector.tensor_copy, "w1_bf0"))
         for h, c in enumerate(halves):
             nc.scalar.activation(y[0][:, c], pre0[h][:], ACT.Tanh)
         for c in halves:
@@ -176,22 +184,22 @@ def tile_picked_cahn8_none_p_kernel(tc, x_words, x_scales, w1, gn, w2, offs, wes
         cubes(1, whole)
         for c in halves:
             add_east(0, c)
-        nc.vector.tensor_scalar(y4[2][:], y[2], 4.0, None, MULT)
         for t in range(1, LAST):
             add_west(t, whole)
             cubes(t + 1, whole)
             add_east(t, whole)
         add_west(LAST, whole)
-        w2_last = weave_w2(halves[1], nc.vector.tensor_copy, "cube_2")
+        y4[2] = sb("y4_2", [P, S], F32, "cube_2")
+        nc.vector.tensor_scalar(y4[2][:], y[2], 4.0, None, MULT)
         add_east(LAST, whole)
         neighbours(0)
-        add_turned(y4[2], 2)
         nc.scalar.activation(y4[3][:], y[3], ACT.Copy, scale=-6.0)
         add_turned(y4[3], 3)
         neighbours(1)
         add_turned(cube[LAST], LAST)
         add_turned(r[2], 2)
         fetch_scalar(rw[2][:], west_t, 2, whole)
+        add_turned(y4[2], 2)
         add_turned(rw[2], 2)
         fetch_scalar(re[2][:], east_t, 2, whole)
 
@@ -201,14 +209,6 @@ def tile_picked_cahn8_none_p_kernel(tc, x_words, x_scales, w1, gn, w2, offs, wes
         z_codes = [sb(f"z_codes{j}", [P, P], U32) for j in range(BLOCKS)]
         z_scales = [sb(f"z_scales{j}", [P, P], U8) for j in range(BLOCKS)]
         out_rows = out.rearrange("(a p) j -> p a j", p=P)
-
-        w2_codes = {}
-
-        def quant_w2(c, woven, over):
-            codes = sb(f"w2_codes{c.start}", [P, c.stop - c.start], U32, over)
-            nc.vector.quantize_mx(codes[:].bitcast(FP8X4), w2_scales[:, c], woven[:])
-            for a in range(c.start // P, c.stop // P):
-                w2_codes[a] = codes[:, a * P - c.start : (a + 1) * P - c.start]
 
         def round_pairs(j):
             nc.vector.tensor_tensor(pairs[j][:].rearrange("q u (p e) -> q u p e", e=2), turned[j][:].rearrange("q (u e) p -> q u p e", e=2), gain_row[:], MULT)
@@ -239,21 +239,23 @@ def tile_picked_cahn8_none_p_kernel(tc, x_words, x_scales, w1, gn, w2, offs, wes
 
         def last_neighbours(j):
             add_block(re[2][:, blocks[j]], 2, j)
-            fetch_scalar(rw[LAST][:, blocks[j]], west_t, LAST, blocks[j])
-            (fetch_vector if j < 2 else fetch_scalar)(re[LAST][:, blocks[j]], east_t, LAST, blocks[j])
+            (fetch_vector if j == 0 else fetch_scalar)(rw[LAST][:, blocks[j]], west_t, LAST, blocks[j])
+            from_east = sb(f"re_last{j}", [P, P], F32)[:]
+            (fetch_vector if j < 2 else fetch_scalar)(from_east, east_t, LAST, blocks[j])
             add_block(rw[LAST][:, blocks[j]], LAST, j)
-            add_block(re[LAST][:, blocks[j]], LAST, j, last=True)
+            add_block(from_east, LAST, j, last=True)
 
         for j in range(LAST):
             last_neighbours(j)
-        quant_w2(halves[0], w2_first, "y_win3")
+        w2_last = sb("w2_last", [P, HALF * PACK], BF16, "re_last0")
+        nc.gpsimd.tensor_scalar(w2_last[:].rearrange("p (c j) -> p c j", j=PACK), w2_raw[1][:].rearrange("p j c -> p c j"), 1.0, 0.0, MULT, ADD)
         round_pairs(0)
         last_neighbours(LAST)
         round_pairs(1)
         round_pairs(2)
         weave_z(0)
         quant_z(0)
-        quant_w2(halves[1], w2_last, "pairs0")
+        quant_w2(halves[1], w2_last)
         acc = product(0)
         round_pairs(LAST)
         for j in range(1, BLOCKS):

@@ -132,7 +132,7 @@ def tile_picked_cahn8_none_p_kernel(tc, x_words, x_scales, w1, gn, w2, offs, wes
         sq = [sb("sq_0", [P, S], F32)[:]] + [w[:, S : 2 * S] for w in y_win[1:]]
         part = [w[:, S : 2 * S] for w in r_win[:LAST]] + [sb("part_3", [P, S], F32)[:]]
         whole = slice(0, S)
-        y4 = {t: sb(f"y4_{t}", [P, S], F32) for t in (0, 3)}
+        y4 = {0: sb("y4_0", [P, S], F32), 2: y_win[0], 3: sb("y4_3", [P, S], F32)}
         turned = [bank(4 + j, [P, PACK, P], f"turned{j}") for j in range(BLOCKS)]
 
         def look(lst, c):
@@ -146,7 +146,8 @@ def tile_picked_cahn8_none_p_kernel(tc, x_words, x_scales, w1, gn, w2, offs, wes
                 add_block(term[:, blocks[j]], t, j, first)
 
         def cubes(t, c):
-            nc.vector.scalar_tensor_tensor(cube[t][:, c], sq[t][:, c], 2.0 if t == LAST else 0.0, y[t][:, c], ADD, MULT)
+            factor = y4[2] if t == 2 else y[t]
+            nc.vector.scalar_tensor_tensor(cube[t][:, c], sq[t][:, c], 2.0 if t == LAST else 0.0, factor[:, c], ADD, MULT)
 
         def add_west(t, c):
             nc.vector.tensor_tensor(part[t][:, c], y_win[t][:].indirect(look(west_t, c)), cube[t][:, c], SUB)
@@ -173,7 +174,7 @@ def tile_picked_cahn8_none_p_kernel(tc, x_words, x_scales, w1, gn, w2, offs, wes
             nc.scalar.activation(sq[0][:, c], y[0][:, c], ACT.Square, scale=math.sqrt(2.0))
         for t in range(1, PACK):
             nc.scalar.activation(y[t], pre[t][:], ACT.Tanh)
-            nc.scalar.activation(sq[t], y[t], ACT.Square, scale=math.sqrt(2.0))
+            nc.scalar.activation(sq[t], y[t], ACT.Square, scale=math.sqrt(0.5 if t == 2 else 2.0))
         nc.vector.tensor_scalar(y4[0][:], y[0], 4.0, None, MULT)
         add_turned(y4[0], 0, first=True)
         for repeat in range(4):
@@ -181,27 +182,33 @@ def tile_picked_cahn8_none_p_kernel(tc, x_words, x_scales, w1, gn, w2, offs, wes
         for step in (cubes, add_west):
             for c in halves:
                 step(0, c)
-        cubes(1, whole)
         for c in halves:
             add_east(0, c)
-        for t in range(1, LAST):
-            add_west(t, whole)
-            cubes(t + 1, whole)
-            add_east(t, whole)
-        add_west(LAST, whole)
-        y4[2] = sb("y4_2", [P, S], F32, "cube_2")
+        cubes(1, whole)
         nc.vector.tensor_scalar(y4[2][:], y[2], 4.0, None, MULT)
-        add_east(LAST, whole)
+        add_west(1, whole)
+        cubes(2, whole)
+        add_east(1, whole)
+        add_west(2, whole)
+        cubes(LAST, whole)
+        add_east(2, whole)
         neighbours(0)
+        add_turned(y4[2], 2)
         nc.scalar.activation(y4[3][:], y[3], ACT.Copy, scale=-6.0)
         add_turned(y4[3], 3)
+        y_west = sb("y_west", [P, S], F32)
+        nc.scalar.activation(y_west[:], y_win[LAST][:].indirect(west_t[:]), ACT.Copy)
+        for c in halves:
+            nc.vector.tensor_tensor(part[LAST][:, c], y_west[:, c], cube[LAST][:, c], SUB)
+        for c in halves:
+            add_east(LAST, c)
         neighbours(1)
-        add_turned(cube[LAST], LAST)
         add_turned(r[2], 2)
         fetch_scalar(rw[2][:], west_t, 2, whole)
-        add_turned(y4[2], 2)
+        add_turned(cube[LAST], LAST)
         add_turned(rw[2], 2)
-        fetch_scalar(re[2][:], east_t, 2, whole)
+        for c in halves:
+            fetch_scalar(re[2][:, c], east_t, 2, c)
 
         pairs = [sb(f"pairs{j}", [P, 2, 2 * P], BF16) for j in range(BLOCKS)]
         back = [bank(j, [P, 2, P], f"back{j}") for j in range(BLOCKS)]
@@ -239,7 +246,7 @@ def tile_picked_cahn8_none_p_kernel(tc, x_words, x_scales, w1, gn, w2, offs, wes
 
         def last_neighbours(j):
             add_block(re[2][:, blocks[j]], 2, j)
-            (fetch_vector if j == 0 else fetch_scalar)(rw[LAST][:, blocks[j]], west_t, LAST, blocks[j])
+            (fetch_vector if j < 2 else fetch_scalar)(rw[LAST][:, blocks[j]], west_t, LAST, blocks[j])
             from_east = sb(f"re_last{j}", [P, P], F32)[:]
             (fetch_vector if j < 2 else fetch_scalar)(from_east, east_t, LAST, blocks[j])
             add_block(rw[LAST][:, blocks[j]], LAST, j)
@@ -261,6 +268,6 @@ def tile_picked_cahn8_none_p_kernel(tc, x_words, x_scales, w1, gn, w2, offs, wes
         for j in range(1, BLOCKS):
             weave_z(j)
             quant_z(j)
-            store(j - 1, acc, [nc.sync])
+            store(j - 1, acc, [nc.sync] * (2 if j == 1 else 1))
             acc = product(j)
         store(LAST, acc, [nc.scalar, nc.sync])

@@ -93,8 +93,9 @@ def tile_picked_cahn8_none_p_kernel(tc, x_words, x_scales, w1, gn, w2, offs, wes
         weave_w1(0, nc.scalar.copy, slice(80, P))
         weave_w1(1, nc.scalar.copy, slice(0, P // 2))
         weave_w1(1, nc.vector.tensor_copy, slice(P // 2, P))
-        for u in range(2):
-            nc.vector.quantize_mx(w1_codes[:, halves[u]].bitcast(FP8X4), w1_scales[:, halves[u]], w1_bf[u][:])
+        for t in range(2):
+            nc.vector.quantize_mx(w1_codes[:, blocks[t]].bitcast(FP8X4), w1_scales[:, blocks[t]], w1_bf[0][:, t * S : (t + 1) * S])
+        nc.vector.quantize_mx(w1_codes[:, halves[1]].bitcast(FP8X4), w1_scales[:, halves[1]], w1_bf[1][:])
         pre0 = [bank(4 * h, [P, HALF], f"pre0{h}") for h in range(2)]
         pre = [None] + [bank(t, [P, S], f"pre{t}") for t in range(1, PACK)]
 
@@ -217,9 +218,10 @@ def tile_picked_cahn8_none_p_kernel(tc, x_words, x_scales, w1, gn, w2, offs, wes
         z_scales = [sb(f"z_scales{j}", [P, P], U8) for j in range(BLOCKS)]
         out_rows = out.rearrange("(a p) j -> p a j", p=P)
 
-        def round_pairs(j):
-            nc.vector.tensor_tensor(pairs[j][:].rearrange("q u (p e) -> q u p e", e=2), turned[j][:].rearrange("q (u e) p -> q u p e", e=2), gain_row[:], MULT)
-            for u in range(2):
+        def round_pairs(j, us=slice(0, 2)):
+            sums = turned[j][:].rearrange("q (u e) p -> q u p e", e=2)
+            nc.vector.tensor_tensor(pairs[j][:].rearrange("q u (p e) -> q u p e", e=2)[:, us], sums[:, us], gain_row[:, us], MULT)
+            for u in range(us.start, us.stop):
                 nc.tensor.transpose(back[j][:, u, :], pairs[j][:, u, :].bitcast(F32), ident[:])
 
         def weave_z(j):
@@ -264,10 +266,18 @@ def tile_picked_cahn8_none_p_kernel(tc, x_words, x_scales, w1, gn, w2, offs, wes
         quant_z(0)
         quant_w2(halves[1], w2_last)
         acc = product(0)
-        round_pairs(LAST)
+        for u in range(2):
+            round_pairs(LAST, slice(u, u + 1))
         for j in range(1, BLOCKS):
             weave_z(j)
             quant_z(j)
             store(j - 1, acc, [nc.sync] * (2 if j == 1 else 1))
-            acc = product(j)
-        store(LAST, acc, [nc.scalar, nc.sync])
+            if j < LAST:
+                acc = product(j)
+        for a in range(PACK):
+            acc = bank((LAST, 4 + LAST, 0, 4)[a], [P, P], f"acc_last{a}")
+            nc.tensor.matmul_mx(acc[:], lhsT=w2_codes[a].bitcast(FP8X4), lhsT_scale=w2_scales[:, blocks[a]],
+                                rhs=z_codes[LAST][:].bitcast(FP8X4), rhs_scale=z_scales[LAST][:], start=True, stop=True)
+            (nc.vector.tensor_copy if a % 2 == 0 else nc.scalar.copy)(results[LAST][:, a, :], acc[:])
+        nc.sync.dma_start(out_rows[:, 0:2, blocks[LAST]], results[LAST][:, 0:2, :])
+        nc.scalar.dma_start(out_rows[:, 2:4, blocks[LAST]], results[LAST][:, 2:4, :])

@@ -271,7 +271,7 @@ def tile_picked_cahn8_none_p_kernel(tc, x_words, x_scales, w1, gn, w2, offs, wes
         for j in range(1, BLOCKS):
             weave_z(j)
             quant_z(j)
-            store(j - 1, acc, [nc.sync] * (2 if j == 1 else 1))
+            store(j - 1, acc, [nc.sync] * 2)
             if j < LAST:
                 acc = product(j)
         for a in range(PACK):

@@ -240,7 +240,7 @@ def tile_picked_cahn8_none_p_kernel(tc, x_words, x_scales, w1, gn, w2, offs, wes
             return acc
 
         def store(j, acc, queues):
-            for h, copy in enumerate((nc.scalar.copy, nc.vector.tensor_copy)):
+            for h, copy in enumerate((nc.scalar.copy, nc.scalar.copy if j == 0 else nc.vector.tensor_copy)):
                 copy(results[j][:, 2 * h : 2 * h + 2, :], acc[h][:])
             rows = PACK // len(queues)
             for i, queue in enumerate(queues):
@@ -258,7 +258,8 @@ def tile_picked_cahn8_none_p_kernel(tc, x_words, x_scales, w1, gn, w2, offs, wes
             last_neighbours(j)
         w2_last = sb("w2_last", [P, HALF * PACK], BF16, "re_last0")
         nc.gpsimd.tensor_scalar(w2_last[:].rearrange("p (c j) -> p c j", j=PACK), w2_raw[1][:].rearrange("p j c -> p c j"), 1.0, 0.0, MULT, ADD)
-        round_pairs(0)
+        for u in range(2):
+            round_pairs(0, slice(u, u + 1))
         last_neighbours(LAST)
         round_pairs(1)
         round_pairs(2)

@@ -60,7 +60,7 @@ def tile_picked_cahn8_none_p_kernel(tc, x_words, x_scales, w1, gn, w2, offs, wes
         nc.sync.dma_start(xw[:], x_words[0].rearrange("p n t -> p (n t)").bitcast(I32))
         nc.sync.dma_start(offs_t[:], offs)
         for q in range(4):
-            nc.sync.dma_start(xs[32 * q : 32 * q + 4, :].bitcast(I32), x_scales[0, 4 * q : 4 * q + 4, :].bitcast(I32))
+            nc.sync.dma_start(xs[q:P:32, :].bitcast(I32), x_scales[0, q:16:4, :].bitcast(I32))
         nc.sync.dma_start(w1_raw[:], w1_rows)
         nc.sync.dma_start(w2_raw[0][:], w2_rows[:, :, halves[0]])
         nc.sync.dma_start(west_t[:], west)
@@ -173,9 +173,14 @@ def tile_picked_cahn8_none_p_kernel(tc, x_words, x_scales, w1, gn, w2, offs, wes
             nc.scalar.activation(y[0][:, c], pre0[h][:], ACT.Tanh)
         for c in halves:
             nc.scalar.activation(sq[0][:, c], y[0][:, c], ACT.Square, scale=math.sqrt(2.0))
-        for t in range(1, PACK):
-            nc.scalar.activation(y[t], pre[t][:], ACT.Tanh)
+        nc.scalar.activation(y[1], pre[1][:], ACT.Tanh)
+        for t in range(1, LAST):
+            nc.scalar.activation(y[t + 1], pre[t + 1][:], ACT.Tanh)
             nc.scalar.activation(sq[t], y[t], ACT.Square, scale=math.sqrt(0.5 if t == 2 else 2.0))
+        y_west = sb("y_west", [P, S], F32)
+        nc.scalar.activation(y4[3][:], y[3], ACT.Copy, scale=-6.0)
+        nc.scalar.activation(sq[LAST], y[LAST], ACT.Square, scale=math.sqrt(2.0))
+        nc.scalar.activation(y_west[:], y_win[LAST][:].indirect(west_t[:]), ACT.Copy)
         nc.vector.tensor_scalar(y4[0][:], y[0], 4.0, None, MULT)
         add_turned(y4[0], 0, first=True)
         for repeat in range(4):
@@ -195,10 +200,7 @@ def tile_picked_cahn8_none_p_kernel(tc, x_words, x_scales, w1, gn, w2, offs, wes
         add_east(2, whole)
         neighbours(0)
         add_turned(y4[2], 2)
-        nc.scalar.activation(y4[3][:], y[3], ACT.Copy, scale=-6.0)
         add_turned(y4[3], 3)
-        y_west = sb("y_west", [P, S], F32)
-        nc.scalar.activation(y_west[:], y_win[LAST][:].indirect(west_t[:]), ACT.Copy)
         for c in halves:
             nc.vector.tensor_tensor(part[LAST][:, c], y_west[:, c], cube[LAST][:, c], SUB)
         for c in halves:
@@ -250,7 +252,7 @@ def tile_picked_cahn8_none_p_kernel(tc, x_words, x_scales, w1, gn, w2, offs, wes
             add_block(re[2][:, blocks[j]], 2, j)
             (fetch_vector if j < 2 else fetch_scalar)(rw[LAST][:, blocks[j]], west_t, LAST, blocks[j])
             from_east = sb(f"re_last{j}", [P, P], F32)[:]
-            (fetch_vector if j < 2 else fetch_scalar)(from_east, east_t, LAST, blocks[j])
+            (fetch_vector if j < 1 else fetch_scalar)(from_east, east_t, LAST, blocks[j])
             add_block(rw[LAST][:, blocks[j]], LAST, j)
             add_block(from_east, LAST, j, last=True)
 

@@ -205,10 +205,14 @@ def tile_picked_cahn8_none_p_kernel(tc, x_words, x_scales, w1, gn, w2, offs, wes
             nc.vector.tensor_tensor(part[LAST][:, c], y_west[:, c], cube[LAST][:, c], SUB)
         for c in halves:
             add_east(LAST, c)
-        neighbours(1)
-        add_turned(r[2], 2)
-        fetch_scalar(rw[2][:], west_t, 2, whole)
+        add_turned(r[1], 1)
         add_turned(cube[LAST], LAST)
+        fetch_scalar(rw[1][:], west_t, 1, whole)
+        add_turned(rw[1], 1)
+        add_turned(r[2], 2)
+        fetch_scalar(re[1][:], east_t, 1, whole)
+        add_turned(re[1], 1)
+        fetch_scalar(rw[2][:], west_t, 2, whole)
         add_turned(rw[2], 2)
         for c in halves:
             fetch_scalar(re[2][:, c], east_t, 2, c)

@@ -133,7 +133,7 @@ def tile_picked_cahn8_none_p_kernel(tc, x_words, x_scales, w1, gn, w2, offs, wes
         sq = [sb("sq_0", [P, S], F32)[:]] + [w[:, S : 2 * S] for w in y_win[1:]]
         part = [w[:, S : 2 * S] for w in r_win[:LAST]] + [sb("part_3", [P, S], F32)[:]]
         whole = slice(0, S)
-        y4 = {0: sb("y4_0", [P, S], F32), 2: y_win[0], 3: sb("y4_3", [P, S], F32)}
+        y4 = {0: sb("y4_0", [P, S], F32), 2: sb("y4_2", [P, S], F32), 3: sb("y4_3", [P, S], F32)}
         turned = [bank(4 + j, [P, PACK, P], f"turned{j}") for j in range(BLOCKS)]
 
         def look(lst, c):
@@ -147,8 +147,7 @@ def tile_picked_cahn8_none_p_kernel(tc, x_words, x_scales, w1, gn, w2, offs, wes
                 add_block(term[:, blocks[j]], t, j, first)
 
         def cubes(t, c):
-            factor = y4[2] if t == 2 else y[t]
-            nc.vector.scalar_tensor_tensor(cube[t][:, c], sq[t][:, c], 2.0 if t == LAST else 0.0, factor[:, c], ADD, MULT)
+            nc.vector.scalar_tensor_tensor(cube[t][:, c], sq[t][:, c], 2.0 if t == LAST else 0.0, y[t][:, c], ADD, MULT)
 
         def add_west(t, c):
             nc.vector.tensor_tensor(part[t][:, c], y_win[t][:].indirect(look(west_t, c)), cube[t][:, c], SUB)
@@ -176,7 +175,7 @@ def tile_picked_cahn8_none_p_kernel(tc, x_words, x_scales, w1, gn, w2, offs, wes
         nc.scalar.activation(y[1], pre[1][:], ACT.Tanh)
         for t in range(1, LAST):
             nc.scalar.activation(y[t + 1], pre[t + 1][:], ACT.Tanh)
-            nc.scalar.activation(sq[t], y[t], ACT.Square, scale=math.sqrt(0.5 if t == 2 else 2.0))
+            nc.scalar.activation(sq[t], y[t], ACT.Square, scale=math.sqrt(2.0))
         y_west = sb("y_west", [P, S], F32)
         nc.scalar.activation(y4[3][:], y[3], ACT.Copy, scale=-6.0)
         nc.scalar.activation(sq[LAST], y[LAST], ACT.Square, scale=math.sqrt(2.0))
@@ -190,11 +189,13 @@ def tile_picked_cahn8_none_p_kernel(tc, x_words, x_scales, w1, gn, w2, offs, wes
                 step(0, c)
         for c in halves:
             add_east(0, c)
-        cubes(1, whole)
-        nc.vector.tensor_scalar(y4[2][:], y[2], 4.0, None, MULT)
-        add_west(1, whole)
+        for step in (cubes, add_west):
+            for c in halves:
+                step(1, c)
+        add_east(1, halves[0])
         cubes(2, whole)
-        add_east(1, whole)
+        add_east(1, halves[1])
+        nc.vector.tensor_scalar(y4[2][:], y[2], 4.0, None, MULT)
         add_west(2, whole)
         cubes(LAST, whole)
         add_east(2, whole)

@@ -19,6 +19,8 @@ MULT = mybir.AluOpType.mult
 ADD = mybir.AluOpType.add
 SUB = mybir.AluOpType.subtract
 
+WIDTH = {F32: 4, I32: 4, U32: 4, BF16: 2, U16: 2, U8: 1}
+
 P = 128
 PACK = 4
 HALF = S // 2
@@ -32,8 +34,14 @@ def tile_picked_cahn8_none_p_kernel(tc, x_words, x_scales, w1, gn, w2, offs, wes
         keep = ctx.enter_context(tc.tile_pool(name="keep", bufs=1))
         psum = ctx.enter_context(tc.psum_pool(name="psum", bufs=1))
 
-        def sb(name, shape, dtype, over=None):
-            return keep.tile(shape, dtype, name=name, tag=over or name, align_bytes=64)
+        free, place = [0], {}
+
+        def sb(name, shape, dtype, over=None, phase=0, room=0):
+            if over is None:
+                place[name] = free[0] + phase
+                size = max(room, math.prod(shape[1:]) * WIDTH[dtype]) + phase
+                free[0] = free[0] + -(-size // 256) * 256
+            return keep.tile(shape, dtype, name=name, tag=over or name, align_bytes=64 if phase else 256, offset=place[over or name])
 
         def bank(b, shape, name):
             return psum.tile(shape, F32, name=name, tag=f"bank{b}")
@@ -49,7 +57,7 @@ def tile_picked_cahn8_none_p_kernel(tc, x_words, x_scales, w1, gn, w2, offs, wes
         w1_raw = sb("w1_raw", [P, PACK, H], F32)
         w2_raw = [sb(f"w2_raw{h}", [P, PACK, N // 2], F32) for h in range(2)]
         g = sb("g", [P, PACK], F32)
-        ident = sb("ident", [P, P], F32)
+        ident = sb("ident", [P, P], F32, phase=192)
         halves = [slice(0, HALF), slice(HALF, S)]
         blocks = [slice(j * P, (j + 1) * P) for j in range(BLOCKS)]
 
@@ -256,7 +264,7 @@ def tile_picked_cahn8_none_p_kernel(tc, x_words, x_scales, w1, gn, w2, offs, wes
         def last_neighbours(j):
             add_block(re[2][:, blocks[j]], 2, j)
             (fetch_vector if j < 2 else fetch_scalar)(rw[LAST][:, blocks[j]], west_t, LAST, blocks[j])
-            from_east = sb(f"re_last{j}", [P, P], F32)[:]
+            from_east = sb(f"re_last{j}", [P, P], F32, room=2 * HALF * PACK if j == 0 else 0)[:]
             (fetch_vector if j < 1 else fetch_scalar)(from_east, east_t, LAST, blocks[j])
             add_block(rw[LAST][:, blocks[j]], LAST, j)
             add_block(from_east, LAST, j, last=True)

@@ -187,7 +187,6 @@ def tile_picked_cahn8_none_p_kernel(tc, x_words, x_scales, w1, gn, w2, offs, wes
         y_west = sb("y_west", [P, S], F32)
         nc.scalar.activation(y4[3][:], y[3], ACT.Copy, scale=-6.0)
         nc.scalar.activation(sq[LAST], y[LAST], ACT.Square, scale=math.sqrt(2.0))
-        nc.scalar.activation(y_west[:], y_win[LAST][:].indirect(west_t[:]), ACT.Copy)
         nc.vector.tensor_scalar(y4[0][:], y[0], 4.0, None, MULT)
         add_turned(y4[0], 0, first=True)
         for repeat in range(4):
@@ -207,19 +206,20 @@ def tile_picked_cahn8_none_p_kernel(tc, x_words, x_scales, w1, gn, w2, offs, wes
         add_west(2, whole)
         cubes(LAST, whole)
         add_east(2, whole)
-        neighbours(0)
-        add_turned(y4[2], 2)
         add_turned(y4[3], 3)
+        neighbours(0)
+        nc.scalar.activation(y_west[:], y_win[LAST][:].indirect(west_t[:]), ACT.Copy)
         for c in halves:
             nc.vector.tensor_tensor(part[LAST][:, c], y_west[:, c], cube[LAST][:, c], SUB)
         for c in halves:
             add_east(LAST, c)
         add_turned(r[1], 1)
-        add_turned(cube[LAST], LAST)
+        add_turned(y4[2], 2)
         fetch_scalar(rw[1][:], west_t, 1, whole)
         add_turned(rw[1], 1)
-        add_turned(r[2], 2)
+        add_turned(cube[LAST], LAST)
         fetch_scalar(re[1][:], east_t, 1, whole)
+        add_turned(r[2], 2)
         add_turned(re[1], 1)
         fetch_scalar(rw[2][:], west_t, 2, whole)
         add_turned(rw[2], 2)

@@ -55,7 +55,7 @@ def tile_picked_cahn8_none_p_kernel(tc, x_words, x_scales, w1, gn, w2, offs, wes
         xw = sb("xw", [P, T], I32)
         xs = sb("xs", [P, T], U8)
         w1_raw = sb("w1_raw", [P, PACK, H], F32)
-        w2_raw = [sb(f"w2_raw{h}", [P, PACK, N // 2], F32) for h in range(2)]
+        w2_raw = [sb(f"w2_raw{a}", [P, PACK, width], F32) for a, width in enumerate((P, P, HALF))]
         g = sb("g", [P, PACK], F32)
         ident = sb("ident", [P, P], F32, phase=192)
         halves = [slice(0, HALF), slice(HALF, S)]
@@ -65,15 +65,23 @@ def tile_picked_cahn8_none_p_kernel(tc, x_words, x_scales, w1, gn, w2, offs, wes
         w2_rows = w2.rearrange("(p j) c -> p j c", j=PACK)
         nc.gpsimd.memset(xs[:].bitcast(I32), 0)
         nc.scalar.dma_start(g[:], gn.rearrange("(p t) o -> p (t o)", t=PACK))
-        nc.sync.dma_start(xw[:], x_words[0].rearrange("p n t -> p (n t)").bitcast(I32))
+        x_rows = x_words[0].rearrange("p n t -> p (n t)").bitcast(I32)
+        nc.sync.dma_start(xw[:, 0 : T // 4], x_rows[:, 0 : T // 4])
         nc.sync.dma_start(offs_t[:], offs)
-        for q in range(4):
-            nc.sync.dma_start(xs[q:P:32, :].bitcast(I32), x_scales[0, q:16:4, :].bitcast(I32))
+        nc.sync.dma_start(xs[0:P:8, :].bitcast(I32), x_scales[0].bitcast(I32))
+        nc.sync.dma_start(xw[:, T // 4 : T], x_rows[:, T // 4 : T])
         nc.sync.dma_start(w1_raw[:], w1_rows)
-        nc.sync.dma_start(w2_raw[0][:], w2_rows[:, :, halves[0]])
+        nc.sync.dma_start(w2_raw[0][:], w2_rows[:, :, blocks[0]])
+        picked_s = sb("picked_s", [P, S], U8)
+        xg_s = sb("xg_s", [P, S], U8)
+        nc.vector.tensor_copy(picked_s[:], xs[:].indirect(offs_t[:]))
+        nc.vector.tensor_copy(xg_s[:].bitcast(I32), picked_s[:].bitcast(I32))
+        for i in range(1, 4):
+            nc.sync.dma_start(xg_s[i:P:32, :].bitcast(I32), picked_s[8 * i : P : 32, :].bitcast(I32))
+        nc.sync.dma_start(w2_raw[1][:], w2_rows[:, :, blocks[1]])
         nc.sync.dma_start(west_t[:], west)
         nc.sync.dma_start(east_t[:], east)
-        nc.sync.dma_start(w2_raw[1][:], w2_rows[:, :, halves[1]])
+        nc.sync.dma_start(w2_raw[2][:], w2_rows[:, :, halves[1]])
         make_identity(nc, ident[:])
 
         spread = bank(5, [P, PACK, P], "spread")
@@ -85,12 +93,10 @@ def tile_picked_cahn8_none_p_kernel(tc, x_words, x_scales, w1, gn, w2, offs, wes
         gain_row = sb("gain_row", [P, 2, P, 2], F32)
         nc.scalar.activation(gain_row[:], spread[:].rearrange("q (u e) p -> q u p e", e=2), ACT.Copy, scale=0.25)
 
-        xg_s = sb("xg_s", [P, S], U8)
         xg = sb("xg", [P, S], U32)
         w1_codes = sb("w1_codes", [P, H], U32)
         w1_scales = sb("w1_scales", [P, H], U8)
         nc.vector.tensor_copy(xg[:], xw[:].bitcast(U32).indirect(offs_t[:]))
-        nc.vector.tensor_copy(xg_s[:], xs[:].indirect(offs_t[:]))
         w1_view = w1_raw[:].rearrange("p j (m t) -> p m j t", t=PACK)
         w1_bf = [sb(f"w1_bf{u}", [P, 2 * P * PACK], BF16) for u in range(2)]
 
@@ -118,11 +124,11 @@ def tile_picked_cahn8_none_p_kernel(tc, x_words, x_scales, w1, gn, w2, offs, wes
 
         w2_scales = sb("w2_scales", [P, N], U8)
 
-        def weave_w2(c, copy, over):
-            woven = sb(f"w2_bf{c.start}", [P, (c.stop - c.start) * PACK], BF16, over)
-            h, c0 = divmod(c.start, HALF)
-            raw = w2_raw[h][:, :, c0 : c0 + c.stop - c.start]
-            copy(woven[:].rearrange("p (c i j) -> p c j i", i=4, j=PACK), raw.rearrange("p j (c i) -> p c j i", i=4))
+        def weave_w2_first():
+            woven = sb("w2_first", [P, HALF * PACK], BF16, "w1_bf0")
+            for a in range(2):
+                nc.vector.tensor_copy(woven[:, a * S : (a + 1) * S].rearrange("p (c i j) -> p c j i", i=4, j=PACK),
+                                      w2_raw[a][:].rearrange("p j (c i) -> p c j i", i=4))
             return woven
 
         w2_codes = {}
@@ -133,13 +139,15 @@ def tile_picked_cahn8_none_p_kernel(tc, x_words, x_scales, w1, gn, w2, offs, wes
             for a in range(c.start // P, c.stop // P):
                 w2_codes[a] = codes[:, a * P - c.start : (a + 1) * P - c.start]
 
-        cube, rw, re = [planes(name) for name in ("cube", "rw", "re")]
+        rw, re = planes("rw"), planes("re")
+        cube = [sb(f"cube_{t}", [P, S], F32) for t in range(PACK)]
         y_win = [sb("y_win0", [P, S], F32)] + [sb(f"y_win{t}", [P, 2 * S], F32) for t in range(1, PACK)]
         r_win = [sb(f"r_win{t}", [P, 2 * S], F32) for t in range(LAST)] + [sb("r_win3", [P, S], F32)]
         y = [w[:, 0:S] for w in y_win]
         r = [w[:, 0:S] for w in r_win]
         sq = [sb("sq_0", [P, S], F32)[:]] + [w[:, S : 2 * S] for w in y_win[1:]]
-        part = [w[:, S : 2 * S] for w in r_win[:LAST]] + [sb("part_3", [P, S], F32)[:]]
+        part = [w[:, S : 2 * S] for w in r_win[:LAST]]
+        part_last = [sb(f"part_last{h}", [P, HALF], F32) for h in range(2)]
         whole = slice(0, S)
         y4 = {0: sb("y4_0", [P, S], F32), 2: sb("y4_2", [P, S], F32), 3: sb("y4_3", [P, S], F32)}
         turned = [bank(4 + j, [P, PACK, P], f"turned{j}") for j in range(BLOCKS)]
@@ -175,7 +183,7 @@ def tile_picked_cahn8_none_p_kernel(tc, x_words, x_scales, w1, gn, w2, offs, wes
                 fetch_scalar(dst[t][:], lst, t, whole)
                 add_turned(dst[t], t)
 
-        quant_w2(halves[0], weave_w2(halves[0], nc.vector.tensor_copy, "w1_bf0"))
+        w2_first = weave_w2_first()
         for h, c in enumerate(halves):
             nc.scalar.activation(y[0][:, c], pre0[h][:], ACT.Tanh)
         for c in halves:
@@ -209,10 +217,11 @@ def tile_picked_cahn8_none_p_kernel(tc, x_words, x_scales, w1, gn, w2, offs, wes
         add_turned(y4[3], 3)
         neighbours(0)
         nc.scalar.activation(y_west[:], y_win[LAST][:].indirect(west_t[:]), ACT.Copy)
-        for c in halves:
-            nc.vector.tensor_tensor(part[LAST][:, c], y_west[:, c], cube[LAST][:, c], SUB)
-        for c in halves:
-            add_east(LAST, c)
+        for h, c in enumerate(halves):
+            nc.vector.tensor_tensor(part_last[h][:], y_west[:, c], cube[LAST][:, c], SUB)
+        for h, c in enumerate(halves):
+            nc.vector.tensor_tensor(r[LAST][:, c], y_win[LAST][:].indirect(look(east_t, c)), part_last[h][:], ADD)
+        quant_w2(halves[0], w2_first, "part_last0")
         add_turned(r[1], 1)
         add_turned(y4[2], 2)
         fetch_scalar(rw[1][:], west_t, 1, whole)
@@ -272,7 +281,7 @@ def tile_picked_cahn8_none_p_kernel(tc, x_words, x_scales, w1, gn, w2, offs, wes
         for j in range(LAST):
             last_neighbours(j)
         w2_last = sb("w2_last", [P, HALF * PACK], BF16, "re_last0")
-        nc.gpsimd.tensor_scalar(w2_last[:].rearrange("p (c j) -> p c j", j=PACK), w2_raw[1][:].rearrange("p j c -> p c j"), 1.0, 0.0, MULT, ADD)
+        nc.gpsimd.tensor_scalar(w2_last[:].rearrange("p (c j) -> p c j", j=PACK), w2_raw[2][:].rearrange("p j c -> p c j"), 1.0, 0.0, MULT, ADD)
         for u in range(2):
             round_pairs(0, slice(u, u + 1))
         last_neighbours(LAST)

@@ -54,7 +54,7 @@ def tile_picked_cahn8_none_p_kernel(tc, x_words, x_scales, w1, gn, w2, offs, wes
         east_t = sb("east_t", [P, S // 16], U16)
         xw = sb("xw", [P, T], I32)
         xs = sb("xs", [P, T], U8)
-        w1_raw = sb("w1_raw", [P, PACK, H], F32)
+        w1_raw = [sb(f"w1_raw{h}", [P, PACK, H // 2], F32) for h in range(2)]
         w2_raw = [sb(f"w2_raw{a}", [P, PACK, width], F32) for a, width in enumerate((P, P, HALF))]
         g = sb("g", [P, PACK], F32)
         ident = sb("ident", [P, P], F32, phase=192)
@@ -70,7 +70,8 @@ def tile_picked_cahn8_none_p_kernel(tc, x_words, x_scales, w1, gn, w2, offs, wes
         nc.sync.dma_start(offs_t[:], offs)
         nc.sync.dma_start(xs[0:P:8, :].bitcast(I32), x_scales[0].bitcast(I32))
         nc.sync.dma_start(xw[:, T // 4 : T], x_rows[:, T // 4 : T])
-        nc.sync.dma_start(w1_raw[:], w1_rows)
+        for h, c in enumerate(halves):
+            nc.sync.dma_start(w1_raw[h][:], w1_rows[:, :, c])
         nc.sync.dma_start(w2_raw[0][:], w2_rows[:, :, blocks[0]])
         picked_s = sb("picked_s", [P, S], U8)
         xg_s = sb("xg_s", [P, S], U8)
@@ -97,19 +98,27 @@ def tile_picked_cahn8_none_p_kernel(tc, x_words, x_scales, w1, gn, w2, offs, wes
         w1_codes = sb("w1_codes", [P, H], U32)
         w1_scales = sb("w1_scales", [P, H], U8)
         nc.vector.tensor_copy(xg[:], xw[:].bitcast(U32).indirect(offs_t[:]))
-        w1_view = w1_raw[:].rearrange("p j (m t) -> p m j t", t=PACK)
+        w1_view = [raw[:].rearrange("p j (m t) -> p m j t", t=PACK) for raw in w1_raw]
         w1_bf = [sb(f"w1_bf{u}", [P, 2 * P * PACK], BF16) for u in range(2)]
 
         def weave_w1(u, copy, ms):
-            copy(w1_bf[u][:].rearrange("p (t m j) -> p m j t", t=2, j=PACK)[:, ms], w1_view[:, ms, :, 2 * u : 2 * u + 2])
+            h, m0 = divmod(ms.start, P // 2)
+            copy(w1_bf[u][:].rearrange("p (t m j) -> p m j t", t=2, j=PACK)[:, ms], w1_view[h][:, m0 : m0 + ms.stop - ms.start, :, 2 * u : 2 * u + 2])
 
-        weave_w1(0, nc.vector.tensor_copy, slice(0, 80))
-        weave_w1(0, nc.scalar.copy, slice(80, P))
-        weave_w1(1, nc.scalar.copy, slice(0, P // 2))
-        weave_w1(1, nc.vector.tensor_copy, slice(P // 2, P))
-        for t in range(2):
-            nc.vector.quantize_mx(w1_codes[:, blocks[t]].bitcast(FP8X4), w1_scales[:, blocks[t]], w1_bf[0][:, t * S : (t + 1) * S])
-        nc.vector.quantize_mx(w1_codes[:, halves[1]].bitcast(FP8X4), w1_scales[:, halves[1]], w1_bf[1][:])
+        def quant_w1(h):
+            for t in range(PACK):
+                c = slice(t * P + h * P // 2, t * P + (h + 1) * P // 2)
+                first = (t % 2) * S + h * HALF
+                nc.vector.quantize_mx(w1_codes[:, c].bitcast(FP8X4), w1_scales[:, c], w1_bf[t // 2][:, first : first + HALF])
+
+        weave_w1(0, nc.vector.tensor_copy, slice(0, 64))
+        weave_w1(1, nc.scalar.copy, slice(0, 64))
+        quant_w1(0)
+        weave_w1(0, nc.vector.tensor_copy, slice(64, 108))
+        weave_w1(0, nc.scalar.copy, slice(108, P))
+        weave_w1(1, nc.vector.tensor_copy, slice(64, 96))
+        weave_w1(1, nc.scalar.copy, slice(96, P))
+        quant_w1(1)
         pre0 = [bank(4 * h, [P, HALF], f"pre0{h}") for h in range(2)]
         pre = [None] + [bank(t, [P, S], f"pre{t}") for t in range(1, PACK)]
 
@@ -151,16 +160,18 @@ def tile_picked_cahn8_none_p_kernel(tc, x_words, x_scales, w1, gn, w2, offs, wes
         whole = slice(0, S)
         y4 = {0: sb("y4_0", [P, S], F32), 2: sb("y4_2", [P, S], F32), 3: sb("y4_3", [P, S], F32)}
         turned = [bank(4 + j, [P, PACK, P], f"turned{j}") for j in range(BLOCKS)]
+        early = bank(0, [P, 2, P], "early")
 
         def look(lst, c):
             return lst[:, c.start // 16 : c.stop // 16]
 
         def add_block(term, t, j, first=False, last=False):
-            nc.tensor.matmul(turned[j][:, t, :], lhsT=term, rhs=ident[:], start=first, stop=last, is_transpose=True)
+            sums = early if j == 0 and t < 2 else turned[j]
+            nc.tensor.matmul(sums[:, t, :], lhsT=term, rhs=ident[:], start=first, stop=last, is_transpose=True)
 
-        def add_turned(term, t, first=False):
+        def add_turned(term, t, first=(), last=()):
             for j in range(BLOCKS):
-                add_block(term[:, blocks[j]], t, j, first)
+                add_block(term[:, blocks[j]], t, j, j in first, j in last)
 
         def cubes(t, c):
             nc.vector.scalar_tensor_tensor(cube[t][:, c], sq[t][:, c], 2.0 if t == LAST else 0.0, y[t][:, c], ADD, MULT)
@@ -196,7 +207,7 @@ def tile_picked_cahn8_none_p_kernel(tc, x_words, x_scales, w1, gn, w2, offs, wes
         nc.scalar.activation(y4[3][:], y[3], ACT.Copy, scale=-6.0)
         nc.scalar.activation(sq[LAST], y[LAST], ACT.Square, scale=math.sqrt(2.0))
         nc.vector.tensor_scalar(y4[0][:], y[0], 4.0, None, MULT)
-        add_turned(y4[0], 0, first=True)
+        add_turned(y4[0], 0, first=range(BLOCKS))
         for repeat in range(4):
             add_turned(y[1], 1)
         for step in (cubes, add_west):
@@ -214,7 +225,7 @@ def tile_picked_cahn8_none_p_kernel(tc, x_words, x_scales, w1, gn, w2, offs, wes
         add_west(2, whole)
         cubes(LAST, whole)
         add_east(2, whole)
-        add_turned(y4[3], 3)
+        add_turned(y4[3], 3, first=[0])
         neighbours(0)
         nc.scalar.activation(y_west[:], y_win[LAST][:].indirect(west_t[:]), ACT.Copy)
         for h, c in enumerate(halves):
@@ -229,7 +240,7 @@ def tile_picked_cahn8_none_p_kernel(tc, x_words, x_scales, w1, gn, w2, offs, wes
         add_turned(cube[LAST], LAST)
         fetch_scalar(re[1][:], east_t, 1, whole)
         add_turned(r[2], 2)
-        add_turned(re[1], 1)
+        add_turned(re[1], 1, last=[0])
         fetch_scalar(rw[2][:], west_t, 2, whole)
         add_turned(rw[2], 2)
         for c in halves:
@@ -243,7 +254,7 @@ def tile_picked_cahn8_none_p_kernel(tc, x_words, x_scales, w1, gn, w2, offs, wes
         out_rows = out.rearrange("(a p) j -> p a j", p=P)
 
         def round_pairs(j, us=slice(0, 2)):
-            sums = turned[j][:].rearrange("q (u e) p -> q u p e", e=2)
+            sums = (early if j == 0 and us.stop == 1 else turned[j])[:].rearrange("q (u e) p -> q u p e", e=2)
             nc.vector.tensor_tensor(pairs[j][:].rearrange("q u (p e) -> q u p e", e=2)[:, us], sums[:, us], gain_row[:, us], MULT)
             for u in range(us.start, us.stop):
                 nc.tensor.transpose(back[j][:, u, :], pairs[j][:, u, :].bitcast(F32), ident[:])
@@ -305,4 +316,4 @@ def tile_picked_cahn8_none_p_kernel(tc, x_words, x_scales, w1, gn, w2, offs, wes
                                 rhs=z_codes[LAST][:].bitcast(FP8X4), rhs_scale=z_scales[LAST][:], start=True, stop=True)
             (nc.vector.tensor_copy if a % 2 == 0 else nc.scalar.copy)(results[LAST][:, a, :], acc[:])
         nc.sync.dma_start(out_rows[:, 0:2, blocks[LAST]], results[LAST][:, 0:2, :])
-        nc.scalar.dma_start(out_rows[:, 2:4, blocks[LAST]], results[LAST][:, 2:4, :])
+        nc.sync.dma_start(out_rows[:, 2:4, blocks[LAST]], results[LAST][:, 2:4, :])

@@ -18,14 +18,18 @@ ACT = mybir.ActivationFunctionType
 MULT = mybir.AluOpType.mult
 ADD = mybir.AluOpType.add
 SUB = mybir.AluOpType.subtract
-
-WIDTH = {F32: 4, I32: 4, U32: 4, BF16: 2, U16: 2, U8: 1}
+ITEM_BYTES = {F32: 4, I32: 4, U32: 4, BF16: 2, U16: 2, U8: 1}
 
 P = 128
 PACK = 4
+LAST = PACK - 1
 HALF = S // 2
 BLOCKS = S // P
-LAST = PACK - 1
+UNIT = 256
+IDENT_AT = 192
+X_FIRST = T // 4
+W1_SPLIT = (108, 96)
+WEST_ON_VECTOR, EAST_ON_VECTOR = 2, 1
 
 
 def tile_picked_cahn8_none_p_kernel(tc, x_words, x_scales, w1, gn, w2, offs, west, east, out):
@@ -33,52 +37,49 @@ def tile_picked_cahn8_none_p_kernel(tc, x_words, x_scales, w1, gn, w2, offs, wes
     with ExitStack() as ctx:
         keep = ctx.enter_context(tc.tile_pool(name="keep", bufs=1))
         psum = ctx.enter_context(tc.psum_pool(name="psum", bufs=1))
-
         free, place = [0], {}
 
         def sb(name, shape, dtype, over=None, phase=0, room=0):
             if over is None:
                 place[name] = free[0] + phase
-                size = max(room, math.prod(shape[1:]) * WIDTH[dtype]) + phase
-                free[0] = free[0] + -(-size // 256) * 256
-            return keep.tile(shape, dtype, name=name, tag=over or name, align_bytes=64 if phase else 256, offset=place[over or name])
+                size = max(room, math.prod(shape[1:]) * ITEM_BYTES[dtype]) + phase
+                free[0] = free[0] + -(-size // UNIT) * UNIT
+            return keep.tile(shape, dtype, name=name, tag=over or name, align_bytes=64 if phase else UNIT, offset=place[over or name])
 
         def bank(b, shape, name):
             return psum.tile(shape, F32, name=name, tag=f"bank{b}")
 
-        def planes(name):
-            return [sb(f"{name}_{t}", [P, S], F32) for t in range(PACK)]
+        halves = [slice(0, HALF), slice(HALF, S)]
+        blocks = [slice(j * P, (j + 1) * P) for j in range(BLOCKS)]
+        whole = slice(0, S)
 
         offs_t = sb("offs_t", [P, S // 16], U16)
         west_t = sb("west_t", [P, S // 16], U16)
         east_t = sb("east_t", [P, S // 16], U16)
-        xw = sb("xw", [P, T], I32)
-        xs = sb("xs", [P, T], U8)
+        x_win = sb("x_win", [P, T], I32)
+        scale_win = sb("scale_win", [P, T], U8)
         w1_raw = [sb(f"w1_raw{h}", [P, PACK, H // 2], F32) for h in range(2)]
         w2_raw = [sb(f"w2_raw{a}", [P, PACK, width], F32) for a, width in enumerate((P, P, HALF))]
         g = sb("g", [P, PACK], F32)
-        ident = sb("ident", [P, P], F32, phase=192)
-        halves = [slice(0, HALF), slice(HALF, S)]
-        blocks = [slice(j * P, (j + 1) * P) for j in range(BLOCKS)]
-
+        ident = sb("ident", [P, P], F32, phase=IDENT_AT)
         w1_rows = w1.rearrange("(p j) c -> p j c", j=PACK)
         w2_rows = w2.rearrange("(p j) c -> p j c", j=PACK)
-        nc.gpsimd.memset(xs[:].bitcast(I32), 0)
+        nc.gpsimd.memset(scale_win[:].bitcast(I32), 0)
         nc.scalar.dma_start(g[:], gn.rearrange("(p t) o -> p (t o)", t=PACK))
         x_rows = x_words[0].rearrange("p n t -> p (n t)").bitcast(I32)
-        nc.sync.dma_start(xw[:, 0 : T // 4], x_rows[:, 0 : T // 4])
+        nc.sync.dma_start(x_win[:, 0:X_FIRST], x_rows[:, 0:X_FIRST])
         nc.sync.dma_start(offs_t[:], offs)
-        nc.sync.dma_start(xs[0:P:8, :].bitcast(I32), x_scales[0].bitcast(I32))
-        nc.sync.dma_start(xw[:, T // 4 : T], x_rows[:, T // 4 : T])
+        nc.sync.dma_start(scale_win[0:P:8, :].bitcast(I32), x_scales[0].bitcast(I32))
+        nc.sync.dma_start(x_win[:, X_FIRST:T], x_rows[:, X_FIRST:T])
         for h, c in enumerate(halves):
             nc.sync.dma_start(w1_raw[h][:], w1_rows[:, :, c])
         nc.sync.dma_start(w2_raw[0][:], w2_rows[:, :, blocks[0]])
-        picked_s = sb("picked_s", [P, S], U8)
-        xg_s = sb("xg_s", [P, S], U8)
-        nc.vector.tensor_copy(picked_s[:], xs[:].indirect(offs_t[:]))
-        nc.vector.tensor_copy(xg_s[:].bitcast(I32), picked_s[:].bitcast(I32))
+        picked_scales = sb("picked_scales", [P, S], U8)
+        x_scale = sb("x_scale", [P, S], U8)
+        nc.vector.tensor_copy(picked_scales[:], scale_win[:].indirect(offs_t[:]))
+        nc.vector.tensor_copy(x_scale[:].bitcast(I32), picked_scales[:].bitcast(I32))
         for i in range(1, 4):
-            nc.sync.dma_start(xg_s[i:P:32, :].bitcast(I32), picked_s[8 * i : P : 32, :].bitcast(I32))
+            nc.sync.dma_start(x_scale[i:P:32, :].bitcast(I32), picked_scales[8 * i : P : 32, :].bitcast(I32))
         nc.sync.dma_start(w2_raw[1][:], w2_rows[:, :, blocks[1]])
         nc.sync.dma_start(west_t[:], west)
         nc.sync.dma_start(east_t[:], east)
@@ -94,10 +95,10 @@ def tile_picked_cahn8_none_p_kernel(tc, x_words, x_scales, w1, gn, w2, offs, wes
         gain_row = sb("gain_row", [P, 2, P, 2], F32)
         nc.scalar.activation(gain_row[:], spread[:].rearrange("q (u e) p -> q u p e", e=2), ACT.Copy, scale=0.25)
 
-        xg = sb("xg", [P, S], U32)
+        x_codes = sb("x_codes", [P, S], U32)
         w1_codes = sb("w1_codes", [P, H], U32)
         w1_scales = sb("w1_scales", [P, H], U8)
-        nc.vector.tensor_copy(xg[:], xw[:].bitcast(U32).indirect(offs_t[:]))
+        nc.vector.tensor_copy(x_codes[:], x_win[:].bitcast(U32).indirect(offs_t[:]))
         w1_view = [raw[:].rearrange("p j (m t) -> p m j t", t=PACK) for raw in w1_raw]
         w1_bf = [sb(f"w1_bf{u}", [P, 2 * P * PACK], BF16) for u in range(2)]
 
@@ -108,38 +109,29 @@ def tile_picked_cahn8_none_p_kernel(tc, x_words, x_scales, w1, gn, w2, offs, wes
         def quant_w1(h):
             for t in range(PACK):
                 c = slice(t * P + h * P // 2, t * P + (h + 1) * P // 2)
-                first = (t % 2) * S + h * HALF
-                nc.vector.quantize_mx(w1_codes[:, c].bitcast(FP8X4), w1_scales[:, c], w1_bf[t // 2][:, first : first + HALF])
+                at = (t % 2) * S + h * HALF
+                nc.vector.quantize_mx(w1_codes[:, c].bitcast(FP8X4), w1_scales[:, c], w1_bf[t // 2][:, at : at + HALF])
 
-        weave_w1(0, nc.vector.tensor_copy, slice(0, 64))
-        weave_w1(1, nc.scalar.copy, slice(0, 64))
+        weave_w1(0, nc.vector.tensor_copy, slice(0, P // 2))
+        weave_w1(1, nc.scalar.copy, slice(0, P // 2))
         quant_w1(0)
-        weave_w1(0, nc.vector.tensor_copy, slice(64, 108))
-        weave_w1(0, nc.scalar.copy, slice(108, P))
-        weave_w1(1, nc.vector.tensor_copy, slice(64, 96))
-        weave_w1(1, nc.scalar.copy, slice(96, P))
+        for u, split in enumerate(W1_SPLIT):
+            weave_w1(u, nc.vector.tensor_copy, slice(P // 2, split))
+            weave_w1(u, nc.scalar.copy, slice(split, P))
         quant_w1(1)
         pre0 = [bank(4 * h, [P, HALF], f"pre0{h}") for h in range(2)]
-        pre = [None] + [bank(t, [P, S], f"pre{t}") for t in range(1, PACK)]
+        pre = {t: bank(t, [P, S], f"pre{t}") for t in range(1, PACK)}
 
         def first_product(acc, t, c):
             nc.tensor.matmul_mx(acc, lhsT=w1_codes[:, blocks[t]].bitcast(FP8X4), lhsT_scale=w1_scales[:, blocks[t]],
-                                rhs=xg[:, c].bitcast(FP8X4), rhs_scale=xg_s[:, c], start=True, stop=True)
+                                rhs=x_codes[:, c].bitcast(FP8X4), rhs_scale=x_scale[:, c], start=True, stop=True)
 
         for h, c in enumerate(halves):
             first_product(pre0[h][:], 0, c)
         for t in range(1, PACK):
-            first_product(pre[t][:], t, slice(0, S))
+            first_product(pre[t][:], t, whole)
 
         w2_scales = sb("w2_scales", [P, N], U8)
-
-        def weave_w2_first():
-            woven = sb("w2_first", [P, HALF * PACK], BF16, "w1_bf0")
-            for a in range(2):
-                nc.vector.tensor_copy(woven[:, a * S : (a + 1) * S].rearrange("p (c i j) -> p c j i", i=4, j=PACK),
-                                      w2_raw[a][:].rearrange("p j (c i) -> p c j i", i=4))
-            return woven
-
         w2_codes = {}
 
         def quant_w2(c, woven, over=None):
@@ -148,17 +140,16 @@ def tile_picked_cahn8_none_p_kernel(tc, x_words, x_scales, w1, gn, w2, offs, wes
             for a in range(c.start // P, c.stop // P):
                 w2_codes[a] = codes[:, a * P - c.start : (a + 1) * P - c.start]
 
-        rw, re = planes("rw"), planes("re")
-        cube = [sb(f"cube_{t}", [P, S], F32) for t in range(PACK)]
-        y_win = [sb("y_win0", [P, S], F32)] + [sb(f"y_win{t}", [P, 2 * S], F32) for t in range(1, PACK)]
+        r_west = [sb(f"r_west{t}", [P, S], F32) for t in range(PACK)]
+        r_east = [sb(f"r_east{t}", [P, S], F32) for t in range(LAST)]
+        cube = [sb(f"cube{t}", [P, S], F32) for t in range(PACK)]
+        y_win = [sb(f"y_win{t}", [P, 2 * S], F32) for t in range(PACK)]
         r_win = [sb(f"r_win{t}", [P, 2 * S], F32) for t in range(LAST)] + [sb("r_win3", [P, S], F32)]
         y = [w[:, 0:S] for w in y_win]
         r = [w[:, 0:S] for w in r_win]
-        sq = [sb("sq_0", [P, S], F32)[:]] + [w[:, S : 2 * S] for w in y_win[1:]]
-        part = [w[:, S : 2 * S] for w in r_win[:LAST]]
-        part_last = [sb(f"part_last{h}", [P, HALF], F32) for h in range(2)]
-        whole = slice(0, S)
-        y4 = {0: sb("y4_0", [P, S], F32), 2: sb("y4_2", [P, S], F32), 3: sb("y4_3", [P, S], F32)}
+        sq = [w[:, S : 2 * S] for w in y_win]
+        part = [w[:, S : 2 * S] for w in r_win[:LAST]] + [sb("part3", [P, S], F32)[:]]
+        own = {t: sb(f"own{t}", [P, S], F32) for t in (0, LAST)}
         turned = [bank(4 + j, [P, PACK, P], f"turned{j}") for j in range(BLOCKS)]
         early = bank(0, [P, 2, P], "early")
 
@@ -179,8 +170,8 @@ def tile_picked_cahn8_none_p_kernel(tc, x_words, x_scales, w1, gn, w2, offs, wes
         def add_west(t, c):
             nc.vector.tensor_tensor(part[t][:, c], y_win[t][:].indirect(look(west_t, c)), cube[t][:, c], SUB)
 
-        def add_east(t, c):
-            nc.vector.tensor_tensor(r[t][:, c], y_win[t][:].indirect(look(east_t, c)), part[t][:, c], ADD)
+        def add_east(t):
+            nc.vector.tensor_tensor(r[t], y_win[t][:].indirect(east_t[:]), part[t], ADD)
 
         def fetch_scalar(dst, lst, t, c):
             nc.scalar.activation(dst, r_win[t][:].indirect(look(lst, c)), ACT.Copy, scale=0.5 if t == LAST else -0.5)
@@ -188,70 +179,77 @@ def tile_picked_cahn8_none_p_kernel(tc, x_words, x_scales, w1, gn, w2, offs, wes
         def fetch_vector(dst, lst, t, c):
             nc.vector.tensor_scalar(dst, r_win[t][:].indirect(look(lst, c)), 0.5, 0.0, MULT, ADD)
 
-        def neighbours(t):
-            add_turned(r[t], t)
-            for dst, lst in ((rw, west_t), (re, east_t)):
-                fetch_scalar(dst[t][:], lst, t, whole)
-                add_turned(dst[t], t)
+        def fetch_and_add(dst, lst, t):
+            fetch_scalar(dst[t][:], lst, t, whole)
+            add_turned(dst[t], t)
 
-        w2_first = weave_w2_first()
+        w2_first = sb("w2_first", [P, HALF * PACK], BF16, "w1_bf0")
+        for a in range(2):
+            nc.vector.tensor_copy(w2_first[:, a * S : (a + 1) * S].rearrange("p (c i j) -> p c j i", i=4, j=PACK),
+                                  w2_raw[a][:].rearrange("p j (c i) -> p c j i", i=4))
         for h, c in enumerate(halves):
             nc.scalar.activation(y[0][:, c], pre0[h][:], ACT.Tanh)
         for c in halves:
-            nc.scalar.activation(sq[0][:, c], y[0][:, c], ACT.Square, scale=math.sqrt(2.0))
+            nc.vector.scalar_tensor_tensor(sq[0][:, c], y[0][:, c], 2.0, y[0][:, c], MULT, MULT)
         nc.scalar.activation(y[1], pre[1][:], ACT.Tanh)
         for t in range(1, LAST):
             nc.scalar.activation(y[t + 1], pre[t + 1][:], ACT.Tanh)
             nc.scalar.activation(sq[t], y[t], ACT.Square, scale=math.sqrt(2.0))
         y_west = sb("y_west", [P, S], F32)
-        nc.scalar.activation(y4[3][:], y[3], ACT.Copy, scale=-6.0)
+        nc.scalar.activation(own[LAST][:], y[LAST], ACT.Copy, scale=-6.0)
         nc.scalar.activation(sq[LAST], y[LAST], ACT.Square, scale=math.sqrt(2.0))
-        nc.vector.tensor_scalar(y4[0][:], y[0], 4.0, None, MULT)
-        add_turned(y4[0], 0, first=range(BLOCKS))
+        nc.scalar.activation(own[0][:], y[0], ACT.Copy, scale=4.0)
         for repeat in range(4):
-            add_turned(y[1], 1)
+            add_turned(y[1], 1, first=range(BLOCKS) if repeat == 0 else ())
+        add_turned(own[0], 0)
         for step in (cubes, add_west):
             for c in halves:
                 step(0, c)
-        for c in halves:
-            add_east(0, c)
-        for step in (cubes, add_west):
-            for c in halves:
-                step(1, c)
-        add_east(1, halves[0])
-        cubes(2, whole)
-        add_east(1, halves[1])
-        nc.vector.tensor_scalar(y4[2][:], y[2], 4.0, None, MULT)
-        add_west(2, whole)
-        cubes(LAST, whole)
-        add_east(2, whole)
-        add_turned(y4[3], 3, first=[0])
-        neighbours(0)
+        for t in range(LAST):
+            cubes(t + 1, whole)
+            add_east(t)
+            if t + 1 < LAST:
+                add_west(t + 1, whole)
+        add_turned(own[LAST], LAST, first=[0])
+        add_turned(r[0], 0)
+        fetch_and_add(r_west, west_t, 0)
+        fetch_and_add(r_east, east_t, 0)
         nc.scalar.activation(y_west[:], y_win[LAST][:].indirect(west_t[:]), ACT.Copy)
-        for h, c in enumerate(halves):
-            nc.vector.tensor_tensor(part_last[h][:], y_west[:, c], cube[LAST][:, c], SUB)
-        for h, c in enumerate(halves):
-            nc.vector.tensor_tensor(r[LAST][:, c], y_win[LAST][:].indirect(look(east_t, c)), part_last[h][:], ADD)
-        quant_w2(halves[0], w2_first, "part_last0")
+        nc.vector.tensor_tensor(part[LAST], y_west[:], cube[LAST][:], SUB)
+        own[2] = sb("own2", [P, S], F32, "cube2")
+        nc.vector.tensor_scalar(own[2][:], y[2], 4.0, None, MULT)
+        add_east(LAST)
+        quant_w2(halves[0], w2_first, "y_west")
         add_turned(r[1], 1)
-        add_turned(y4[2], 2)
-        fetch_scalar(rw[1][:], west_t, 1, whole)
-        add_turned(rw[1], 1)
+        fetch_and_add(r_west, west_t, 1)
         add_turned(cube[LAST], LAST)
-        fetch_scalar(re[1][:], east_t, 1, whole)
+        fetch_scalar(r_east[1][:], east_t, 1, whole)
         add_turned(r[2], 2)
-        add_turned(re[1], 1, last=[0])
-        fetch_scalar(rw[2][:], west_t, 2, whole)
-        add_turned(rw[2], 2)
+        add_turned(r_east[1], 1, last=[0])
+        add_turned(own[2], 2)
+        fetch_and_add(r_west, west_t, 2)
         for c in halves:
-            fetch_scalar(re[2][:, c], east_t, 2, c)
+            fetch_scalar(r_east[2][:, c], east_t, 2, c)
+        for j in range(2):
+            add_block(r_east[2][:, blocks[j]], 2, j)
 
         pairs = [sb(f"pairs{j}", [P, 2, 2 * P], BF16) for j in range(BLOCKS)]
         back = [bank(j, [P, 2, P], f"back{j}") for j in range(BLOCKS)]
         z_bf = [sb(f"z_bf{j}", [P, P * PACK], BF16) for j in range(BLOCKS)]
         z_codes = [sb(f"z_codes{j}", [P, P], U32) for j in range(BLOCKS)]
         z_scales = [sb(f"z_scales{j}", [P, P], U8) for j in range(BLOCKS)]
+        results = [sb(f"res{j}", [P, PACK, P], F32) for j in range(BLOCKS)]
         out_rows = out.rearrange("(a p) j -> p a j", p=P)
+
+        def last_neighbours(j):
+            if j == 1:
+                for later in (2, LAST):
+                    add_block(r_east[2][:, blocks[later]], 2, later)
+            (fetch_vector if j < WEST_ON_VECTOR else fetch_scalar)(r_west[LAST][:, blocks[j]], west_t, LAST, blocks[j])
+            from_east = sb(f"from_east{j}", [P, P], F32, room=2 * HALF * PACK if j == 0 else 0)[:]
+            (fetch_vector if j < EAST_ON_VECTOR else fetch_scalar)(from_east, east_t, LAST, blocks[j])
+            add_block(r_west[LAST][:, blocks[j]], LAST, j)
+            add_block(from_east, LAST, j, last=True)
 
         def round_pairs(j, us=slice(0, 2)):
             sums = (early if j == 0 and us.stop == 1 else turned[j])[:].rearrange("q (u e) p -> q u p e", e=2)
@@ -265,33 +263,28 @@ def tile_picked_cahn8_none_p_kernel(tc, x_words, x_scales, w1, gn, w2, offs, wes
         def quant_z(j):
             nc.vector.quantize_mx(z_codes[j][:].bitcast(FP8X4), z_scales[j][:], z_bf[j][:])
 
-        results = [sb(f"res{j}", [P, PACK, P], F32) for j in range(BLOCKS)]
+        def out_pass(acc, a, j):
+            nc.tensor.matmul_mx(acc, lhsT=w2_codes[a].bitcast(FP8X4), lhsT_scale=w2_scales[:, blocks[a]],
+                                rhs=z_codes[j][:].bitcast(FP8X4), rhs_scale=z_scales[j][:], start=True, stop=True)
 
         def product(j):
             acc = [bank(b, [P, 2, P], f"acc{j}{h}") for h, b in enumerate((4 + j, j))]
             for a in range(PACK):
-                nc.tensor.matmul_mx(acc[a // 2][:, a % 2, :], lhsT=w2_codes[a].bitcast(FP8X4), lhsT_scale=w2_scales[:, blocks[a]],
-                                    rhs=z_codes[j][:].bitcast(FP8X4), rhs_scale=z_scales[j][:], start=True, stop=True)
+                out_pass(acc[a // 2][:, a % 2, :], a, j)
             return acc
 
-        def store(j, acc, queues):
+        def store_halves(j):
+            for h in range(2):
+                nc.sync.dma_start(out_rows[:, 2 * h : 2 * h + 2, blocks[j]], results[j][:, 2 * h : 2 * h + 2, :])
+
+        def store(j, acc):
             for h, copy in enumerate((nc.scalar.copy, nc.scalar.copy if j == 0 else nc.vector.tensor_copy)):
                 copy(results[j][:, 2 * h : 2 * h + 2, :], acc[h][:])
-            rows = PACK // len(queues)
-            for i, queue in enumerate(queues):
-                queue.dma_start(out_rows[:, i * rows : (i + 1) * rows, blocks[j]], results[j][:, i * rows : (i + 1) * rows, :])
-
-        def last_neighbours(j):
-            add_block(re[2][:, blocks[j]], 2, j)
-            (fetch_vector if j < 2 else fetch_scalar)(rw[LAST][:, blocks[j]], west_t, LAST, blocks[j])
-            from_east = sb(f"re_last{j}", [P, P], F32, room=2 * HALF * PACK if j == 0 else 0)[:]
-            (fetch_vector if j < 1 else fetch_scalar)(from_east, east_t, LAST, blocks[j])
-            add_block(rw[LAST][:, blocks[j]], LAST, j)
-            add_block(from_east, LAST, j, last=True)
+            store_halves(j)
 
         for j in range(LAST):
             last_neighbours(j)
-        w2_last = sb("w2_last", [P, HALF * PACK], BF16, "re_last0")
+        w2_last = sb("w2_last", [P, HALF * PACK], BF16, "from_east0")
         nc.gpsimd.tensor_scalar(w2_last[:].rearrange("p (c j) -> p c j", j=PACK), w2_raw[2][:].rearrange("p j c -> p c j"), 1.0, 0.0, MULT, ADD)
         for u in range(2):
             round_pairs(0, slice(u, u + 1))
@@ -307,13 +300,11 @@ def tile_picked_cahn8_none_p_kernel(tc, x_words, x_scales, w1, gn, w2, offs, wes
         for j in range(1, BLOCKS):
             weave_z(j)
             quant_z(j)
-            store(j - 1, acc, [nc.sync] * 2)
+            store(j - 1, acc)
             if j < LAST:
                 acc = product(j)
-        for a in range(PACK):
-            acc = bank((LAST, 4 + LAST, 0, 4)[a], [P, P], f"acc_last{a}")
-            nc.tensor.matmul_mx(acc[:], lhsT=w2_codes[a].bitcast(FP8X4), lhsT_scale=w2_scales[:, blocks[a]],
-                                rhs=z_codes[LAST][:].bitcast(FP8X4), rhs_scale=z_scales[LAST][:], start=True, stop=True)
-            (nc.vector.tensor_copy if a % 2 == 0 else nc.scalar.copy)(results[LAST][:, a, :], acc[:])
-        nc.sync.dma_start(out_rows[:, 0:2, blocks[LAST]], results[LAST][:, 0:2, :])
-        nc.sync.dma_start(out_rows[:, 2:4, blocks[LAST]], results[LAST][:, 2:4, :])
+        for a, b in enumerate((LAST, 4 + LAST, 0, 4)):
+            rows = bank(b, [P, P], f"rows{a}")
+            out_pass(rows[:], a, LAST)
+            (nc.vector.tensor_copy if a % 2 == 0 else nc.scalar.copy)(results[LAST][:, a, :], rows[:])
+        store_halves(LAST)

import math
from contextlib import ExitStack

import concourse.mybir as mybir
from concourse.masks import make_identity

K, T, S, H, N = 512, 2048, 512, 512, 512
FLOPS = 2 * K * H * S + 2 * H * N * S

F32 = mybir.dt.float32
BF16 = mybir.dt.bfloat16
I32 = mybir.dt.int32
U32 = mybir.dt.uint32
U16 = mybir.dt.uint16
U8 = mybir.dt.uint8
FP8X4 = mybir.dt.float8_e4m3fn_x4
ACT = mybir.ActivationFunctionType
MULT = mybir.AluOpType.mult
ADD = mybir.AluOpType.add
SUB = mybir.AluOpType.subtract
ITEM_BYTES = {F32: 4, I32: 4, U32: 4, BF16: 2, U16: 2, U8: 1}

P = 128
PACK = 4
LAST = PACK - 1
HALF = S // 2
BLOCKS = S // P
UNIT = 256
IDENT_AT = 192
X_FIRST = T // 4
W1_SPLIT = (108, 96)
WEST_ON_VECTOR, EAST_ON_VECTOR = 2, 1


def tile_picked_cahn8_none_p_kernel(tc, x_words, x_scales, w1, gn, w2, offs, west, east, out):
    nc = tc.nc
    with ExitStack() as ctx:
        keep = ctx.enter_context(tc.tile_pool(name="keep", bufs=1))
        psum = ctx.enter_context(tc.psum_pool(name="psum", bufs=1))
        free, place = [0], {}

        def sb(name, shape, dtype, over=None, phase=0, room=0):
            if over is None:
                place[name] = free[0] + phase
                size = max(room, math.prod(shape[1:]) * ITEM_BYTES[dtype]) + phase
                free[0] = free[0] + -(-size // UNIT) * UNIT
            return keep.tile(shape, dtype, name=name, tag=over or name, align_bytes=64 if phase else UNIT, offset=place[over or name])

        def bank(b, shape, name):
            return psum.tile(shape, F32, name=name, tag=f"bank{b}")

        halves = [slice(0, HALF), slice(HALF, S)]
        blocks = [slice(j * P, (j + 1) * P) for j in range(BLOCKS)]
        whole = slice(0, S)

        offs_t = sb("offs_t", [P, S // 16], U16)
        west_t = sb("west_t", [P, S // 16], U16)
        east_t = sb("east_t", [P, S // 16], U16)
        x_win = sb("x_win", [P, T], I32)
        scale_win = sb("scale_win", [P, T], U8)
        w1_raw = [sb(f"w1_raw{h}", [P, PACK, H // 2], F32) for h in range(2)]
        w2_raw = [sb(f"w2_raw{a}", [P, PACK, width], F32) for a, width in enumerate((P, P, HALF))]
        g = sb("g", [P, PACK], F32)
        ident = sb("ident", [P, P], F32, phase=IDENT_AT)
        w1_rows = w1.rearrange("(p j) c -> p j c", j=PACK)
        w2_rows = w2.rearrange("(p j) c -> p j c", j=PACK)
        nc.gpsimd.memset(scale_win[:].bitcast(I32), 0)
        nc.scalar.dma_start(g[:], gn.rearrange("(p t) o -> p (t o)", t=PACK))
        x_rows = x_words[0].rearrange("p n t -> p (n t)").bitcast(I32)
        nc.sync.dma_start(x_win[:, 0:X_FIRST], x_rows[:, 0:X_FIRST])
        nc.sync.dma_start(offs_t[:], offs)
        nc.sync.dma_start(scale_win[0:P:8, :].bitcast(I32), x_scales[0].bitcast(I32))
        nc.sync.dma_start(x_win[:, X_FIRST:T], x_rows[:, X_FIRST:T])
        for h, c in enumerate(halves):
            nc.sync.dma_start(w1_raw[h][:], w1_rows[:, :, c])
        nc.sync.dma_start(w2_raw[0][:], w2_rows[:, :, blocks[0]])
        picked_scales = sb("picked_scales", [P, S], U8)
        x_scale = sb("x_scale", [P, S], U8)
        nc.vector.tensor_copy(picked_scales[:], scale_win[:].indirect(offs_t[:]))
        nc.vector.tensor_copy(x_scale[:].bitcast(I32), picked_scales[:].bitcast(I32))
        for i in range(1, 4):
            nc.sync.dma_start(x_scale[i:P:32, :].bitcast(I32), picked_scales[8 * i : P : 32, :].bitcast(I32))
        nc.sync.dma_start(w2_raw[1][:], w2_rows[:, :, blocks[1]])
        nc.sync.dma_start(west_t[:], west)
        nc.sync.dma_start(east_t[:], east)
        nc.sync.dma_start(w2_raw[2][:], w2_rows[:, :, halves[1]])
        make_identity(nc, ident[:])

        spread = bank(5, [P, PACK, P], "spread")
        g_last = sb("g_last", [P, 1], F32)
        nc.scalar.activation(g_last[:], g[:, LAST : LAST + 1], ACT.Copy, scale=-1.0)
        for t in range(PACK):
            column = g_last[:] if t == LAST else g[:, t : t + 1]
            nc.tensor.transpose(spread[:, t, :], column.to_broadcast([P, P]), ident[:])
        gain_row = sb("gain_row", [P, 2, P, 2], F32)
        nc.scalar.activation(gain_row[:], spread[:].rearrange("q (u e) p -> q u p e", e=2), ACT.Copy, scale=0.25)

        x_codes = sb("x_codes", [P, S], U32)
        w1_codes = sb("w1_codes", [P, H], U32)
        w1_scales = sb("w1_scales", [P, H], U8)
        nc.vector.tensor_copy(x_codes[:], x_win[:].bitcast(U32).indirect(offs_t[:]))
        w1_view = [raw[:].rearrange("p j (m t) -> p m j t", t=PACK) for raw in w1_raw]
        w1_bf = [sb(f"w1_bf{u}", [P, 2 * P * PACK], BF16) for u in range(2)]

        def weave_w1(u, copy, ms):
            h, m0 = divmod(ms.start, P // 2)
            copy(w1_bf[u][:].rearrange("p (t m j) -> p m j t", t=2, j=PACK)[:, ms], w1_view[h][:, m0 : m0 + ms.stop - ms.start, :, 2 * u : 2 * u + 2])

        def quant_w1(h):
            for t in range(PACK):
                c = slice(t * P + h * P // 2, t * P + (h + 1) * P // 2)
                at = (t % 2) * S + h * HALF
                nc.vector.quantize_mx(w1_codes[:, c].bitcast(FP8X4), w1_scales[:, c], w1_bf[t // 2][:, at : at + HALF])

        weave_w1(0, nc.vector.tensor_copy, slice(0, P // 2))
        weave_w1(1, nc.scalar.copy, slice(0, P // 2))
        quant_w1(0)
        for u, split in enumerate(W1_SPLIT):
            weave_w1(u, nc.vector.tensor_copy, slice(P // 2, split))
            weave_w1(u, nc.scalar.copy, slice(split, P))
        quant_w1(1)
        pre0 = [bank(4 * h, [P, HALF], f"pre0{h}") for h in range(2)]
        pre = {t: bank(t, [P, S], f"pre{t}") for t in range(1, PACK)}

        def first_product(acc, t, c):
            nc.tensor.matmul_mx(acc, lhsT=w1_codes[:, blocks[t]].bitcast(FP8X4), lhsT_scale=w1_scales[:, blocks[t]],
                                rhs=x_codes[:, c].bitcast(FP8X4), rhs_scale=x_scale[:, c], start=True, stop=True)

        for h, c in enumerate(halves):
            first_product(pre0[h][:], 0, c)
        for t in range(1, PACK):
            first_product(pre[t][:], t, whole)

        w2_scales = sb("w2_scales", [P, N], U8)
        w2_codes = {}

        def quant_w2(c, woven, over=None):
            codes = sb(f"w2_codes{c.start}", [P, c.stop - c.start], U32, over)
            nc.vector.quantize_mx(codes[:].bitcast(FP8X4), w2_scales[:, c], woven[:])
            for a in range(c.start // P, c.stop // P):
                w2_codes[a] = codes[:, a * P - c.start : (a + 1) * P - c.start]

        r_west = [sb(f"r_west{t}", [P, S], F32) for t in range(PACK)]
        r_east = [sb(f"r_east{t}", [P, S], F32) for t in range(LAST)]
        cube = [sb(f"cube{t}", [P, S], F32) for t in range(PACK)]
        y_win = [sb(f"y_win{t}", [P, 2 * S], F32) for t in range(PACK)]
        r_win = [sb(f"r_win{t}", [P, 2 * S], F32) for t in range(LAST)] + [sb("r_win3", [P, S], F32)]
        y = [w[:, 0:S] for w in y_win]
        r = [w[:, 0:S] for w in r_win]
        sq = [w[:, S : 2 * S] for w in y_win]
        part = [w[:, S : 2 * S] for w in r_win[:LAST]] + [sb("part3", [P, S], F32)[:]]
        own = {t: sb(f"own{t}", [P, S], F32) for t in (0, LAST)}
        turned = [bank(4 + j, [P, PACK, P], f"turned{j}") for j in range(BLOCKS)]
        early = bank(0, [P, 2, P], "early")

        def look(lst, c):
            return lst[:, c.start // 16 : c.stop // 16]

        def add_block(term, t, j, first=False, last=False):
            sums = early if j == 0 and t < 2 else turned[j]
            nc.tensor.matmul(sums[:, t, :], lhsT=term, rhs=ident[:], start=first, stop=last, is_transpose=True)

        def add_turned(term, t, first=(), last=()):
            for j in range(BLOCKS):
                add_block(term[:, blocks[j]], t, j, j in first, j in last)

        def cubes(t, c):
            nc.vector.scalar_tensor_tensor(cube[t][:, c], sq[t][:, c], 2.0 if t == LAST else 0.0, y[t][:, c], ADD, MULT)

        def add_west(t, c):
            nc.vector.tensor_tensor(part[t][:, c], y_win[t][:].indirect(look(west_t, c)), cube[t][:, c], SUB)

        def add_east(t):
            nc.vector.tensor_tensor(r[t], y_win[t][:].indirect(east_t[:]), part[t], ADD)

        def fetch_scalar(dst, lst, t, c):
            nc.scalar.activation(dst, r_win[t][:].indirect(look(lst, c)), ACT.Copy, scale=0.5 if t == LAST else -0.5)

        def fetch_vector(dst, lst, t, c):
            nc.vector.tensor_scalar(dst, r_win[t][:].indirect(look(lst, c)), 0.5, 0.0, MULT, ADD)

        def fetch_and_add(dst, lst, t):
            fetch_scalar(dst[t][:], lst, t, whole)
            add_turned(dst[t], t)

        w2_first = sb("w2_first", [P, HALF * PACK], BF16, "w1_bf0")
        for a in range(2):
            nc.vector.tensor_copy(w2_first[:, a * S : (a + 1) * S].rearrange("p (c i j) -> p c j i", i=4, j=PACK),
                                  w2_raw[a][:].rearrange("p j (c i) -> p c j i", i=4))
        for h, c in enumerate(halves):
            nc.scalar.activation(y[0][:, c], pre0[h][:], ACT.Tanh)
        for c in halves:
            nc.vector.scalar_tensor_tensor(sq[0][:, c], y[0][:, c], 2.0, y[0][:, c], MULT, MULT)
        nc.scalar.activation(y[1], pre[1][:], ACT.Tanh)
        for t in range(1, LAST):
            nc.scalar.activation(y[t + 1], pre[t + 1][:], ACT.Tanh)
            nc.scalar.activation(sq[t], y[t], ACT.Square, scale=math.sqrt(2.0))
        y_west = sb("y_west", [P, S], F32)
        nc.scalar.activation(own[LAST][:], y[LAST], ACT.Copy, scale=-6.0)
        nc.scalar.activation(sq[LAST], y[LAST], ACT.Square, scale=math.sqrt(2.0))
        nc.scalar.activation(own[0][:], y[0], ACT.Copy, scale=4.0)
        for repeat in range(4):
            add_turned(y[1], 1, first=range(BLOCKS) if repeat == 0 else ())
        add_turned(own[0], 0)
        for step in (cubes, add_west):
            for c in halves:
                step(0, c)
        for t in range(LAST):
            cubes(t + 1, whole)
            add_east(t)
            if t + 1 < LAST:
                add_west(t + 1, whole)
        add_turned(own[LAST], LAST, first=[0])
        add_turned(r[0], 0)
        fetch_and_add(r_west, west_t, 0)
        fetch_and_add(r_east, east_t, 0)
        nc.scalar.activation(y_west[:], y_win[LAST][:].indirect(west_t[:]), ACT.Copy)
        nc.vector.tensor_tensor(part[LAST], y_west[:], cube[LAST][:], SUB)
        own[2] = sb("own2", [P, S], F32, "cube2")
        nc.vector.tensor_scalar(own[2][:], y[2], 4.0, None, MULT)
        add_east(LAST)
        quant_w2(halves[0], w2_first, "y_west")
        add_turned(r[1], 1)
        fetch_and_add(r_west, west_t, 1)
        add_turned(cube[LAST], LAST)
        fetch_scalar(r_east[1][:], east_t, 1, whole)
        add_turned(r[2], 2)
        add_turned(r_east[1], 1, last=[0])
        add_turned(own[2], 2)
        fetch_and_add(r_west, west_t, 2)
        for c in halves:
            fetch_scalar(r_east[2][:, c], east_t, 2, c)
        for j in range(2):
            add_block(r_east[2][:, blocks[j]], 2, j)

        pairs = [sb(f"pairs{j}", [P, 2, 2 * P], BF16) for j in range(BLOCKS)]
        back = [bank(j, [P, 2, P], f"back{j}") for j in range(BLOCKS)]
        z_bf = [sb(f"z_bf{j}", [P, P * PACK], BF16) for j in range(BLOCKS)]
        z_codes = [sb(f"z_codes{j}", [P, P], U32) for j in range(BLOCKS)]
        z_scales = [sb(f"z_scales{j}", [P, P], U8) for j in range(BLOCKS)]
        results = [sb(f"res{j}", [P, PACK, P], F32) for j in range(BLOCKS)]
        out_rows = out.rearrange("(a p) j -> p a j", p=P)

        def last_neighbours(j):
            if j == 1:
                for later in (2, LAST):
                    add_block(r_east[2][:, blocks[later]], 2, later)
            (fetch_vector if j < WEST_ON_VECTOR else fetch_scalar)(r_west[LAST][:, blocks[j]], west_t, LAST, blocks[j])
            from_east = sb(f"from_east{j}", [P, P], F32, room=2 * HALF * PACK if j == 0 else 0)[:]
            (fetch_vector if j < EAST_ON_VECTOR else fetch_scalar)(from_east, east_t, LAST, blocks[j])
            add_block(r_west[LAST][:, blocks[j]], LAST, j)
            add_block(from_east, LAST, j, last=True)

        def round_pairs(j, us=slice(0, 2)):
            sums = (early if j == 0 and us.stop == 1 else turned[j])[:].rearrange("q (u e) p -> q u p e", e=2)
            nc.vector.tensor_tensor(pairs[j][:].rearrange("q u (p e) -> q u p e", e=2)[:, us], sums[:, us], gain_row[:, us], MULT)
            for u in range(us.start, us.stop):
                nc.tensor.transpose(back[j][:, u, :], pairs[j][:, u, :].bitcast(F32), ident[:])

        def weave_z(j):
            nc.scalar.copy(z_bf[j][:].bitcast(F32).rearrange("p (q u) -> p q u", u=2), back[j][:].rearrange("p u q -> p q u"))

        def quant_z(j):
            nc.vector.quantize_mx(z_codes[j][:].bitcast(FP8X4), z_scales[j][:], z_bf[j][:])

        def out_pass(acc, a, j):
            nc.tensor.matmul_mx(acc, lhsT=w2_codes[a].bitcast(FP8X4), lhsT_scale=w2_scales[:, blocks[a]],
                                rhs=z_codes[j][:].bitcast(FP8X4), rhs_scale=z_scales[j][:], start=True, stop=True)

        def product(j):
            acc = [bank(b, [P, 2, P], f"acc{j}{h}") for h, b in enumerate((4 + j, j))]
            for a in range(PACK):
                out_pass(acc[a // 2][:, a % 2, :], a, j)
            return acc

        def store_halves(j):
            for h in range(2):
                nc.sync.dma_start(out_rows[:, 2 * h : 2 * h + 2, blocks[j]], results[j][:, 2 * h : 2 * h + 2, :])

        def store(j, acc):
            for h, copy in enumerate((nc.scalar.copy, nc.scalar.copy if j == 0 else nc.vector.tensor_copy)):
                copy(results[j][:, 2 * h : 2 * h + 2, :], acc[h][:])
            store_halves(j)

        for j in range(LAST):
            last_neighbours(j)
        w2_last = sb("w2_last", [P, HALF * PACK], BF16, "from_east0")
        nc.gpsimd.tensor_scalar(w2_last[:].rearrange("p (c j) -> p c j", j=PACK), w2_raw[2][:].rearrange("p j c -> p c j"), 1.0, 0.0, MULT, ADD)
        for u in range(2):
            round_pairs(0, slice(u, u + 1))
        last_neighbours(LAST)
        round_pairs(1)
        round_pairs(2)
        weave_z(0)
        quant_z(0)
        quant_w2(halves[1], w2_last)
        acc = product(0)
        for u in range(2):
            round_pairs(LAST, slice(u, u + 1))
        for j in range(1, BLOCKS):
            weave_z(j)
            quant_z(j)
            store(j - 1, acc)
            if j < LAST:
                acc = product(j)
        for a, b in enumerate((LAST, 4 + LAST, 0, 4)):
            rows = bank(b, [P, P], f"rows{a}")
            out_pass(rows[:], a, LAST)
            (nc.vector.tensor_copy if a % 2 == 0 else nc.scalar.copy)(results[LAST][:, a, :], rows[:])
        store_halves(LAST)
